import numpy as np
import ml_dtypes


def mxq(x, axis, fmt="e4m3"):
    dtype, down = {"e4m3": (ml_dtypes.float8_e4m3fn, 7), "e5m2": (ml_dtypes.float8_e5m2, 14)}[fmt]
    v = np.moveaxis(np.asarray(x, np.float32).astype(ml_dtypes.bfloat16).astype(np.float64), axis, -1)
    blocks = v.reshape(v.shape[:-1] + (-1, 32))
    amax = np.abs(blocks).max(-1, keepdims=True)
    byte = np.maximum(np.where(amax > 0, np.frexp(amax)[1] - 1 + 127, 0) - down, 1)
    scale = np.exp2(byte - 127.0)
    codes = (blocks / scale).astype(np.float32).astype(dtype).astype(np.float64)
    return np.moveaxis((codes * scale).reshape(v.shape), -1, axis)


WIDE = False


def mx_kscale(k):
    if not WIDE:
        return np.ones(k)
    levels = np.array([10, -10, 5, -5, 0])
    if k % 512:
        return np.exp2(np.random.permutation(np.resize(levels, k // 32))).repeat(32)
    a = np.empty((k // 512, 16))
    for p in range(k // 512):
        a[p, :8] = np.random.permutation(np.resize(levels, 8))
        for g in range(8):
            far = levels[np.abs(levels - a[p, g]) >= 10]
            a[p, g + 8] = far[np.random.randint(len(far))]
    return np.exp2(a.ravel()).repeat(32)


def f64(x):
    return np.asarray(x).astype(np.float64)


def striped(idx):
    return np.tile(idx.reshape(-1, 16).T, (8, 1)).astype(np.uint16)


def unstriped(offs):
    return offs[:16].T.reshape(-1).astype(np.int64)


def striped8(idx):
    return np.concatenate([x.reshape(-1, 16).T for x in idx]).astype(np.uint16)


def runs(offs, k):
    lists = np.stack([offs[16 * r : 16 * r + 16].T.reshape(-1) for r in range(8)]).astype(np.int64)
    return lists[np.arange(k) % 512 // 64]


def pack_weight(w):
    k, n = w.shape
    w = f64(np.asarray(w, np.float32).astype(ml_dtypes.bfloat16)).reshape(k // 32, 32, n)
    amax = np.abs(w).max(1)
    byte = np.clip(np.where(amax > 0, np.frexp(amax)[1] - 1 + 127 - 7, 1), 1, 254)
    scaled = (w * np.exp2(127.0 - byte)[:, None, :]).reshape(k, n).astype(np.float32)
    words = np.ascontiguousarray(scaled.reshape(k // 512, 128, 4, n).transpose(0, 1, 3, 2)).astype(ml_dtypes.float8_e4m3fn).view(np.uint8)
    return words, np.ascontiguousarray(byte.astype(np.uint8).reshape(k // 512, 16, n))


def unpack_weight(words, scales):
    g, p, n, _ = words.shape
    vals = np.ascontiguousarray(words).view(ml_dtypes.float8_e4m3fn).astype(np.float64) * np.repeat(np.exp2(scales.astype(np.float64) - 127.0), 8, axis=1)[..., None]
    return vals.transpose(0, 1, 3, 2).reshape(g * 512, n)


def sigmoid(v):
    return 1.0 / (1.0 + np.exp(-np.maximum(v, -700.0)))


K, T, S, N, H = 512, 2048, 512, 512, 512


def setup_inputs():
    n = np.random.standard_normal
    s = mx_kscale(K)[:, None]
    u = mx_kscale(H)
    packed_xT = pack_weight(n((K, T)) * s)
    return {
        "x_words": packed_xT[0],
        "x_scales": packed_xT[1],
        "w1": (n((K, H)) / np.sqrt(K) / s).astype(np.float32),
        "gn": (np.random.uniform(0.5, 1.5, (H, 1)) * u[:, None]).astype(np.float32),
        "w2": (n((H, N)) / np.sqrt(H) / u[:, None]).astype(np.float32),
        "offs": striped(np.random.permutation(T)[:S]),
        "p1": striped8(np.stack([np.random.permutation(S) for _ in range(8)])),
        "p2": striped8(np.stack([np.random.permutation(S) for _ in range(8)])),
        "p3": striped8(np.stack([np.random.permutation(S) for _ in range(8)])),
    }


def reference(x_words, x_scales, w1, gn, w2, offs, p1, p2, p3):
    xq = unpack_weight(x_words, x_scales)[:, unstriped(offs)]
    y = mxq(f64(w1), 0, "e4m3").T @ xq
    z = f64(gn) * (0.5 * (sigmoid(4.0 * (y[np.arange(H)[:, None], runs(p1, H)] - y)) + 2.0 * (sigmoid(4.0 * (y[np.arange(H)[:, None], runs(p2, H)] - y))) + 4.0 * (sigmoid(4.0 * (y[np.arange(H)[:, None], runs(p3, H)] - y)))) + -1.75)
    return mxq(f64(w2), 0, "e4m3").T @ mxq(z, 0, "e4m3")

@@ -1,0 +1,185 @@
+from contextlib import ExitStack
+
+import concourse.mybir as mybir
+from concourse.masks import make_identity
+
+K, T, S, N, H = 512, 2048, 512, 512, 512
+FLOPS = 2 * K * H * S + 2 * H * N * S
+
+F32 = mybir.dt.float32
+BF16 = mybir.dt.bfloat16
+I32 = mybir.dt.int32
+U32 = mybir.dt.uint32
+U16 = mybir.dt.uint16
+U8 = mybir.dt.uint8
+FP8X4 = mybir.dt.float8_e4m3fn_x4
+ACT = mybir.ActivationFunctionType
+ALU = mybir.AluOpType
+
+P = 128
+PACK = 4
+HALF = S // 2
+CHUNKS = (HALF, P, P)
+
+
+def tile_picked_census8_none_p_kernel(tc, x_words, x_scales, w1, gn, w2, offs, p1, p2, p3, out):
+    nc = tc.nc
+    with ExitStack() as ctx:
+        keep = ctx.enter_context(tc.tile_pool(name="keep", bufs=1))
+        ring = ctx.enter_context(tc.tile_pool(name="ring", bufs=3))
+        acc = ctx.enter_context(tc.psum_pool(name="acc", bufs=3))
+        sums = ctx.enter_context(tc.psum_pool(name="sums", bufs=3))
+        turn = ctx.enter_context(tc.psum_pool(name="turn", bufs=2))
+
+        scale_table = keep.tile([P, T], U8, name="scale_table", align_bytes=64)
+        nc.vector.memset(scale_table[:].bitcast(I32), 0)
+        for q in range(4):
+            queue = nc.scalar if q < 2 else nc.gpsimd
+            queue.dma_start(scale_table[32 * q : 32 * q + 4, :].bitcast(I32), x_scales[0, 4 * q : 4 * q + 4, :].bitcast(I32))
+
+        def load_list(name, source):
+            held = keep.tile([P, S // 16], U16, name=name)
+            nc.sync.dma_start(held[:], source)
+            return held
+
+        picks = load_list("picks", offs)
+        list3 = load_list("list3", p3)
+        w1_rows = w1.rearrange("(p j) c -> p j c", j=PACK)
+        w1_low = keep.tile([P, PACK, H // 2], F32, name="w1_low", tag="low", align_bytes=64)
+        nc.sync.dma_start(w1_low[:], w1_rows[:, :, 0 : H // 2])
+        w1_high = keep.tile([P, PACK, H // 2], F32, name="w1_high", tag="high")
+        nc.sync.dma_start(w1_high[:], w1_rows[:, :, H // 2 : H])
+        word_table = keep.tile([P, T], U32, name="word_table", align_bytes=64)
+        nc.sync.dma_start(word_table[:].bitcast(I32), x_words[0].rearrange("p n t -> p (n t)").bitcast(I32))
+        list2 = load_list("list2", p2)
+        list1 = load_list("list1", p1)
+        lists = (list3, list2, list1)
+
+        ident = keep.tile([P, P], F32, name="ident")
+        make_identity(nc, ident[:])
+        gain = keep.tile([P, PACK], F32, name="gain")
+        nc.sync.dma_start(gain[:], gn.rearrange("(p t) o -> p (t o)", t=PACK))
+
+        warm = keep.tile([P, 1], F32, name="warm")
+        nc.scalar.activation(warm[:], ident[:, 0:1], ACT.Sigmoid)
+
+        w1_bf = keep.tile([P, PACK, P, PACK], BF16, name="w1_bf", align_bytes=64)
+        w1_dst = w1_bf[:].rearrange("p t m j -> p m j t")
+        nc.vector.tensor_copy(w1_dst[:, 0:64], w1_low[:].rearrange("p j (m t) -> p m j t", t=PACK))
+        nc.scalar.copy(w1_dst[:, 64:128], w1_high[:].rearrange("p j (m t) -> p m j t", t=PACK))
+        w2_raw = keep.tile([P, PACK, N], F32, name="w2_raw", tag="high")
+        nc.sync.dma_start(w2_raw[:], w2.rearrange("(p j) c -> p j c", j=PACK))
+
+        x_bytes = keep.tile([P, S], U8, name="x_bytes", tag="low", align_bytes=64)
+        nc.vector.tensor_copy(x_bytes[:], scale_table[:].indirect(picks[:]))
+        w1_codes = keep.tile([P, H], U32, name="w1_codes", align_bytes=64)
+        w1_scales = keep.tile([P, H], U8, name="w1_scales", align_bytes=64)
+        nc.vector.quantize_mx(w1_codes[:].bitcast(FP8X4), w1_scales[:], w1_bf[:].rearrange("p t m j -> p (t m j)"))
+        x_codes = []
+        for h in range(2):
+            codes = keep.tile([P, HALF], U32, name="x_codes%d" % h, align_bytes=64)
+            nc.vector.tensor_copy(codes[:], word_table[:].indirect(picks[:, h * HALF // 16 : (h + 1) * HALF // 16]))
+            x_codes.append(codes)
+
+        gain_ps = turn.tile([P, PACK, P], F32, name="turned", tag="turned")
+        for t in range(PACK):
+            nc.tensor.transpose(gain_ps[:, t, :], gain[:, t : t + 1].to_broadcast([P, P]), ident[:])
+        half_gain = keep.tile([P, 2, P, 2], F32, name="half_gain")
+        nc.scalar.activation(half_gain[:], gain_ps[:].rearrange("j (u e) p -> j u p e", e=2), ACT.Copy, scale=0.5)
+
+        windows = []
+        centres = {}
+        for t in range(PACK):
+            cols = slice(t * P, (t + 1) * P)
+            window = keep.tile([P, S], F32, name="window%d" % t)
+            first = keep.tile([P, HALF], F32, name="first%d" % t)
+            rest = keep.tile([P, HALF], F32, name="rest%d" % t)
+            for h in range(2):
+                cells = slice(h * HALF, (h + 1) * HALF)
+                y_ps = acc.tile([P, HALF], F32, name="y_ps", tag="acc")
+                nc.tensor.matmul_mx(y_ps[:], w1_codes[:, cols].bitcast(FP8X4), w1_scales[:, cols], x_codes[h][:].bitcast(FP8X4), x_bytes[:, cells], start=True, stop=True)
+                nc.scalar.copy(window[:, cells], y_ps[:])
+                if h == 0:
+                    nc.scalar.copy(first[:], y_ps[:])
+            nc.sync.dma_start(rest[:], window[:, HALF:S])
+            windows.append(window)
+            centres[0, t] = first[:]
+            centres[1, t] = rest[:, 0:P]
+            centres[2, t] = rest[:, P:HALF]
+
+        w2_bf = keep.tile([P, N, PACK], BF16, name="w2_bf", align_bytes=64)
+        w2_codes = keep.tile([P, N], U32, name="w2_codes", align_bytes=64)
+        w2_scales = keep.tile([P, N], U8, name="w2_scales", align_bytes=64)
+        w2_src = w2_raw[:].rearrange("p j (c i) -> p c j i", i=4)
+        w2_dst = w2_bf[:].rearrange("p (c i) j -> p c j i", i=4)
+
+        def census(c, t, bank):
+            width = CHUNKS[c]
+            c0 = sum(CHUNKS[:c])
+            diff = ring.tile([P, 3, width], F32, name="diff", tag="diff")
+            soft = ring.tile([P, 3, width], F32, name="soft", tag="soft")
+            for l in range(3):
+                nc.vector.tensor_tensor(diff[:, l, :], windows[t][:].indirect(lists[l][:, c0 // 16 : (c0 + width) // 16]), centres[c, t], ALU.subtract)
+                if l == 1:
+                    nc.scalar.activation(soft[:, 0:2, :], diff[:, 0:2, :], ACT.Tanh, scale=2.0)
+            nc.scalar.activation(soft[:, 2, :], diff[:, 2, :], ACT.Sigmoid, scale=4.0)
+            terms = (0, 0, 1, 2)
+            for b in range(width // P):
+                for i, l in enumerate(terms):
+                    nc.tensor.matmul(bank[:, b, t % 2, :], soft[:, l, b * P : (b + 1) * P], ident[:], start=(i == 0), stop=(i == len(terms) - 1), is_transpose=True)
+
+        def weigh(c, u, bank, turned):
+            for b in range(CHUNKS[c] // P):
+                z_rows = ring.tile([P, P, 2], BF16, name="z_rows", tag="z_rows")
+                nc.vector.scalar_tensor_tensor(z_rows[:], bank[:, b].rearrange("j e p -> j p e"), -0.5, half_gain[:, u], ALU.add, ALU.mult)
+                nc.tensor.transpose(turned[:, b, u, :], z_rows[:].rearrange("j p e -> j (p e)").bitcast(F32), ident[:])
+
+        def pack(c, turned):
+            width = CHUNKS[c]
+            z_bf = ring.tile([P, width * PACK], BF16, name="z_bf", tag="z_bf", align_bytes=64)
+            nc.scalar.copy(z_bf[:].bitcast(F32).rearrange("p (b j u) -> p b j u", u=2, j=P), turned[:].rearrange("p b u j -> p b j u"))
+            z_codes = ring.tile([P, width], U32, name="z_codes", tag="z_codes", align_bytes=64)
+            z_scales = ring.tile([P, width], U8, name="z_scales", tag="z_scales", align_bytes=64)
+            nc.vector.quantize_mx(z_codes[:].bitcast(FP8X4), z_scales[:], z_bf[:])
+            return z_codes, z_scales
+
+        def project(c, z_codes, z_scales):
+            width = CHUNKS[c]
+            c0 = sum(CHUNKS[:c])
+            for h in range(2):
+                o_ps = acc.tile([P, 2, width], F32, name="o_ps", tag="acc")
+                for i in range(2):
+                    cols = slice((2 * h + i) * P, (2 * h + i + 1) * P)
+                    nc.tensor.matmul_mx(o_ps[:, i, :], w2_codes[:, cols].bitcast(FP8X4), w2_scales[:, cols], z_codes[:].bitcast(FP8X4), z_scales[:], start=True, stop=True)
+                result = ring.tile([P, 2, width], F32, name="result", tag="result")
+                if c == len(CHUNKS) - 1 and h == 1:
+                    nc.vector.tensor_copy(result[:], o_ps[:])
+                else:
+                    nc.scalar.copy(result[:], o_ps[:])
+                nc.sync.dma_start(out[2 * h * P : 2 * (h + 1) * P, c0 : c0 + width].rearrange("(i p) j -> p i j", p=P), result[:])
+
+        steps = [(c, t) for c in range(len(CHUNKS)) for t in range(PACK)]
+        banks = {}
+        turneds = {}
+        packed = {}
+        for s in range(len(steps) + 4):
+            if s < len(steps):
+                c, t = steps[s]
+                if t % 2 == 0:
+                    banks[c, t // 2] = sums.tile([P, CHUNKS[c] // P, 2, P], F32, name="bank", tag="bank")
+                census(c, t, banks[c, t // 2])
+            if 1 <= s <= 4:
+                nc.scalar.copy(w2_dst[:, 32 * (s - 1) : 32 * s], w2_src[:, 32 * (s - 1) : 32 * s])
+            if s == 5:
+                nc.vector.quantize_mx(w2_codes[:].bitcast(FP8X4), w2_scales[:], w2_bf[:].rearrange("p n j -> p (n j)"))
+            if 0 <= s - 2 < len(steps) and steps[s - 2][1] % 2 == 1:
+                c, t = steps[s - 2]
+                if t == 1:
+                    turneds[c] = turn.tile([P, CHUNKS[c] // P, 2, P], F32, name="turned", tag="turned")
+                weigh(c, t // 2, banks[c, t // 2], turneds[c])
+            if 0 <= s - 3 < len(steps) and steps[s - 3][1] == 3:
+                c = steps[s - 3][0]
+                packed[c] = pack(c, turneds[c])
+            if 0 <= s - 4 < len(steps) and steps[s - 4][1] == 3:
+                c = steps[s - 4][0]
+                project(c, *packed[c])

@@ -20,6 +20,7 @@ P = 128
 PACK = 4
 HALF = S // 2
 CHUNKS = (HALF, P, P)
+EARLY = 72
 
 
 def tile_picked_census8_none_p_kernel(tc, x_words, x_scales, w1, gn, w2, offs, p1, p2, p3, out):
@@ -28,14 +29,13 @@ def tile_picked_census8_none_p_kernel(tc, x_words, x_scales, w1, gn, w2, offs, p
         keep = ctx.enter_context(tc.tile_pool(name="keep", bufs=1))
         ring = ctx.enter_context(tc.tile_pool(name="ring", bufs=3))
         acc = ctx.enter_context(tc.psum_pool(name="acc", bufs=3))
-        sums = ctx.enter_context(tc.psum_pool(name="sums", bufs=3))
+        sums = ctx.enter_context(tc.psum_pool(name="sums", bufs=2))
         turn = ctx.enter_context(tc.psum_pool(name="turn", bufs=2))
 
         scale_table = keep.tile([P, T], U8, name="scale_table", align_bytes=64)
         nc.vector.memset(scale_table[:].bitcast(I32), 0)
         for q in range(4):
-            queue = nc.scalar if q < 2 else nc.gpsimd
-            queue.dma_start(scale_table[32 * q : 32 * q + 4, :].bitcast(I32), x_scales[0, 4 * q : 4 * q + 4, :].bitcast(I32))
+            nc.scalar.dma_start(scale_table[32 * q : 32 * q + 4, :].bitcast(I32), x_scales[0, 4 * q : 4 * q + 4, :].bitcast(I32))
 
         def load_list(name, source):
             held = keep.tile([P, S // 16], U16, name=name)
@@ -44,48 +44,48 @@ def tile_picked_census8_none_p_kernel(tc, x_words, x_scales, w1, gn, w2, offs, p
 
         picks = load_list("picks", offs)
         list3 = load_list("list3", p3)
-        w1_rows = w1.rearrange("(p j) c -> p j c", j=PACK)
-        w1_low = keep.tile([P, PACK, H // 2], F32, name="w1_low", tag="low", align_bytes=64)
-        nc.sync.dma_start(w1_low[:], w1_rows[:, :, 0 : H // 2])
-        w1_high = keep.tile([P, PACK, H // 2], F32, name="w1_high", tag="high")
-        nc.sync.dma_start(w1_high[:], w1_rows[:, :, H // 2 : H])
-        word_table = keep.tile([P, T], U32, name="word_table", align_bytes=64)
-        nc.sync.dma_start(word_table[:].bitcast(I32), x_words[0].rearrange("p n t -> p (n t)").bitcast(I32))
         list2 = load_list("list2", p2)
+        gain = keep.tile([P, PACK], F32, name="gain")
+        nc.sync.dma_start(gain[:], gn.rearrange("(p t) o -> p (t o)", t=PACK))
+        word_table = keep.tile([P, T], U32, name="word_table", tag="table", align_bytes=64)
+        nc.sync.dma_start(word_table[:].bitcast(I32), x_words[0].rearrange("p n t -> p (n t)").bitcast(I32))
+        w1_rows = w1.rearrange("(p j) c -> p j c", j=PACK)
+        w1_early = keep.tile([P, PACK, PACK * EARLY], F32, name="w1_early", tag="raw")
+        nc.sync.dma_start(w1_early[:], w1_rows[:, :, 0 : PACK * EARLY])
+        w1_late = keep.tile([P, PACK, H - PACK * EARLY], F32, name="w1_late")
+        nc.sync.dma_start(w1_late[:], w1_rows[:, :, PACK * EARLY : H])
         list1 = load_list("list1", p1)
         lists = (list3, list2, list1)
 
+        warm = keep.tile([P, 1], F32, name="warm")
+        nc.gpsimd.memset(warm[:], 0.0)
+        nc.scalar.activation(warm[:], warm[:], ACT.Sigmoid)
         ident = keep.tile([P, P], F32, name="ident")
         make_identity(nc, ident[:])
-        gain = keep.tile([P, PACK], F32, name="gain")
-        nc.sync.dma_start(gain[:], gn.rearrange("(p t) o -> p (t o)", t=PACK))
 
-        warm = keep.tile([P, 1], F32, name="warm")
-        nc.scalar.activation(warm[:], ident[:, 0:1], ACT.Sigmoid)
+        x_codes = keep.tile([P, S], U32, name="x_codes", align_bytes=64)
+        nc.vector.tensor_copy(x_codes[:], word_table[:].indirect(picks[:]))
+        x_bytes = keep.tile([P, S], U8, name="x_bytes", tag="table", align_bytes=64)
+        nc.vector.tensor_copy(x_bytes[:], scale_table[:].indirect(picks[:]))
 
         w1_bf = keep.tile([P, PACK, P, PACK], BF16, name="w1_bf", align_bytes=64)
-        w1_dst = w1_bf[:].rearrange("p t m j -> p m j t")
-        nc.vector.tensor_copy(w1_dst[:, 0:64], w1_low[:].rearrange("p j (m t) -> p m j t", t=PACK))
-        nc.scalar.copy(w1_dst[:, 64:128], w1_high[:].rearrange("p j (m t) -> p m j t", t=PACK))
-        w2_raw = keep.tile([P, PACK, N], F32, name="w2_raw", tag="high")
+        w1_dst = w1_bf[:].rearrange("p t (g i) j -> p g t j i", i=4)
+        nc.scalar.copy(w1_dst[:, 0 : EARLY // 4], w1_early[:].rearrange("p j (g t i) -> p g t j i", t=PACK, i=4))
+        nc.vector.tensor_copy(w1_dst[:, EARLY // 4 : P // 4], w1_late[:].rearrange("p j (g t i) -> p g t j i", t=PACK, i=4))
+        w2_raw = keep.tile([P, PACK, N], F32, name="w2_raw", tag="raw")
         nc.sync.dma_start(w2_raw[:], w2.rearrange("(p j) c -> p j c", j=PACK))
 
-        x_bytes = keep.tile([P, S], U8, name="x_bytes", tag="low", align_bytes=64)
-        nc.vector.tensor_copy(x_bytes[:], scale_table[:].indirect(picks[:]))
         w1_codes = keep.tile([P, H], U32, name="w1_codes", align_bytes=64)
         w1_scales = keep.tile([P, H], U8, name="w1_scales", align_bytes=64)
-        nc.vector.quantize_mx(w1_codes[:].bitcast(FP8X4), w1_scales[:], w1_bf[:].rearrange("p t m j -> p (t m j)"))
-        x_codes = []
-        for h in range(2):
-            codes = keep.tile([P, HALF], U32, name="x_codes%d" % h, align_bytes=64)
-            nc.vector.tensor_copy(codes[:], word_table[:].indirect(picks[:, h * HALF // 16 : (h + 1) * HALF // 16]))
-            x_codes.append(codes)
+        for t0, t1 in ((0, 1), (1, 2), (2, 4)):
+            cols = slice(t0 * P, t1 * P)
+            nc.vector.quantize_mx(w1_codes[:, cols].bitcast(FP8X4), w1_scales[:, cols], w1_bf[:, t0:t1].rearrange("p t m j -> p (t m j)"))
 
         gain_ps = turn.tile([P, PACK, P], F32, name="turned", tag="turned")
         for t in range(PACK):
             nc.tensor.transpose(gain_ps[:, t, :], gain[:, t : t + 1].to_broadcast([P, P]), ident[:])
-        half_gain = keep.tile([P, 2, P, 2], F32, name="half_gain")
-        nc.scalar.activation(half_gain[:], gain_ps[:].rearrange("j (u e) p -> j u p e", e=2), ACT.Copy, scale=0.5)
+        half_gain = keep.tile([P, H], F32, name="half_gain")
+        nc.scalar.activation(half_gain[:].rearrange("j (p t) -> j p t", t=PACK), gain_ps[:].rearrange("j t p -> j p t"), ACT.Copy, scale=0.5)
 
         windows = []
         centres = {}
@@ -97,9 +97,11 @@ def tile_picked_census8_none_p_kernel(tc, x_words, x_scales, w1, gn, w2, offs, p
             for h in range(2):
                 cells = slice(h * HALF, (h + 1) * HALF)
                 y_ps = acc.tile([P, HALF], F32, name="y_ps", tag="acc")
-                nc.tensor.matmul_mx(y_ps[:], w1_codes[:, cols].bitcast(FP8X4), w1_scales[:, cols], x_codes[h][:].bitcast(FP8X4), x_bytes[:, cells], start=True, stop=True)
+                nc.tensor.matmul_mx(y_ps[:], w1_codes[:, cols].bitcast(FP8X4), w1_scales[:, cols], x_codes[:, cells].bitcast(FP8X4), x_bytes[:, cells], start=True, stop=True)
                 nc.scalar.copy(window[:, cells], y_ps[:])
-                if h == 0:
+                if h == 0 and t == 0:
+                    nc.vector.tensor_copy(first[:], y_ps[:])
+                elif h == 0:
                     nc.scalar.copy(first[:], y_ps[:])
             nc.sync.dma_start(rest[:], window[:, HALF:S])
             windows.append(window)
@@ -116,26 +118,37 @@ def tile_picked_census8_none_p_kernel(tc, x_words, x_scales, w1, gn, w2, offs, p
         def census(c, t, bank):
             width = CHUNKS[c]
             c0 = sum(CHUNKS[:c])
-            diff = ring.tile([P, 3, width], F32, name="diff", tag="diff")
-            soft = ring.tile([P, 3, width], F32, name="soft", tag="soft")
-            for l in range(3):
-                nc.vector.tensor_tensor(diff[:, l, :], windows[t][:].indirect(lists[l][:, c0 // 16 : (c0 + width) // 16]), centres[c, t], ALU.subtract)
-                if l == 1:
-                    nc.scalar.activation(soft[:, 0:2, :], diff[:, 0:2, :], ACT.Tanh, scale=2.0)
-            nc.scalar.activation(soft[:, 2, :], diff[:, 2, :], ACT.Sigmoid, scale=4.0)
+            far = ring.tile([P, 2, width], F32, name="far", tag="far", bufs=2)
+            near = ring.tile([P, width], F32, name="near", tag="near", bufs=2)
+            soft = ring.tile([P, 3, width], F32, name="soft", tag="soft", bufs=2)
+            entries = slice(c0 // 16, (c0 + width) // 16)
+            for l in range(2):
+                nc.vector.tensor_tensor(far[:, l, :], windows[t][:].indirect(lists[l][:, entries]), centres[c, t], ALU.subtract)
+            nc.scalar.activation(soft[:, 0:2, :], far[:], ACT.Tanh, scale=2.0)
+            nc.vector.tensor_tensor(near[:], windows[t][:].indirect(lists[2][:, entries]), centres[c, t], ALU.subtract)
+            nc.scalar.activation(soft[:, 2, :], near[:], ACT.Sigmoid, scale=4.0)
             terms = (0, 0, 1, 2)
             for b in range(width // P):
                 for i, l in enumerate(terms):
-                    nc.tensor.matmul(bank[:, b, t % 2, :], soft[:, l, b * P : (b + 1) * P], ident[:], start=(i == 0), stop=(i == len(terms) - 1), is_transpose=True)
+                    nc.tensor.matmul(bank[:, b, :, t % 2, :], soft[:, l, b * P : (b + 1) * P], ident[:], start=(i == 0), stop=(i == len(terms) - 1), is_transpose=True)
 
-        def weigh(c, u, bank, turned):
+        def weigh(c, u, bank, z_rows):
             for b in range(CHUNKS[c] // P):
-                z_rows = ring.tile([P, P, 2], BF16, name="z_rows", tag="z_rows")
-                nc.vector.scalar_tensor_tensor(z_rows[:], bank[:, b].rearrange("j e p -> j p e"), -0.5, half_gain[:, u], ALU.add, ALU.mult)
-                nc.tensor.transpose(turned[:, b, u, :], z_rows[:].rearrange("j p e -> j (p e)").bitcast(F32), ident[:])
+                nc.vector.scalar_tensor_tensor(
+                    z_rows[b][:].rearrange("j (g u n) -> j g u n", u=2, n=8)[:, :, u, :],
+                    bank[:, b].rearrange("j g e i -> j g (e i)"),
+                    -0.5,
+                    half_gain[:].rearrange("j (g u n) -> j g u n", u=2, n=8)[:, :, u, :],
+                    ALU.add,
+                    ALU.mult,
+                )
 
-        def pack(c, turned):
+        def pack(c, z_rows):
             width = CHUNKS[c]
+            turned = turn.tile([P, width // P, 2, P], F32, name="turned", tag="turned")
+            for b in range(width // P):
+                for v in range(2):
+                    nc.tensor.transpose(turned[:, b, v, :], z_rows[b][:].bitcast(F32)[:, v : 2 * P : 2], ident[:])
             z_bf = ring.tile([P, width * PACK], BF16, name="z_bf", tag="z_bf", align_bytes=64)
             nc.scalar.copy(z_bf[:].bitcast(F32).rearrange("p (b j u) -> p b j u", u=2, j=P), turned[:].rearrange("p b u j -> p b j u"))
             z_codes = ring.tile([P, width], U32, name="z_codes", tag="z_codes", align_bytes=64)
@@ -146,40 +159,46 @@ def tile_picked_census8_none_p_kernel(tc, x_words, x_scales, w1, gn, w2, offs, p
         def project(c, z_codes, z_scales):
             width = CHUNKS[c]
             c0 = sum(CHUNKS[:c])
-            for h in range(2):
-                o_ps = acc.tile([P, 2, width], F32, name="o_ps", tag="acc")
-                for i in range(2):
-                    cols = slice((2 * h + i) * P, (2 * h + i + 1) * P)
+            rows = 4 if c == 1 else 2
+            for h in range(4 // rows):
+                if c == 1:
+                    o_ps = sums.tile([P, rows, width], F32, name="o_ps", tag="last", bufs=1)
+                else:
+                    o_ps = acc.tile([P, rows, width], F32, name="o_ps", tag="acc")
+                for i in range(rows):
+                    cols = slice((rows * h + i) * P, (rows * h + i + 1) * P)
                     nc.tensor.matmul_mx(o_ps[:, i, :], w2_codes[:, cols].bitcast(FP8X4), w2_scales[:, cols], z_codes[:].bitcast(FP8X4), z_scales[:], start=True, stop=True)
-                result = ring.tile([P, 2, width], F32, name="result", tag="result")
+                result = ring.tile([P, rows, width], F32, name="result", tag="result", bufs=5)
                 if c == len(CHUNKS) - 1 and h == 1:
                     nc.vector.tensor_copy(result[:], o_ps[:])
                 else:
                     nc.scalar.copy(result[:], o_ps[:])
-                nc.sync.dma_start(out[2 * h * P : 2 * (h + 1) * P, c0 : c0 + width].rearrange("(i p) j -> p i j", p=P), result[:])
+                nc.sync.dma_start(out[rows * h * P : rows * (h + 1) * P, c0 : c0 + width].rearrange("(i p) j -> p i j", p=P), result[:])
 
         steps = [(c, t) for c in range(len(CHUNKS)) for t in range(PACK)]
         banks = {}
         turneds = {}
         packed = {}
-        for s in range(len(steps) + 4):
+        for s in range(len(steps) + 3):
             if s < len(steps):
                 c, t = steps[s]
                 if t % 2 == 0:
-                    banks[c, t // 2] = sums.tile([P, CHUNKS[c] // P, 2, P], F32, name="bank", tag="bank")
+                    tag, bufs = ("last", 1) if s == len(steps) - 2 else ("bank", 2)
+                    banks[c, t // 2] = sums.tile([P, CHUNKS[c] // P, P // 4, 2, 4], F32, name="bank", tag=tag, bufs=bufs)
                 census(c, t, banks[c, t // 2])
-            if 1 <= s <= 4:
-                nc.scalar.copy(w2_dst[:, 32 * (s - 1) : 32 * s], w2_src[:, 32 * (s - 1) : 32 * s])
-            if s == 5:
+            if s < 4:
+                nc.scalar.copy(w2_dst[:, 32 * s : 32 * (s + 1)], w2_src[:, 32 * s : 32 * (s + 1)])
+            if s == 4:
                 nc.vector.quantize_mx(w2_codes[:].bitcast(FP8X4), w2_scales[:], w2_bf[:].rearrange("p n j -> p (n j)"))
             if 0 <= s - 2 < len(steps) and steps[s - 2][1] % 2 == 1:
                 c, t = steps[s - 2]
                 if t == 1:
-                    turneds[c] = turn.tile([P, CHUNKS[c] // P, 2, P], F32, name="turned", tag="turned")
+                    turneds[c] = [ring.tile([P, H], BF16, name="z_rows", tag="z_rows", bufs=4) for b in range(CHUNKS[c] // P)]
                 weigh(c, t // 2, banks[c, t // 2], turneds[c])
             if 0 <= s - 3 < len(steps) and steps[s - 3][1] == 3:
                 c = steps[s - 3][0]
                 packed[c] = pack(c, turneds[c])
-            if 0 <= s - 4 < len(steps) and steps[s - 4][1] == 3:
-                c = steps[s - 4][0]
-                project(c, *packed[c])
+            if s == 7:
+                project(0, *packed[0])
+        project(1, *packed[1])
+        project(2, *packed[2])

@@ -29,7 +29,7 @@ def tile_picked_census8_none_p_kernel(tc, x_words, x_scales, w1, gn, w2, offs, p
         keep = ctx.enter_context(tc.tile_pool(name="keep", bufs=1))
         ring = ctx.enter_context(tc.tile_pool(name="ring", bufs=3))
         acc = ctx.enter_context(tc.psum_pool(name="acc", bufs=3))
-        sums = ctx.enter_context(tc.psum_pool(name="sums", bufs=2))
+        sums = ctx.enter_context(tc.psum_pool(name="sums", bufs=3))
         turn = ctx.enter_context(tc.psum_pool(name="turn", bufs=2))
 
         scale_table = keep.tile([P, T], U8, name="scale_table", align_bytes=64)
@@ -69,9 +69,9 @@ def tile_picked_census8_none_p_kernel(tc, x_words, x_scales, w1, gn, w2, offs, p
         nc.vector.tensor_copy(x_bytes[:], scale_table[:].indirect(picks[:]))
 
         w1_bf = keep.tile([P, PACK, P, PACK], BF16, name="w1_bf", align_bytes=64)
-        w1_dst = w1_bf[:].rearrange("p t (g i) j -> p g t j i", i=4)
-        nc.scalar.copy(w1_dst[:, 0 : EARLY // 4], w1_early[:].rearrange("p j (g t i) -> p g t j i", t=PACK, i=4))
-        nc.vector.tensor_copy(w1_dst[:, EARLY // 4 : P // 4], w1_late[:].rearrange("p j (g t i) -> p g t j i", t=PACK, i=4))
+        w1_dst = w1_bf[:].rearrange("p t m j -> p m j t")
+        nc.scalar.copy(w1_dst[:, 0:EARLY], w1_early[:].rearrange("p j (m t) -> p m j t", t=PACK))
+        nc.vector.tensor_copy(w1_dst[:, EARLY:P], w1_late[:].rearrange("p j (m t) -> p m j t", t=PACK))
         w2_raw = keep.tile([P, PACK, N], F32, name="w2_raw", tag="raw")
         nc.sync.dma_start(w2_raw[:], w2.rearrange("(p j) c -> p j c", j=PACK))
 
@@ -86,6 +86,9 @@ def tile_picked_census8_none_p_kernel(tc, x_words, x_scales, w1, gn, w2, offs, p
             nc.tensor.transpose(gain_ps[:, t, :], gain[:, t : t + 1].to_broadcast([P, P]), ident[:])
         half_gain = keep.tile([P, H], F32, name="half_gain")
         nc.scalar.activation(half_gain[:].rearrange("j (p t) -> j p t", t=PACK), gain_ps[:].rearrange("j t p -> j p t"), ACT.Copy, scale=0.5)
+
+        gain_half = keep.tile([P, PACK], F32, name="gain_half")
+        nc.vector.tensor_scalar(gain_half[:], gain[:], 0.5, None, ALU.mult)
 
         windows = []
         centres = {}
@@ -115,7 +118,9 @@ def tile_picked_census8_none_p_kernel(tc, x_words, x_scales, w1, gn, w2, offs, p
         w2_src = w2_raw[:].rearrange("p j (c i) -> p c j i", i=4)
         w2_dst = w2_bf[:].rearrange("p (c i) j -> p c j i", i=4)
 
-        def census(c, t, bank):
+        last = len(CHUNKS) - 1
+
+        def census(c, t):
             width = CHUNKS[c]
             c0 = sum(CHUNKS[:c])
             far = ring.tile([P, 2, width], F32, name="far", tag="far", bufs=2)
@@ -126,79 +131,81 @@ def tile_picked_census8_none_p_kernel(tc, x_words, x_scales, w1, gn, w2, offs, p
                 nc.vector.tensor_tensor(far[:, l, :], windows[t][:].indirect(lists[l][:, entries]), centres[c, t], ALU.subtract)
             nc.scalar.activation(soft[:, 0:2, :], far[:], ACT.Tanh, scale=2.0)
             nc.vector.tensor_tensor(near[:], windows[t][:].indirect(lists[2][:, entries]), centres[c, t], ALU.subtract)
+            return soft, near
+
+        def add_up(c, t, soft, near, banks):
             nc.scalar.activation(soft[:, 2, :], near[:], ACT.Sigmoid, scale=4.0)
             terms = (0, 0, 1, 2)
-            for b in range(width // P):
+            for b, bank in enumerate(banks):
                 for i, l in enumerate(terms):
-                    nc.tensor.matmul(bank[:, b, :, t % 2, :], soft[:, l, b * P : (b + 1) * P], ident[:], start=(i == 0), stop=(i == len(terms) - 1), is_transpose=True)
+                    nc.tensor.matmul(bank[:, t, :], soft[:, l, b * P : (b + 1) * P], ident[:], start=(i == 0), stop=(i == len(terms) - 1), is_transpose=True)
 
-        def weigh(c, u, bank, z_rows):
-            for b in range(CHUNKS[c] // P):
-                nc.vector.scalar_tensor_tensor(
-                    z_rows[b][:].rearrange("j (g u n) -> j g u n", u=2, n=8)[:, :, u, :],
-                    bank[:, b].rearrange("j g e i -> j g (e i)"),
-                    -0.5,
-                    half_gain[:].rearrange("j (g u n) -> j g u n", u=2, n=8)[:, :, u, :],
-                    ALU.add,
-                    ALU.mult,
-                )
+        def direct(t, soft, near, z_bf):
+            part = ring.tile([P, 2, P], F32, name="part", tag="part", bufs=2)
+            nc.scalar.activation(soft[:, 2, :], near[:], ACT.Sigmoid, scale=4.0)
+            nc.vector.scalar_tensor_tensor(part[:, 0, :], soft[:, 0, :], 2.0, soft[:, 1, :], ALU.mult, ALU.add)
+            nc.vector.tensor_scalar(part[:, 1, :], part[:, 0, :], -0.5, gain_half[:, t : t + 1], ALU.add, ALU.mult)
+            nc.vector.scalar_tensor_tensor(z_bf[:, :, t], soft[:, 2, :], gain_half[:, t : t + 1], part[:, 1, :], ALU.mult, ALU.add)
 
-        def pack(c, z_rows):
-            width = CHUNKS[c]
-            turned = turn.tile([P, width // P, 2, P], F32, name="turned", tag="turned")
-            for b in range(width // P):
-                for v in range(2):
-                    nc.tensor.transpose(turned[:, b, v, :], z_rows[b][:].bitcast(F32)[:, v : 2 * P : 2], ident[:])
-            z_bf = ring.tile([P, width * PACK], BF16, name="z_bf", tag="z_bf", align_bytes=64)
-            nc.scalar.copy(z_bf[:].bitcast(F32).rearrange("p (b j u) -> p b j u", u=2, j=P), turned[:].rearrange("p b u j -> p b j u"))
-            z_codes = ring.tile([P, width], U32, name="z_codes", tag="z_codes", align_bytes=64)
-            z_scales = ring.tile([P, width], U8, name="z_scales", tag="z_scales", align_bytes=64)
-            nc.vector.quantize_mx(z_codes[:].bitcast(FP8X4), z_scales[:], z_bf[:])
+        def weigh(banks, planes):
+            turned = turn.tile([P, len(banks), planes // 2, P], F32, name="turned", tag="turned")
+            for b, bank in enumerate(banks):
+                z_rows = ring.tile([P, P, planes], BF16, name="z_rows", tag="z_rows")
+                nc.vector.scalar_tensor_tensor(z_rows[:], bank[:, 0:planes, :].rearrange("j t p -> j p t"), -0.5, half_gain[:].rearrange("j (p t) -> j p t", t=PACK)[:, :, 0:planes], ALU.add, ALU.mult)
+                pairs = z_rows[:].rearrange("j p t -> j (p t)").bitcast(F32).rearrange("j (p u) -> j p u", p=P)
+                for u in range(planes // 2):
+                    nc.tensor.transpose(turned[:, b, u, :], pairs[:, :, u], ident[:])
+            return turned
+
+        def interleave(turned, z_bf):
+            words = z_bf[:].rearrange("p j t -> p (j t)").bitcast(F32).rearrange("p (b j u) -> p b j u", u=2, j=P)
+            nc.scalar.copy(words[:, :, :, 0 : turned.shape[2]], turned[:].rearrange("p b u j -> p b j u"))
+
+        def pack(c, z_bf):
+            z_codes = ring.tile([P, CHUNKS[c]], U32, name="z_codes", tag="z_codes", align_bytes=64)
+            z_scales = ring.tile([P, CHUNKS[c]], U8, name="z_scales", tag="z_scales", align_bytes=64)
+            nc.vector.quantize_mx(z_codes[:].bitcast(FP8X4), z_scales[:], z_bf[:].rearrange("p j t -> p (j t)"))
             return z_codes, z_scales
 
         def project(c, z_codes, z_scales):
             width = CHUNKS[c]
             c0 = sum(CHUNKS[:c])
-            rows = 4 if c == 1 else 2
+            rows = 2
             for h in range(4 // rows):
-                if c == 1:
-                    o_ps = sums.tile([P, rows, width], F32, name="o_ps", tag="last", bufs=1)
-                else:
-                    o_ps = acc.tile([P, rows, width], F32, name="o_ps", tag="acc")
+                o_ps = acc.tile([P, rows, width], F32, name="o_ps", tag="acc")
                 for i in range(rows):
                     cols = slice((rows * h + i) * P, (rows * h + i + 1) * P)
                     nc.tensor.matmul_mx(o_ps[:, i, :], w2_codes[:, cols].bitcast(FP8X4), w2_scales[:, cols], z_codes[:].bitcast(FP8X4), z_scales[:], start=True, stop=True)
                 result = ring.tile([P, rows, width], F32, name="result", tag="result", bufs=5)
-                if c == len(CHUNKS) - 1 and h == 1:
+                if c == last and h == 1:
                     nc.vector.tensor_copy(result[:], o_ps[:])
                 else:
                     nc.scalar.copy(result[:], o_ps[:])
                 nc.sync.dma_start(out[rows * h * P : rows * (h + 1) * P, c0 : c0 + width].rearrange("(i p) j -> p i j", p=P), result[:])
 
-        steps = [(c, t) for c in range(len(CHUNKS)) for t in range(PACK)]
+        z_tiles = [ring.tile([P, width, PACK], BF16, name="z_bf", tag="z_bf", align_bytes=64) for width in CHUNKS]
         banks = {}
-        turneds = {}
+        turned = {}
         packed = {}
-        for s in range(len(steps) + 3):
-            if s < len(steps):
-                c, t = steps[s]
-                if t % 2 == 0:
-                    tag, bufs = ("last", 1) if s == len(steps) - 2 else ("bank", 2)
-                    banks[c, t // 2] = sums.tile([P, CHUNKS[c] // P, P // 4, 2, 4], F32, name="bank", tag=tag, bufs=bufs)
-                census(c, t, banks[c, t // 2])
-            if s < 4:
-                nc.scalar.copy(w2_dst[:, 32 * s : 32 * (s + 1)], w2_src[:, 32 * s : 32 * (s + 1)])
-            if s == 4:
-                nc.vector.quantize_mx(w2_codes[:].bitcast(FP8X4), w2_scales[:], w2_bf[:].rearrange("p n j -> p (n j)"))
-            if 0 <= s - 2 < len(steps) and steps[s - 2][1] % 2 == 1:
-                c, t = steps[s - 2]
-                if t == 1:
-                    turneds[c] = [ring.tile([P, H], BF16, name="z_rows", tag="z_rows", bufs=4) for b in range(CHUNKS[c] // P)]
-                weigh(c, t // 2, banks[c, t // 2], turneds[c])
-            if 0 <= s - 3 < len(steps) and steps[s - 3][1] == 3:
-                c = steps[s - 3][0]
-                packed[c] = pack(c, turneds[c])
-            if s == 7:
-                project(0, *packed[0])
-        project(1, *packed[1])
-        project(2, *packed[2])
+        for c, width in enumerate(CHUNKS):
+            banks[c] = [sums.tile([P, PACK, P], F32, name="bank", tag="bank") for b in range(width // P)]
+            for t in range(PACK):
+                soft, near = census(c, t)
+                if c == last and t == 3:
+                    interleave(weigh(banks[c], 2), z_tiles[c])
+                if c == last and t >= 2:
+                    direct(t, soft, near, z_tiles[c])
+                else:
+                    add_up(c, t, soft, near, banks[c])
+                if c == 0:
+                    nc.scalar.copy(w2_dst[:, 32 * t : 32 * (t + 1)], w2_src[:, 32 * t : 32 * (t + 1)])
+                elif t == 0 and c == 1:
+                    nc.vector.quantize_mx(w2_codes[:].bitcast(FP8X4), w2_scales[:], w2_bf[:].rearrange("p n j -> p (n j)"))
+                elif t == 1:
+                    turned[c - 1] = weigh(banks[c - 1], PACK)
+                elif t == 2:
+                    interleave(turned[c - 1], z_tiles[c - 1])
+                    packed[c - 1] = pack(c - 1, z_tiles[c - 1])
+                elif t == 3:
+                    project(c - 1, *packed[c - 1])
+        project(last, *pack(last, z_tiles[last]))

@@ -20,7 +20,8 @@ P = 128
 PACK = 4
 HALF = S // 2
 CHUNKS = (HALF, P, P)
-EARLY = 72
+EARLY = 64
+SCALAR_SHARE = 24
 
 
 def tile_picked_census8_none_p_kernel(tc, x_words, x_scales, w1, gn, w2, offs, p1, p2, p3, out):
@@ -35,7 +36,7 @@ def tile_picked_census8_none_p_kernel(tc, x_words, x_scales, w1, gn, w2, offs, p
         scale_table = keep.tile([P, T], U8, name="scale_table", align_bytes=64)
         nc.vector.memset(scale_table[:].bitcast(I32), 0)
         for q in range(4):
-            nc.scalar.dma_start(scale_table[32 * q : 32 * q + 4, :].bitcast(I32), x_scales[0, 4 * q : 4 * q + 4, :].bitcast(I32))
+            nc.sync.dma_start(scale_table[32 * q : 32 * q + 4, :].bitcast(I32), x_scales[0, 4 * q : 4 * q + 4, :].bitcast(I32))
 
         def load_list(name, source):
             held = keep.tile([P, S // 16], U16, name=name)
@@ -43,17 +44,17 @@ def tile_picked_census8_none_p_kernel(tc, x_words, x_scales, w1, gn, w2, offs, p
             return held
 
         picks = load_list("picks", offs)
-        list3 = load_list("list3", p3)
-        list2 = load_list("list2", p2)
         gain = keep.tile([P, PACK], F32, name="gain")
         nc.sync.dma_start(gain[:], gn.rearrange("(p t) o -> p (t o)", t=PACK))
-        word_table = keep.tile([P, T], U32, name="word_table", tag="table", align_bytes=64)
+        list3 = load_list("list3", p3)
+        word_table = keep.tile([P, T], U32, name="word_table", align_bytes=64)
         nc.sync.dma_start(word_table[:].bitcast(I32), x_words[0].rearrange("p n t -> p (n t)").bitcast(I32))
         w1_rows = w1.rearrange("(p j) c -> p j c", j=PACK)
         w1_early = keep.tile([P, PACK, PACK * EARLY], F32, name="w1_early", tag="raw")
         nc.sync.dma_start(w1_early[:], w1_rows[:, :, 0 : PACK * EARLY])
         w1_late = keep.tile([P, PACK, H - PACK * EARLY], F32, name="w1_late")
         nc.sync.dma_start(w1_late[:], w1_rows[:, :, PACK * EARLY : H])
+        list2 = load_list("list2", p2)
         list1 = load_list("list1", p1)
         lists = (list3, list2, list1)
 
@@ -63,15 +64,17 @@ def tile_picked_census8_none_p_kernel(tc, x_words, x_scales, w1, gn, w2, offs, p
         ident = keep.tile([P, P], F32, name="ident")
         make_identity(nc, ident[:])
 
+        x_bytes = keep.tile([P, S], U8, name="x_bytes", align_bytes=64)
+        nc.vector.tensor_copy(x_bytes[:], scale_table[:].indirect(picks[:]))
         x_codes = keep.tile([P, S], U32, name="x_codes", align_bytes=64)
         nc.vector.tensor_copy(x_codes[:], word_table[:].indirect(picks[:]))
-        x_bytes = keep.tile([P, S], U8, name="x_bytes", tag="table", align_bytes=64)
-        nc.vector.tensor_copy(x_bytes[:], scale_table[:].indirect(picks[:]))
 
         w1_bf = keep.tile([P, PACK, P, PACK], BF16, name="w1_bf", align_bytes=64)
         w1_dst = w1_bf[:].rearrange("p t m j -> p m j t")
-        nc.scalar.copy(w1_dst[:, 0:EARLY], w1_early[:].rearrange("p j (m t) -> p m j t", t=PACK))
-        nc.vector.tensor_copy(w1_dst[:, EARLY:P], w1_late[:].rearrange("p j (m t) -> p m j t", t=PACK))
+        nc.vector.tensor_copy(w1_dst[:, 0:EARLY], w1_early[:].rearrange("p j (m t) -> p m j t", t=PACK))
+        late_src = w1_late[:].rearrange("p j (m t) -> p m j t", t=PACK)
+        nc.scalar.copy(w1_dst[:, EARLY : EARLY + SCALAR_SHARE], late_src[:, 0:SCALAR_SHARE])
+        nc.vector.tensor_copy(w1_dst[:, EARLY + SCALAR_SHARE : P], late_src[:, SCALAR_SHARE : P - EARLY])
         w2_raw = keep.tile([P, PACK, N], F32, name="w2_raw", tag="raw")
         nc.sync.dma_start(w2_raw[:], w2.rearrange("(p j) c -> p j c", j=PACK))
 

@@ -19,101 +19,98 @@ ALU = mybir.AluOpType
 P = 128
 PACK = 4
 HALF = S // 2
-CHUNKS = (HALF, P, P)
 EARLY = 64
-SCALAR_SHARE = 24
+SCALAR_SHARE = 8
 
 
 def tile_picked_census8_none_p_kernel(tc, x_words, x_scales, w1, gn, w2, offs, p1, p2, p3, out):
     nc = tc.nc
     with ExitStack() as ctx:
         keep = ctx.enter_context(tc.tile_pool(name="keep", bufs=1))
-        ring = ctx.enter_context(tc.tile_pool(name="ring", bufs=3))
+        ring = ctx.enter_context(tc.tile_pool(name="ring", bufs=2))
         acc = ctx.enter_context(tc.psum_pool(name="acc", bufs=3))
         sums = ctx.enter_context(tc.psum_pool(name="sums", bufs=3))
         turn = ctx.enter_context(tc.psum_pool(name="turn", bufs=2))
-
-        scale_table = keep.tile([P, T], U8, name="scale_table", align_bytes=64)
-        nc.vector.memset(scale_table[:].bitcast(I32), 0)
-        for q in range(4):
-            nc.sync.dma_start(scale_table[32 * q : 32 * q + 4, :].bitcast(I32), x_scales[0, 4 * q : 4 * q + 4, :].bitcast(I32))
 
         def load_list(name, source):
             held = keep.tile([P, S // 16], U16, name=name)
             nc.sync.dma_start(held[:], source)
             return held
 
+        warm = keep.tile([P, 1], F32, name="warm")
+        nc.gpsimd.memset(warm[:], 0.0)
+        scale_table = keep.tile([P, T], U8, name="scale_table", align_bytes=64)
+        nc.gpsimd.memset(scale_table[:].bitcast(I32), 0)
+
         picks = load_list("picks", offs)
         gain = keep.tile([P, PACK], F32, name="gain")
-        nc.sync.dma_start(gain[:], gn.rearrange("(p t) o -> p (t o)", t=PACK))
-        list3 = load_list("list3", p3)
-        word_table = keep.tile([P, T], U32, name="word_table", align_bytes=64)
-        nc.sync.dma_start(word_table[:].bitcast(I32), x_words[0].rearrange("p n t -> p (n t)").bitcast(I32))
+        nc.scalar.dma_start(gain[:], gn.rearrange("(p t) o -> p (t o)", t=PACK))
         w1_rows = w1.rearrange("(p j) c -> p j c", j=PACK)
-        w1_early = keep.tile([P, PACK, PACK * EARLY], F32, name="w1_early", tag="raw")
+        w1_early = keep.tile([P, PACK, PACK * EARLY], F32, name="w1_early")
         nc.sync.dma_start(w1_early[:], w1_rows[:, :, 0 : PACK * EARLY])
         w1_late = keep.tile([P, PACK, H - PACK * EARLY], F32, name="w1_late")
         nc.sync.dma_start(w1_late[:], w1_rows[:, :, PACK * EARLY : H])
-        list2 = load_list("list2", p2)
-        list1 = load_list("list1", p1)
-        lists = (list3, list2, list1)
+        for q in range(4):
+            nc.sync.dma_start(scale_table[32 * q : 32 * q + 4, :].bitcast(I32), x_scales[0, 4 * q : 4 * q + 4, :].bitcast(I32))
+        word_table = keep.tile([P, T], U32, name="word_table", align_bytes=64)
+        nc.sync.dma_start(word_table[:].bitcast(I32), x_words[0].rearrange("p n t -> p (n t)").bitcast(I32))
+        lists = (load_list("list3", p3), load_list("list2", p2), load_list("list1", p1))
+        w2_raw = keep.tile([P, PACK, N], F32, name="w2_raw")
+        nc.sync.dma_start(w2_raw[:], w2.rearrange("(p j) c -> p j c", j=PACK))
 
-        warm = keep.tile([P, 1], F32, name="warm")
-        nc.gpsimd.memset(warm[:], 0.0)
         nc.scalar.activation(warm[:], warm[:], ACT.Sigmoid)
         ident = keep.tile([P, P], F32, name="ident")
         make_identity(nc, ident[:])
 
-        x_bytes = keep.tile([P, S], U8, name="x_bytes", align_bytes=64)
-        nc.vector.tensor_copy(x_bytes[:], scale_table[:].indirect(picks[:]))
-        x_codes = keep.tile([P, S], U32, name="x_codes", align_bytes=64)
-        nc.vector.tensor_copy(x_codes[:], word_table[:].indirect(picks[:]))
-
-        w1_bf = keep.tile([P, PACK, P, PACK], BF16, name="w1_bf", align_bytes=64)
-        w1_dst = w1_bf[:].rearrange("p t m j -> p m j t")
-        nc.vector.tensor_copy(w1_dst[:, 0:EARLY], w1_early[:].rearrange("p j (m t) -> p m j t", t=PACK))
-        late_src = w1_late[:].rearrange("p j (m t) -> p m j t", t=PACK)
-        nc.scalar.copy(w1_dst[:, EARLY : EARLY + SCALAR_SHARE], late_src[:, 0:SCALAR_SHARE])
-        nc.vector.tensor_copy(w1_dst[:, EARLY + SCALAR_SHARE : P], late_src[:, SCALAR_SHARE : P - EARLY])
-        w2_raw = keep.tile([P, PACK, N], F32, name="w2_raw", tag="raw")
-        nc.sync.dma_start(w2_raw[:], w2.rearrange("(p j) c -> p j c", j=PACK))
-
-        w1_codes = keep.tile([P, H], U32, name="w1_codes", align_bytes=64)
-        w1_scales = keep.tile([P, H], U8, name="w1_scales", align_bytes=64)
-        for t0, t1 in ((0, 1), (1, 2), (2, 4)):
-            cols = slice(t0 * P, t1 * P)
-            nc.vector.quantize_mx(w1_codes[:, cols].bitcast(FP8X4), w1_scales[:, cols], w1_bf[:, t0:t1].rearrange("p t m j -> p (t m j)"))
-
-        gain_ps = turn.tile([P, PACK, P], F32, name="turned", tag="turned")
+        gain_ps = acc.tile([P, PACK, P], F32, name="gain_ps", tag="acc")
         for t in range(PACK):
             nc.tensor.transpose(gain_ps[:, t, :], gain[:, t : t + 1].to_broadcast([P, P]), ident[:])
-        half_gain = keep.tile([P, H], F32, name="half_gain")
-        nc.scalar.activation(half_gain[:].rearrange("j (p t) -> j p t", t=PACK), gain_ps[:].rearrange("j t p -> j p t"), ACT.Copy, scale=0.5)
-
+        half_gain = keep.tile([P, 2, 2, P, 2], F32, name="half_gain")
+        for b in range(2):
+            nc.scalar.activation(half_gain[:, :, b], gain_ps[:].rearrange("j (u e) p -> j u p e", e=2), ACT.Copy, scale=0.5)
         gain_half = keep.tile([P, PACK], F32, name="gain_half")
         nc.vector.tensor_scalar(gain_half[:], gain[:], 0.5, None, ALU.mult)
 
-        windows = []
-        centres = {}
-        for t in range(PACK):
+        w1_bf = keep.tile([P, PACK, P, PACK], BF16, name="w1_bf", align_bytes=64)
+        w1_dst = w1_bf[:].rearrange("p t m j -> p m j t")
+        nc.scalar.copy(w1_dst[:, 0:EARLY], w1_early[:].rearrange("p j (m t) -> p m j t", t=PACK))
+        late_src = w1_late[:].rearrange("p j (m t) -> p m j t", t=PACK)
+        nc.scalar.copy(w1_dst[:, EARLY : EARLY + SCALAR_SHARE], late_src[:, 0:SCALAR_SHARE])
+        nc.vector.tensor_copy(w1_dst[:, EARLY + SCALAR_SHARE : P], late_src[:, SCALAR_SHARE : P - EARLY])
+
+        w1_codes = keep.tile([P, H], U32, name="w1_codes", align_bytes=64)
+        w1_scales = keep.tile([P, H], U8, name="w1_scales", align_bytes=64)
+        nc.vector.quantize_mx(w1_codes[:].bitcast(FP8X4), w1_scales[:], w1_bf[:].rearrange("p t m j -> p (t m j)"))
+
+        x_bytes = keep.tile([P, S], U8, name="x_bytes", align_bytes=64)
+        nc.vector.tensor_copy(x_bytes[:], scale_table[:].indirect(picks[:]))
+        x_codes = keep.tile([P, S], U32, name="x_codes", align_bytes=64)
+        for h in range(2):
+            nc.vector.tensor_copy(x_codes[:, h * HALF : (h + 1) * HALF], word_table[:].indirect(picks[:, h * 16 : (h + 1) * 16]))
+
+        def first_product(t, cells, y_ps):
             cols = slice(t * P, (t + 1) * P)
-            window = keep.tile([P, S], F32, name="window%d" % t)
-            first = keep.tile([P, HALF], F32, name="first%d" % t)
-            rest = keep.tile([P, HALF], F32, name="rest%d" % t)
-            for h in range(2):
-                cells = slice(h * HALF, (h + 1) * HALF)
-                y_ps = acc.tile([P, HALF], F32, name="y_ps", tag="acc")
-                nc.tensor.matmul_mx(y_ps[:], w1_codes[:, cols].bitcast(FP8X4), w1_scales[:, cols], x_codes[:, cells].bitcast(FP8X4), x_bytes[:, cells], start=True, stop=True)
-                nc.scalar.copy(window[:, cells], y_ps[:])
-                if h == 0 and t == 0:
-                    nc.vector.tensor_copy(first[:], y_ps[:])
-                elif h == 0:
-                    nc.scalar.copy(first[:], y_ps[:])
-            nc.sync.dma_start(rest[:], window[:, HALF:S])
-            windows.append(window)
-            centres[0, t] = first[:]
-            centres[1, t] = rest[:, 0:P]
-            centres[2, t] = rest[:, P:HALF]
+            nc.tensor.matmul_mx(y_ps, w1_codes[:, cols].bitcast(FP8X4), w1_scales[:, cols], x_codes[:, cells].bitcast(FP8X4), x_bytes[:, cells], start=True, stop=True)
+
+        windows = [keep.tile([P, 2 * S if t < 2 else S], F32, name="window%d" % t) for t in range(PACK)]
+        nc.gpsimd.memset(windows[0][:, S : 2 * S], 0.0)
+        centres = [windows[1][:, S : 2 * S]] + [keep.tile([P, S], F32, name="centre%d" % t)[:] for t in range(1, PACK)]
+
+        low, high = slice(0, HALF), slice(HALF, S)
+        y_low = acc.tile([P, HALF], F32, name="y_low", tag="acc")
+        y_high = acc.tile([P, HALF], F32, name="y_high", tag="acc")
+        first_product(0, low, y_low[:])
+        first_product(0, high, y_high[:])
+        nc.scalar.copy(windows[0][:, low], y_low[:])
+        nc.vector.tensor_copy(windows[0][:, high], y_high[:])
+        nc.scalar.copy(centres[0][:, low], y_low[:])
+        nc.scalar.copy(centres[0][:, high], y_high[:])
+
+        def later_tile(t):
+            y_ps = acc.tile([P, S], F32, name="y_ps", tag="acc")
+            first_product(t, slice(0, S), y_ps[:])
+            nc.scalar.copy(windows[t][:, 0:S], y_ps[:])
+            nc.sync.dma_start(centres[t], windows[t][:, 0:S])
 
         w2_bf = keep.tile([P, N, PACK], BF16, name="w2_bf", align_bytes=64)
         w2_codes = keep.tile([P, N], U32, name="w2_codes", align_bytes=64)
@@ -121,94 +118,101 @@ def tile_picked_census8_none_p_kernel(tc, x_words, x_scales, w1, gn, w2, offs, p
         w2_src = w2_raw[:].rearrange("p j (c i) -> p c j i", i=4)
         w2_dst = w2_bf[:].rearrange("p (c i) j -> p c j i", i=4)
 
-        last = len(CHUNKS) - 1
+        def round_w2(quarter):
+            nc.scalar.copy(w2_dst[:, 32 * quarter : 32 * (quarter + 1)], w2_src[:, 32 * quarter : 32 * (quarter + 1)])
 
-        def census(c, t):
-            width = CHUNKS[c]
-            c0 = sum(CHUNKS[:c])
-            far = ring.tile([P, 2, width], F32, name="far", tag="far", bufs=2)
-            near = ring.tile([P, width], F32, name="near", tag="near", bufs=2)
-            soft = ring.tile([P, 3, width], F32, name="soft", tag="soft", bufs=2)
+        def census(t, c0, width):
+            far = ring.tile([P, 2, width], F32, name="far", tag="far")
+            near = ring.tile([P, width], F32, name="near", tag="near")
+            soft = ring.tile([P, 3, width], F32, name="soft", tag="soft")
             entries = slice(c0 // 16, (c0 + width) // 16)
+            centre = centres[t][:, c0 : c0 + width]
             for l in range(2):
-                nc.vector.tensor_tensor(far[:, l, :], windows[t][:].indirect(lists[l][:, entries]), centres[c, t], ALU.subtract)
+                nc.vector.tensor_tensor(far[:, l, :], windows[t][:].indirect(lists[l][:, entries]), centre, ALU.subtract)
             nc.scalar.activation(soft[:, 0:2, :], far[:], ACT.Tanh, scale=2.0)
-            nc.vector.tensor_tensor(near[:], windows[t][:].indirect(lists[2][:, entries]), centres[c, t], ALU.subtract)
-            return soft, near
-
-        def add_up(c, t, soft, near, banks):
+            nc.vector.tensor_tensor(near[:], windows[t][:].indirect(lists[2][:, entries]), centre, ALU.subtract)
             nc.scalar.activation(soft[:, 2, :], near[:], ACT.Sigmoid, scale=4.0)
+            return soft
+
+        def add_up(soft, bank, e, first=0):
             terms = (0, 0, 1, 2)
-            for b, bank in enumerate(banks):
+            for b in range(bank.shape[2]):
                 for i, l in enumerate(terms):
-                    nc.tensor.matmul(bank[:, t, :], soft[:, l, b * P : (b + 1) * P], ident[:], start=(i == 0), stop=(i == len(terms) - 1), is_transpose=True)
+                    nc.tensor.matmul(bank[:, e, b, :], soft[:, l, (first + b) * P : (first + b + 1) * P], ident[:], start=(i == 0), stop=(i == len(terms) - 1), is_transpose=True)
 
-        def direct(t, soft, near, z_bf):
-            part = ring.tile([P, 2, P], F32, name="part", tag="part", bufs=2)
-            nc.scalar.activation(soft[:, 2, :], near[:], ACT.Sigmoid, scale=4.0)
+        def direct(t, soft, z_bf):
+            part = ring.tile([P, 2, P], F32, name="part", tag="part")
             nc.vector.scalar_tensor_tensor(part[:, 0, :], soft[:, 0, :], 2.0, soft[:, 1, :], ALU.mult, ALU.add)
             nc.vector.tensor_scalar(part[:, 1, :], part[:, 0, :], -0.5, gain_half[:, t : t + 1], ALU.add, ALU.mult)
             nc.vector.scalar_tensor_tensor(z_bf[:, :, t], soft[:, 2, :], gain_half[:, t : t + 1], part[:, 1, :], ALU.mult, ALU.add)
 
-        def weigh(banks, planes):
-            turned = turn.tile([P, len(banks), planes // 2, P], F32, name="turned", tag="turned")
-            for b, bank in enumerate(banks):
-                z_rows = ring.tile([P, P, planes], BF16, name="z_rows", tag="z_rows")
-                nc.vector.scalar_tensor_tensor(z_rows[:], bank[:, 0:planes, :].rearrange("j t p -> j p t"), -0.5, half_gain[:].rearrange("j (p t) -> j p t", t=PACK)[:, :, 0:planes], ALU.add, ALU.mult)
-                pairs = z_rows[:].rearrange("j p t -> j (p t)").bitcast(F32).rearrange("j (p u) -> j p u", p=P)
-                for u in range(planes // 2):
-                    nc.tensor.transpose(turned[:, b, u, :], pairs[:, :, u], ident[:])
-            return turned
+        def weigh(bank, u, targets):
+            blocks = bank.shape[2]
+            z_rows = ring.tile([P, blocks, P, 2], BF16, name="z_rows", tag="z_rows")
+            nc.vector.scalar_tensor_tensor(z_rows[:].rearrange("j b p e -> j (b p) e"), bank[:].rearrange("j e b p -> j (b p) e"), -0.5, half_gain[:, u, 0:blocks].rearrange("j b p e -> j (b p) e"), ALU.add, ALU.mult)
+            pairs = z_rows[:].rearrange("j b p e -> j (b p e)").bitcast(F32)
+            for b in range(blocks):
+                nc.tensor.transpose(targets[b], pairs[:, b * P : (b + 1) * P], ident[:])
 
-        def interleave(turned, z_bf):
-            words = z_bf[:].rearrange("p j t -> p (j t)").bitcast(F32).rearrange("p (b j u) -> p b j u", u=2, j=P)
-            nc.scalar.copy(words[:, :, :, 0 : turned.shape[2]], turned[:].rearrange("p b u j -> p b j u"))
+        def words_of(z_bf):
+            return z_bf[:].rearrange("p j t -> p (j t)").bitcast(F32).rearrange("p (j u) -> p j u", u=2)
 
-        def pack(c, z_bf):
-            z_codes = ring.tile([P, CHUNKS[c]], U32, name="z_codes", tag="z_codes", align_bytes=64)
-            z_scales = ring.tile([P, CHUNKS[c]], U8, name="z_scales", tag="z_scales", align_bytes=64)
+        def pack(z_bf):
+            width = z_bf.shape[1]
+            z_codes = ring.tile([P, width], U32, name="z_codes", tag="z_codes", align_bytes=64, bufs=3)
+            z_scales = ring.tile([P, width], U8, name="z_scales", tag="z_scales", align_bytes=64, bufs=3)
             nc.vector.quantize_mx(z_codes[:].bitcast(FP8X4), z_scales[:], z_bf[:].rearrange("p j t -> p (j t)"))
             return z_codes, z_scales
 
-        def project(c, z_codes, z_scales):
-            width = CHUNKS[c]
-            c0 = sum(CHUNKS[:c])
+        def project(c0, z_codes, z_scales, last):
+            width = z_codes.shape[1]
             rows = 2
             for h in range(4 // rows):
                 o_ps = acc.tile([P, rows, width], F32, name="o_ps", tag="acc")
                 for i in range(rows):
                     cols = slice((rows * h + i) * P, (rows * h + i + 1) * P)
                     nc.tensor.matmul_mx(o_ps[:, i, :], w2_codes[:, cols].bitcast(FP8X4), w2_scales[:, cols], z_codes[:].bitcast(FP8X4), z_scales[:], start=True, stop=True)
-                result = ring.tile([P, rows, width], F32, name="result", tag="result", bufs=5)
-                if c == last and h == 1:
+                result = ring.tile([P, rows, width], F32, name="result", tag="result", bufs=6)
+                if last and h == 1:
                     nc.vector.tensor_copy(result[:], o_ps[:])
                 else:
                     nc.scalar.copy(result[:], o_ps[:])
                 nc.sync.dma_start(out[rows * h * P : rows * (h + 1) * P, c0 : c0 + width].rearrange("(i p) j -> p i j", p=P), result[:])
 
-        z_tiles = [ring.tile([P, width, PACK], BF16, name="z_bf", tag="z_bf", align_bytes=64) for width in CHUNKS]
-        banks = {}
-        turned = {}
-        packed = {}
-        for c, width in enumerate(CHUNKS):
-            banks[c] = [sums.tile([P, PACK, P], F32, name="bank", tag="bank") for b in range(width // P)]
-            for t in range(PACK):
-                soft, near = census(c, t)
-                if c == last and t == 3:
-                    interleave(weigh(banks[c], 2), z_tiles[c])
-                if c == last and t >= 2:
-                    direct(t, soft, near, z_tiles[c])
-                else:
-                    add_up(c, t, soft, near, banks[c])
-                if c == 0:
-                    nc.scalar.copy(w2_dst[:, 32 * t : 32 * (t + 1)], w2_src[:, 32 * t : 32 * (t + 1)])
-                elif t == 0 and c == 1:
-                    nc.vector.quantize_mx(w2_codes[:].bitcast(FP8X4), w2_scales[:], w2_bf[:].rearrange("p n j -> p (n j)"))
-                elif t == 1:
-                    turned[c - 1] = weigh(banks[c - 1], PACK)
-                elif t == 2:
-                    interleave(turned[c - 1], z_tiles[c - 1])
-                    packed[c - 1] = pack(c - 1, z_tiles[c - 1])
-                elif t == 3:
-                    project(c - 1, *packed[c - 1])
-        project(last, *pack(last, z_tiles[last]))
+        z_a = keep.tile([P, HALF, PACK], BF16, name="z_a", align_bytes=64)
+        z_b = keep.tile([P, P, PACK], BF16, name="z_b", align_bytes=64)
+        z_c = keep.tile([P, P, PACK], BF16, name="z_c", align_bytes=64)
+        turned_low = turn.tile([P, 2, HALF], F32, name="turned_low", tag="turned")
+        turned_high = turn.tile([P, 3, P], F32, name="turned_high", tag="turned")
+
+        later_tile(1)
+        front = [sums.tile([P, 2, 2, P], F32, name="front", tag="bank") for h in range(2)]
+        for t in range(2):
+            soft = census(t, 0, S)
+            for h in range(2):
+                add_up(soft, front[h], t, 2 * h)
+                round_w2(2 * t + h)
+            later_tile(t + 2)
+        back_a = sums.tile([P, 2, 2, P], F32, name="back_a", tag="bank")
+        add_up(census(2, 0, HALF), back_a, 0)
+        weigh(front[0], 0, [turned_low[:, 0, 0:P], turned_low[:, 0, P:HALF]])
+        weigh(front[1], 0, [turned_high[:, 0, :], turned_high[:, 2, :]])
+        add_up(census(3, 0, HALF), back_a, 1)
+        nc.vector.quantize_mx(w2_codes[:].bitcast(FP8X4), w2_scales[:], w2_bf[:].rearrange("p n j -> p (n j)"))
+        back_b = sums.tile([P, 2, 1, P], F32, name="back_b", tag="bank")
+        add_up(census(2, HALF, P), back_b, 0)
+        weigh(back_a, 1, [turned_low[:, 1, 0:P], turned_low[:, 1, P:HALF]])
+        add_up(census(3, HALF, P), back_b, 1)
+        nc.scalar.copy(words_of(z_a), turned_low[:].rearrange("p u j -> p j u"))
+        nc.scalar.copy(words_of(z_c)[:, :, 0], turned_high[:, 2, :])
+        packed_a = pack(z_a)
+        soft2 = census(2, HALF + P, P)
+        weigh(back_b, 1, [turned_high[:, 1, :]])
+        project(0, *packed_a, False)
+        soft3 = census(3, HALF + P, P)
+        nc.scalar.copy(words_of(z_b), turned_high[:, 0:2, :].rearrange("p u j -> p j u"))
+        direct(2, soft2, z_c)
+        packed_b = pack(z_b)
+        direct(3, soft3, z_c)
+        project(HALF, *packed_b, False)
+        project(HALF + P, *pack(z_c), True)

@@ -19,8 +19,6 @@ ALU = mybir.AluOpType
 P = 128
 PACK = 4
 HALF = S // 2
-EARLY = 64
-SCALAR_SHARE = 8
 
 
 def tile_picked_census8_none_p_kernel(tc, x_words, x_scales, w1, gn, w2, offs, p1, p2, p3, out):
@@ -43,47 +41,40 @@ def tile_picked_census8_none_p_kernel(tc, x_words, x_scales, w1, gn, w2, offs, p
         nc.gpsimd.memset(scale_table[:].bitcast(I32), 0)
 
         picks = load_list("picks", offs)
-        gain = keep.tile([P, PACK], F32, name="gain")
-        nc.scalar.dma_start(gain[:], gn.rearrange("(p t) o -> p (t o)", t=PACK))
         w1_rows = w1.rearrange("(p j) c -> p j c", j=PACK)
-        w1_early = keep.tile([P, PACK, PACK * EARLY], F32, name="w1_early")
-        nc.sync.dma_start(w1_early[:], w1_rows[:, :, 0 : PACK * EARLY])
-        w1_late = keep.tile([P, PACK, H - PACK * EARLY], F32, name="w1_late")
-        nc.sync.dma_start(w1_late[:], w1_rows[:, :, PACK * EARLY : H])
-        for q in range(4):
-            nc.sync.dma_start(scale_table[32 * q : 32 * q + 4, :].bitcast(I32), x_scales[0, 4 * q : 4 * q + 4, :].bitcast(I32))
+        w1_early = keep.tile([P, 2, H], F32, name="w1_early")
+        nc.sync.dma_start(w1_early[:], w1_rows[:, 0:2, :])
+        nc.sync.dma_start(scale_table[0:P:8, :].bitcast(I32), x_scales[0].bitcast(I32))
+        w1_late = keep.tile([P, 2, H], F32, name="w1_late", tag="raw")
+        nc.sync.dma_start(w1_late[:], w1_rows[:, 2:4, :])
         word_table = keep.tile([P, T], U32, name="word_table", align_bytes=64)
         nc.sync.dma_start(word_table[:].bitcast(I32), x_words[0].rearrange("p n t -> p (n t)").bitcast(I32))
         lists = (load_list("list3", p3), load_list("list2", p2), load_list("list1", p1))
-        w2_raw = keep.tile([P, PACK, N], F32, name="w2_raw")
-        nc.sync.dma_start(w2_raw[:], w2.rearrange("(p j) c -> p j c", j=PACK))
+
+        x_bytes = keep.tile([P, S], U8, name="x_bytes", align_bytes=64)
+        nc.gpsimd.memset(x_bytes[:].bitcast(I32), 0)
+        picked_bytes = keep.tile([P, S], U8, name="picked_bytes", tag="staged", align_bytes=64)
+        nc.vector.tensor_copy(picked_bytes[:], scale_table[:].indirect(picks[:]))
+        for r in range(4):
+            nc.sync.dma_start(x_bytes[r:P:32, :].bitcast(I32), picked_bytes[8 * r : P : 32, :].bitcast(I32))
 
         nc.scalar.activation(warm[:], warm[:], ACT.Sigmoid)
         ident = keep.tile([P, P], F32, name="ident")
         make_identity(nc, ident[:])
 
-        gain_ps = acc.tile([P, PACK, P], F32, name="gain_ps", tag="acc")
-        for t in range(PACK):
-            nc.tensor.transpose(gain_ps[:, t, :], gain[:, t : t + 1].to_broadcast([P, P]), ident[:])
-        half_gain = keep.tile([P, 2, 2, P, 2], F32, name="half_gain")
-        for b in range(2):
-            nc.scalar.activation(half_gain[:, :, b], gain_ps[:].rearrange("j (u e) p -> j u p e", e=2), ACT.Copy, scale=0.5)
-        gain_half = keep.tile([P, PACK], F32, name="gain_half")
-        nc.vector.tensor_scalar(gain_half[:], gain[:], 0.5, None, ALU.mult)
-
         w1_bf = keep.tile([P, PACK, P, PACK], BF16, name="w1_bf", align_bytes=64)
         w1_dst = w1_bf[:].rearrange("p t m j -> p m j t")
-        nc.scalar.copy(w1_dst[:, 0:EARLY], w1_early[:].rearrange("p j (m t) -> p m j t", t=PACK))
-        late_src = w1_late[:].rearrange("p j (m t) -> p m j t", t=PACK)
-        nc.scalar.copy(w1_dst[:, EARLY : EARLY + SCALAR_SHARE], late_src[:, 0:SCALAR_SHARE])
-        nc.vector.tensor_copy(w1_dst[:, EARLY + SCALAR_SHARE : P], late_src[:, SCALAR_SHARE : P - EARLY])
+        nc.scalar.copy(w1_dst[:, :, 0:2, :], w1_early[:].rearrange("p j (m t) -> p m j t", t=PACK))
+        nc.vector.tensor_copy(w1_dst[:, :, 2:4, :], w1_late[:].rearrange("p j (m t) -> p m j t", t=PACK))
+        w2_raw = keep.tile([P, PACK, N], F32, name="w2_raw", tag="raw")
+        nc.sync.dma_start(w2_raw[:], w2.rearrange("(p j) c -> p j c", j=PACK))
+        gain = keep.tile([P, PACK], F32, name="gain", tag="staged", align_bytes=64)
+        nc.sync.dma_start(gain[:], gn.rearrange("(p t) o -> p (t o)", t=PACK))
 
         w1_codes = keep.tile([P, H], U32, name="w1_codes", align_bytes=64)
         w1_scales = keep.tile([P, H], U8, name="w1_scales", align_bytes=64)
         nc.vector.quantize_mx(w1_codes[:].bitcast(FP8X4), w1_scales[:], w1_bf[:].rearrange("p t m j -> p (t m j)"))
 
-        x_bytes = keep.tile([P, S], U8, name="x_bytes", align_bytes=64)
-        nc.vector.tensor_copy(x_bytes[:], scale_table[:].indirect(picks[:]))
         x_codes = keep.tile([P, S], U32, name="x_codes", align_bytes=64)
         for h in range(2):
             nc.vector.tensor_copy(x_codes[:, h * HALF : (h + 1) * HALF], word_table[:].indirect(picks[:, h * 16 : (h + 1) * 16]))
@@ -92,9 +83,9 @@ def tile_picked_census8_none_p_kernel(tc, x_words, x_scales, w1, gn, w2, offs, p
             cols = slice(t * P, (t + 1) * P)
             nc.tensor.matmul_mx(y_ps, w1_codes[:, cols].bitcast(FP8X4), w1_scales[:, cols], x_codes[:, cells].bitcast(FP8X4), x_bytes[:, cells], start=True, stop=True)
 
-        windows = [keep.tile([P, 2 * S if t < 2 else S], F32, name="window%d" % t) for t in range(PACK)]
+        windows = [keep.tile([P, 2 * S if t == 0 else S], F32, name="window%d" % t) for t in range(PACK)]
         nc.gpsimd.memset(windows[0][:, S : 2 * S], 0.0)
-        centres = [windows[1][:, S : 2 * S]] + [keep.tile([P, S], F32, name="centre%d" % t)[:] for t in range(1, PACK)]
+        centres = [keep.tile([P, S], F32, name="centre%d" % t)[:] for t in range(PACK)]
 
         low, high = slice(0, HALF), slice(HALF, S)
         y_low = acc.tile([P, HALF], F32, name="y_low", tag="acc")
@@ -112,6 +103,21 @@ def tile_picked_census8_none_p_kernel(tc, x_words, x_scales, w1, gn, w2, offs, p
             nc.scalar.copy(windows[t][:, 0:S], y_ps[:])
             nc.sync.dma_start(centres[t], windows[t][:, 0:S])
 
+        gain_front = [keep.tile([P, 2, P, 2], F32, name="gain_front%d" % h, tag="after_front%d" % h) for h in range(2)]
+        gain_a = keep.tile([P, 2, P, 2], F32, name="gain_a", tag="after_a")
+        gain_b = keep.tile([P, 1, P, 2], F32, name="gain_b", tag="after_b")
+        gain_half = keep.tile([P, PACK], F32, name="gain_half")
+
+        def spread_gain():
+            gain_ps = acc.tile([P, PACK, P], F32, name="gain_ps", tag="acc")
+            for t in range(PACK):
+                nc.tensor.transpose(gain_ps[:, t, :], gain[:, t : t + 1].to_broadcast([P, P]), ident[:])
+            spread = keep.tile([P, 2, P, 2], F32, name="spread")
+            nc.scalar.activation(spread[:], gain_ps[:].rearrange("j (u e) p -> j u p e", e=2), ACT.Copy, scale=0.5)
+            for held, u in ((gain_front[0], 0), (gain_front[1], 0), (gain_a, 1), (gain_b, 1)):
+                nc.sync.dma_start(held[:], spread[:, u : u + 1].to_broadcast([P, held.shape[1], P, 2]))
+            nc.scalar.activation(gain_half[:], gain[:], ACT.Copy, scale=0.5)
+
         w2_bf = keep.tile([P, N, PACK], BF16, name="w2_bf", align_bytes=64)
         w2_codes = keep.tile([P, N], U32, name="w2_codes", align_bytes=64)
         w2_scales = keep.tile([P, N], U8, name="w2_scales", align_bytes=64)
@@ -121,17 +127,29 @@ def tile_picked_census8_none_p_kernel(tc, x_words, x_scales, w1, gn, w2, offs, p
         def round_w2(quarter):
             nc.scalar.copy(w2_dst[:, 32 * quarter : 32 * (quarter + 1)], w2_src[:, 32 * quarter : 32 * (quarter + 1)])
 
-        def census(t, c0, width):
-            far = ring.tile([P, 2, width], F32, name="far", tag="far")
-            near = ring.tile([P, width], F32, name="near", tag="near")
-            soft = ring.tile([P, 3, width], F32, name="soft", tag="soft")
-            entries = slice(c0 // 16, (c0 + width) // 16)
-            centre = centres[t][:, c0 : c0 + width]
-            for l in range(2):
-                nc.vector.tensor_tensor(far[:, l, :], windows[t][:].indirect(lists[l][:, entries]), centre, ALU.subtract)
-            nc.scalar.activation(soft[:, 0:2, :], far[:], ACT.Tanh, scale=2.0)
-            nc.vector.tensor_tensor(near[:], windows[t][:].indirect(lists[2][:, entries]), centre, ALU.subtract)
-            nc.scalar.activation(soft[:, 2, :], near[:], ACT.Sigmoid, scale=4.0)
+        def census(t, c0, width, far=None, near=None, near_first=False):
+            if far is None:
+                far = ring.tile([P, 2, width], F32, name="far", tag="far")[:]
+            if near is None:
+                near = ring.tile([P, width], F32, name="near", tag="near")[:]
+            soft = ring.tile([P, 3, width], F32, name="soft", tag="soft", bufs=3)
+
+            def differences(plane, l, step):
+                for s0 in range(0, width, step):
+                    entries = slice((c0 + s0) // 16, (c0 + s0 + step) // 16)
+                    nc.vector.tensor_tensor(plane[:, s0 : s0 + step], windows[t][:].indirect(lists[l][:, entries]), centres[t][:, c0 + s0 : c0 + s0 + step], ALU.subtract)
+
+            def far_pair():
+                differences(far[:, 0, :], 0, HALF if t == 0 else width)
+                differences(far[:, 1, :], 1, width)
+                nc.scalar.activation(soft[:, 0:2, :], far, ACT.Tanh, scale=2.0)
+
+            if not near_first:
+                far_pair()
+            differences(near, 2, width)
+            nc.scalar.activation(soft[:, 2, :], near, ACT.Sigmoid, scale=4.0)
+            if near_first:
+                far_pair()
             return soft
 
         def add_up(soft, bank, e, first=0):
@@ -140,16 +158,19 @@ def tile_picked_census8_none_p_kernel(tc, x_words, x_scales, w1, gn, w2, offs, p
                 for i, l in enumerate(terms):
                     nc.tensor.matmul(bank[:, e, b, :], soft[:, l, (first + b) * P : (first + b + 1) * P], ident[:], start=(i == 0), stop=(i == len(terms) - 1), is_transpose=True)
 
-        def direct(t, soft, z_bf):
-            part = ring.tile([P, 2, P], F32, name="part", tag="part")
-            nc.vector.scalar_tensor_tensor(part[:, 0, :], soft[:, 0, :], 2.0, soft[:, 1, :], ALU.mult, ALU.add)
-            nc.vector.tensor_scalar(part[:, 1, :], part[:, 0, :], -0.5, gain_half[:, t : t + 1], ALU.add, ALU.mult)
-            nc.vector.scalar_tensor_tensor(z_bf[:, :, t], soft[:, 2, :], gain_half[:, t : t + 1], part[:, 1, :], ALU.mult, ALU.add)
+        def far_sum(soft, part):
+            nc.vector.scalar_tensor_tensor(part, soft[:, 0, :], 2.0, soft[:, 1, :], ALU.mult, ALU.add)
 
-        def weigh(bank, u, targets):
+        def far_weigh(t, part, weighed):
+            nc.vector.tensor_scalar(weighed, part, -0.5, gain_half[:, t : t + 1], ALU.add, ALU.mult)
+
+        def finish(t, soft, weighed, z_bf):
+            nc.vector.scalar_tensor_tensor(z_bf[:, :, t], soft[:, 2, :], gain_half[:, t : t + 1], weighed, ALU.mult, ALU.add)
+
+        def weigh(bank, gains, targets, tag):
             blocks = bank.shape[2]
-            z_rows = ring.tile([P, blocks, P, 2], BF16, name="z_rows", tag="z_rows")
-            nc.vector.scalar_tensor_tensor(z_rows[:].rearrange("j b p e -> j (b p) e"), bank[:].rearrange("j e b p -> j (b p) e"), -0.5, half_gain[:, u, 0:blocks].rearrange("j b p e -> j (b p) e"), ALU.add, ALU.mult)
+            z_rows = keep.tile([P, blocks, P, 2], BF16, name="z_rows", tag=tag)
+            nc.vector.scalar_tensor_tensor(z_rows[:].rearrange("j b p e -> j (b p) e"), bank[:].rearrange("j e b p -> j (b p) e"), -0.5, gains[:].rearrange("j b p e -> j (b p) e"), ALU.add, ALU.mult)
             pairs = z_rows[:].rearrange("j b p e -> j (b p e)").bitcast(F32)
             for b in range(blocks):
                 nc.tensor.transpose(targets[b], pairs[:, b * P : (b + 1) * P], ident[:])
@@ -179,7 +200,7 @@ def tile_picked_census8_none_p_kernel(tc, x_words, x_scales, w1, gn, w2, offs, p
                     nc.scalar.copy(result[:], o_ps[:])
                 nc.sync.dma_start(out[rows * h * P : rows * (h + 1) * P, c0 : c0 + width].rearrange("(i p) j -> p i j", p=P), result[:])
 
-        z_a = keep.tile([P, HALF, PACK], BF16, name="z_a", align_bytes=64)
+        z_a = keep.tile([P, HALF, PACK], BF16, name="z_a", tag="after_pack", align_bytes=64)
         z_b = keep.tile([P, P, PACK], BF16, name="z_b", align_bytes=64)
         z_c = keep.tile([P, P, PACK], BF16, name="z_c", align_bytes=64)
         turned_low = turn.tile([P, 2, HALF], F32, name="turned_low", tag="turned")
@@ -187,32 +208,49 @@ def tile_picked_census8_none_p_kernel(tc, x_words, x_scales, w1, gn, w2, offs, p
 
         later_tile(1)
         front = [sums.tile([P, 2, 2, P], F32, name="front", tag="bank") for h in range(2)]
-        for t in range(2):
-            soft = census(t, 0, S)
-            for h in range(2):
-                add_up(soft, front[h], t, 2 * h)
-                round_w2(2 * t + h)
-            later_tile(t + 2)
+        later_tile(2)
+        later_tile(3)
+        spread_gain()
+        soft = census(0, 0, S)
+        for h in range(2):
+            add_up(soft, front[h], 0, 2 * h)
+        round_w2(0)
+        add_up(census(1, 0, HALF), front[0], 1)
+        round_w2(1)
         back_a = sums.tile([P, 2, 2, P], F32, name="back_a", tag="bank")
         add_up(census(2, 0, HALF), back_a, 0)
-        weigh(front[0], 0, [turned_low[:, 0, 0:P], turned_low[:, 0, P:HALF]])
-        weigh(front[1], 0, [turned_high[:, 0, :], turned_high[:, 2, :]])
+        round_w2(2)
+        weigh(front[0], gain_front[0], [turned_low[:, 0, 0:P], turned_low[:, 0, P:HALF]], "rows_front0")
         add_up(census(3, 0, HALF), back_a, 1)
+        round_w2(3)
+        held_0 = keep.tile([P, 3, HALF], F32, name="held_0", tag="after_front0")
+        add_up(census(1, HALF, HALF, held_0[:, 0:2, :], held_0[:, 2, :]), front[1], 1)
         nc.vector.quantize_mx(w2_codes[:].bitcast(FP8X4), w2_scales[:], w2_bf[:].rearrange("p n j -> p (n j)"))
-        back_b = sums.tile([P, 2, 1, P], F32, name="back_b", tag="bank")
-        add_up(census(2, HALF, P), back_b, 0)
-        weigh(back_a, 1, [turned_low[:, 1, 0:P], turned_low[:, 1, P:HALF]])
-        add_up(census(3, HALF, P), back_b, 1)
+        weigh(back_a, gain_a, [turned_low[:, 1, 0:P], turned_low[:, 1, P:HALF]], "rows_a")
         nc.scalar.copy(words_of(z_a), turned_low[:].rearrange("p u j -> p j u"))
-        nc.scalar.copy(words_of(z_c)[:, :, 0], turned_high[:, 2, :])
+        back_b = sums.tile([P, 2, 1, P], F32, name="back_b", tag="bank")
+        near_a = keep.tile([P, HALF], F32, name="near_a", tag="after_a")
+        far_a = keep.tile([P, 2, HALF], F32, name="far_a", tag="rows_a")
+        soft2 = census(2, HALF, HALF, far_a[:], near_a[:], True)
+        add_up(soft2, back_b, 0)
         packed_a = pack(z_a)
-        soft2 = census(2, HALF + P, P)
-        weigh(back_b, 1, [turned_high[:, 1, :]])
+        weigh(front[1], gain_front[1], [turned_high[:, 0, :], turned_high[:, 2, :]], "rows_front1")
+        held_pack = keep.tile([P, 5, P], F32, name="held_pack", tag="after_pack", align_bytes=64)
+        nc.scalar.copy(words_of(z_c)[:, :, 0], turned_high[:, 2, :])
+        add_up(census(3, HALF, P, held_pack[:, 0:2, :], held_pack[:, 2, :]), back_b, 1)
         project(0, *packed_a, False)
-        soft3 = census(3, HALF + P, P)
+        part2 = keep.tile([P, P], F32, name="part2")
+        far_sum(soft2[:, :, P:HALF], part2[:])
+        weigh(back_b, gain_b, [turned_high[:, 1, :]], "rows_b")
         nc.scalar.copy(words_of(z_b), turned_high[:, 0:2, :].rearrange("p u j -> p j u"))
-        direct(2, soft2, z_c)
+        near_b = keep.tile([P, P], F32, name="near_b", tag="rows_b")
+        soft3 = census(3, HALF + P, P, held_pack[:, 3:5, :], near_b[:])
+        parts = keep.tile([P, 3, P], F32, name="parts", tag="after_b")
+        far_sum(soft3, parts[:, 0, :])
+        far_weigh(2, part2[:], parts[:, 1, :])
+        far_weigh(3, parts[:, 0, :], parts[:, 2, :])
+        finish(2, soft2[:, :, P:HALF], parts[:, 1, :], z_c)
         packed_b = pack(z_b)
-        direct(3, soft3, z_c)
+        finish(3, soft3, parts[:, 2, :], z_c)
         project(HALF, *packed_b, False)
         project(HALF + P, *pack(z_c), True)

@@ -19,6 +19,8 @@ ALU = mybir.AluOpType
 P = 128
 PACK = 4
 HALF = S // 2
+SCALAR_SHARE = 44
+WIDE = 3
 
 
 def tile_picked_census8_none_p_kernel(tc, x_words, x_scales, w1, gn, w2, offs, p1, p2, p3, out):
@@ -26,8 +28,8 @@ def tile_picked_census8_none_p_kernel(tc, x_words, x_scales, w1, gn, w2, offs, p
     with ExitStack() as ctx:
         keep = ctx.enter_context(tc.tile_pool(name="keep", bufs=1))
         ring = ctx.enter_context(tc.tile_pool(name="ring", bufs=2))
-        acc = ctx.enter_context(tc.psum_pool(name="acc", bufs=3))
-        sums = ctx.enter_context(tc.psum_pool(name="sums", bufs=3))
+        acc = ctx.enter_context(tc.psum_pool(name="acc", bufs=2))
+        sums = ctx.enter_context(tc.psum_pool(name="sums", bufs=4))
         turn = ctx.enter_context(tc.psum_pool(name="turn", bufs=2))
 
         def load_list(name, source):
@@ -42,11 +44,10 @@ def tile_picked_census8_none_p_kernel(tc, x_words, x_scales, w1, gn, w2, offs, p
 
         picks = load_list("picks", offs)
         w1_rows = w1.rearrange("(p j) c -> p j c", j=PACK)
-        w1_early = keep.tile([P, 2, H], F32, name="w1_early")
-        nc.sync.dma_start(w1_early[:], w1_rows[:, 0:2, :])
+        w1_raw = keep.tile([P, PACK, H], F32, name="w1_raw", tag="raw")
+        nc.sync.dma_start(w1_raw[:, 0:2, :], w1_rows[:, 0:2, :])
         nc.sync.dma_start(scale_table[0:P:8, :].bitcast(I32), x_scales[0].bitcast(I32))
-        w1_late = keep.tile([P, 2, H], F32, name="w1_late", tag="raw")
-        nc.sync.dma_start(w1_late[:], w1_rows[:, 2:4, :])
+        nc.sync.dma_start(w1_raw[:, 2:4, :], w1_rows[:, 2:4, :])
         word_table = keep.tile([P, T], U32, name="word_table", align_bytes=64)
         nc.sync.dma_start(word_table[:].bitcast(I32), x_words[0].rearrange("p n t -> p (n t)").bitcast(I32))
         lists = (load_list("list3", p3), load_list("list2", p2), load_list("list1", p1))
@@ -64,8 +65,9 @@ def tile_picked_census8_none_p_kernel(tc, x_words, x_scales, w1, gn, w2, offs, p
 
         w1_bf = keep.tile([P, PACK, P, PACK], BF16, name="w1_bf", align_bytes=64)
         w1_dst = w1_bf[:].rearrange("p t m j -> p m j t")
-        nc.scalar.copy(w1_dst[:, :, 0:2, :], w1_early[:].rearrange("p j (m t) -> p m j t", t=PACK))
-        nc.vector.tensor_copy(w1_dst[:, :, 2:4, :], w1_late[:].rearrange("p j (m t) -> p m j t", t=PACK))
+        w1_src = w1_raw[:].rearrange("p j (m t) -> p m j t", t=PACK)
+        nc.scalar.copy(w1_dst[:, 0:SCALAR_SHARE], w1_src[:, 0:SCALAR_SHARE])
+        nc.vector.tensor_copy(w1_dst[:, SCALAR_SHARE:P], w1_src[:, SCALAR_SHARE:P])
         w2_raw = keep.tile([P, PACK, N], F32, name="w2_raw", tag="raw")
         nc.sync.dma_start(w2_raw[:], w2.rearrange("(p j) c -> p j c", j=PACK))
         gain = keep.tile([P, PACK], F32, name="gain", tag="staged", align_bytes=64)
@@ -83,9 +85,9 @@ def tile_picked_census8_none_p_kernel(tc, x_words, x_scales, w1, gn, w2, offs, p
             cols = slice(t * P, (t + 1) * P)
             nc.tensor.matmul_mx(y_ps, w1_codes[:, cols].bitcast(FP8X4), w1_scales[:, cols], x_codes[:, cells].bitcast(FP8X4), x_bytes[:, cells], start=True, stop=True)
 
-        windows = [keep.tile([P, 2 * S if t == 0 else S], F32, name="window%d" % t) for t in range(PACK)]
+        windows = [keep.tile([P, 2 * S if t < WIDE else S], F32, name="window%d" % t) for t in range(PACK)]
         nc.gpsimd.memset(windows[0][:, S : 2 * S], 0.0)
-        centres = [keep.tile([P, S], F32, name="centre%d" % t)[:] for t in range(PACK)]
+        centres = [windows[t + 1][:, S : 2 * S] if t + 1 < WIDE else keep.tile([P, S], F32, name="centre%d" % t)[:] for t in range(PACK)]
 
         low, high = slice(0, HALF), slice(HALF, S)
         y_low = acc.tile([P, HALF], F32, name="y_low", tag="acc")
@@ -103,19 +105,18 @@ def tile_picked_census8_none_p_kernel(tc, x_words, x_scales, w1, gn, w2, offs, p
             nc.scalar.copy(windows[t][:, 0:S], y_ps[:])
             nc.sync.dma_start(centres[t], windows[t][:, 0:S])
 
-        gain_front = [keep.tile([P, 2, P, 2], F32, name="gain_front%d" % h, tag="after_front%d" % h) for h in range(2)]
-        gain_a = keep.tile([P, 2, P, 2], F32, name="gain_a", tag="after_a")
-        gain_b = keep.tile([P, 1, P, 2], F32, name="gain_b", tag="after_b")
+        gain_rows = keep.tile([P, P, PACK], F32, name="gain_rows")
+        gain_a = keep.tile([P, P, PACK], F32, name="gain_a", tag="after_a")
+        gain_b = keep.tile([P, P, PACK], F32, name="gain_b", tag="after_b")
         gain_half = keep.tile([P, PACK], F32, name="gain_half")
 
         def spread_gain():
-            gain_ps = acc.tile([P, PACK, P], F32, name="gain_ps", tag="acc")
+            gain_ps = turn.tile([P, PACK, P], F32, name="gain_ps", tag="turned")
             for t in range(PACK):
                 nc.tensor.transpose(gain_ps[:, t, :], gain[:, t : t + 1].to_broadcast([P, P]), ident[:])
-            spread = keep.tile([P, 2, P, 2], F32, name="spread")
-            nc.scalar.activation(spread[:], gain_ps[:].rearrange("j (u e) p -> j u p e", e=2), ACT.Copy, scale=0.5)
-            for held, u in ((gain_front[0], 0), (gain_front[1], 0), (gain_a, 1), (gain_b, 1)):
-                nc.sync.dma_start(held[:], spread[:, u : u + 1].to_broadcast([P, held.shape[1], P, 2]))
+            nc.scalar.activation(gain_rows[:], gain_ps[:].rearrange("j t p -> j p t"), ACT.Copy, scale=0.5)
+            nc.sync.dma_start(gain_a[:], gain_rows[:])
+            nc.sync.dma_start(gain_b[:], gain_rows[:])
             nc.scalar.activation(gain_half[:], gain[:], ACT.Copy, scale=0.5)
 
         w2_bf = keep.tile([P, N, PACK], BF16, name="w2_bf", align_bytes=64)
@@ -141,8 +142,13 @@ def tile_picked_census8_none_p_kernel(tc, x_words, x_scales, w1, gn, w2, offs, p
 
             def far_pair():
                 differences(far[:, 0, :], 0, HALF if t == 0 else width)
+                if width > P:
+                    nc.scalar.activation(soft[:, 0, :], far[:, 0, :], ACT.Tanh, scale=2.0)
                 differences(far[:, 1, :], 1, width)
-                nc.scalar.activation(soft[:, 0:2, :], far, ACT.Tanh, scale=2.0)
+                if width > P:
+                    nc.scalar.activation(soft[:, 1, :], far[:, 1, :], ACT.Tanh, scale=2.0)
+                else:
+                    nc.scalar.activation(soft[:, 0:2, :], far, ACT.Tanh, scale=2.0)
 
             if not near_first:
                 far_pair()
@@ -152,11 +158,10 @@ def tile_picked_census8_none_p_kernel(tc, x_words, x_scales, w1, gn, w2, offs, p
                 far_pair()
             return soft
 
-        def add_up(soft, bank, e, first=0):
-            terms = (0, 0, 1, 2)
-            for b in range(bank.shape[2]):
-                for i, l in enumerate(terms):
-                    nc.tensor.matmul(bank[:, e, b, :], soft[:, l, (first + b) * P : (first + b + 1) * P], ident[:], start=(i == 0), stop=(i == len(terms) - 1), is_transpose=True)
+        def add_up(soft, t, first, count, terms=(0, 0, 1, 2)):
+            for i, l in enumerate(terms):
+                for b in range(count):
+                    nc.tensor.matmul(banks[first + b][:, t, :], soft[:, l, b * P : (b + 1) * P], ident[:], start=(i == 0), stop=(i == len(terms) - 1), is_transpose=True)
 
         def far_sum(soft, part):
             nc.vector.scalar_tensor_tensor(part, soft[:, 0, :], 2.0, soft[:, 1, :], ALU.mult, ALU.add)
@@ -167,13 +172,19 @@ def tile_picked_census8_none_p_kernel(tc, x_words, x_scales, w1, gn, w2, offs, p
         def finish(t, soft, weighed, z_bf):
             nc.vector.scalar_tensor_tensor(z_bf[:, :, t], soft[:, 2, :], gain_half[:, t : t + 1], weighed, ALU.mult, ALU.add)
 
-        def weigh(bank, gains, targets, tag):
-            blocks = bank.shape[2]
-            z_rows = keep.tile([P, blocks, P, 2], BF16, name="z_rows", tag=tag)
-            nc.vector.scalar_tensor_tensor(z_rows[:].rearrange("j b p e -> j (b p) e"), bank[:].rearrange("j e b p -> j (b p) e"), -0.5, gains[:].rearrange("j b p e -> j (b p) e"), ALU.add, ALU.mult)
-            pairs = z_rows[:].rearrange("j b p e -> j (b p e)").bitcast(F32)
-            for b in range(blocks):
-                nc.tensor.transpose(targets[b], pairs[:, b * P : (b + 1) * P], ident[:])
+        def weigh(b, gains, target, tag):
+            z_rows = keep.tile([P, P, PACK], BF16, name="z_rows", tag=tag)
+            nc.vector.scalar_tensor_tensor(z_rows[:], banks[b][:].rearrange("j t p -> j p t"), -0.5, gains[:], ALU.add, ALU.mult)
+            pairs = z_rows[:].rearrange("j p t -> j (p t)").bitcast(F32).rearrange("j (p u) -> j p u", u=2)
+            for u in range(2):
+                nc.tensor.transpose(target[:, u, :], pairs[:, :, u], ident[:])
+
+        def weigh_three(b, target):
+            z_rows = keep.tile([P, 2, P, 2], BF16, name="z_rows_three", tag="after_a")
+            nc.vector.scalar_tensor_tensor(z_rows[:, 0], banks[b][:, 0:2, :].rearrange("j t p -> j p t"), -0.5, gain_rows[:, :, 0:2], ALU.add, ALU.mult)
+            nc.vector.scalar_tensor_tensor(z_rows[:, 1], banks[b][:, 2, :].unsqueeze(2).to_broadcast([P, P, 2]), -0.5, gain_rows[:, :, 2:3].to_broadcast([P, P, 2]), ALU.add, ALU.mult)
+            for u in range(2):
+                nc.tensor.transpose(target[:, u, :], z_rows[:, u].rearrange("j p e -> j (p e)").bitcast(F32), ident[:])
 
         def words_of(z_bf):
             return z_bf[:].rearrange("p j t -> p (j t)").bitcast(F32).rearrange("p (j u) -> p j u", u=2)
@@ -185,72 +196,53 @@ def tile_picked_census8_none_p_kernel(tc, x_words, x_scales, w1, gn, w2, offs, p
             nc.vector.quantize_mx(z_codes[:].bitcast(FP8X4), z_scales[:], z_bf[:].rearrange("p j t -> p (j t)"))
             return z_codes, z_scales
 
-        def project(c0, z_codes, z_scales, last):
+        def project(c0, z_codes, z_scales, rows, banks, movers, tags=("", "")):
             width = z_codes.shape[1]
-            rows = 2
-            for h in range(4 // rows):
-                o_ps = acc.tile([P, rows, width], F32, name="o_ps", tag="acc")
+            for h in range(PACK // rows):
+                pool, tag = banks[h]
+                o_ps = pool.tile([P, rows, width], F32, name="o_ps", tag=tag)
                 for i in range(rows):
                     cols = slice((rows * h + i) * P, (rows * h + i + 1) * P)
                     nc.tensor.matmul_mx(o_ps[:, i, :], w2_codes[:, cols].bitcast(FP8X4), w2_scales[:, cols], z_codes[:].bitcast(FP8X4), z_scales[:], start=True, stop=True)
-                result = ring.tile([P, rows, width], F32, name="result", tag="result", bufs=6)
-                if last and h == 1:
-                    nc.vector.tensor_copy(result[:], o_ps[:])
-                else:
-                    nc.scalar.copy(result[:], o_ps[:])
+                result = keep.tile([P, rows, width], F32, name="result%d_%d" % (c0, h), tag=tags[h % 2] or "result%d_%d" % (c0, h), align_bytes=64)
+                movers[h](result[:], o_ps[:])
                 nc.sync.dma_start(out[rows * h * P : rows * (h + 1) * P, c0 : c0 + width].rearrange("(i p) j -> p i j", p=P), result[:])
 
         z_a = keep.tile([P, HALF, PACK], BF16, name="z_a", tag="after_pack", align_bytes=64)
         z_b = keep.tile([P, P, PACK], BF16, name="z_b", align_bytes=64)
         z_c = keep.tile([P, P, PACK], BF16, name="z_c", align_bytes=64)
-        turned_low = turn.tile([P, 2, HALF], F32, name="turned_low", tag="turned")
-        turned_high = turn.tile([P, 3, P], F32, name="turned_high", tag="turned")
-
         later_tile(1)
-        front = [sums.tile([P, 2, 2, P], F32, name="front", tag="bank") for h in range(2)]
         later_tile(2)
         later_tile(3)
         spread_gain()
-        soft = census(0, 0, S)
-        for h in range(2):
-            add_up(soft, front[h], 0, 2 * h)
-        round_w2(0)
-        add_up(census(1, 0, HALF), front[0], 1)
-        round_w2(1)
-        back_a = sums.tile([P, 2, 2, P], F32, name="back_a", tag="bank")
-        add_up(census(2, 0, HALF), back_a, 0)
-        round_w2(2)
-        weigh(front[0], gain_front[0], [turned_low[:, 0, 0:P], turned_low[:, 0, P:HALF]], "rows_front0")
-        add_up(census(3, 0, HALF), back_a, 1)
-        round_w2(3)
-        held_0 = keep.tile([P, 3, HALF], F32, name="held_0", tag="after_front0")
-        add_up(census(1, HALF, HALF, held_0[:, 0:2, :], held_0[:, 2, :]), front[1], 1)
+        banks = [sums.tile([P, PACK, P], F32, name="bank", tag="bank") for b in range(4)]
+        for t in range(3):
+            add_up(census(t, 0, S), t, 0, 4)
+            if t < 2:
+                round_w2(2 * t)
+                round_w2(2 * t + 1)
+        turned_low = turn.tile([P, 2, 2, P], F32, name="turned_low", tag="turned")
+        turned_high = turn.tile([P, 2, 2, P], F32, name="turned_high", tag="turned")
+        add_up(census(3, 0, HALF), 3, 0, 2)
+        add_up(census(3, HALF, P), 3, 2, 1)
         nc.vector.quantize_mx(w2_codes[:].bitcast(FP8X4), w2_scales[:], w2_bf[:].rearrange("p n j -> p (n j)"))
-        weigh(back_a, gain_a, [turned_low[:, 1, 0:P], turned_low[:, 1, P:HALF]], "rows_a")
-        nc.scalar.copy(words_of(z_a), turned_low[:].rearrange("p u j -> p j u"))
-        back_b = sums.tile([P, 2, 1, P], F32, name="back_b", tag="bank")
-        near_a = keep.tile([P, HALF], F32, name="near_a", tag="after_a")
-        far_a = keep.tile([P, 2, HALF], F32, name="far_a", tag="rows_a")
-        soft2 = census(2, HALF, HALF, far_a[:], near_a[:], True)
-        add_up(soft2, back_b, 0)
+        for b in range(2):
+            weigh(b, gain_a, turned_low[:, b], "rows_a%d" % b)
+        weigh(2, gain_b, turned_high[:, 0], "rows_b")
+        weigh_three(3, turned_high[:, 1])
+        nc.scalar.copy(words_of(z_a).rearrange("p (b j) u -> p b j u", b=2), turned_low[:].rearrange("p b u j -> p b j u"))
+        nc.scalar.copy(words_of(z_b), turned_high[:, 0].rearrange("p u j -> p j u"))
+        nc.scalar.copy(words_of(z_c), turned_high[:, 1].rearrange("p u j -> p j u"))
         packed_a = pack(z_a)
-        weigh(front[1], gain_front[1], [turned_high[:, 0, :], turned_high[:, 2, :]], "rows_front1")
-        held_pack = keep.tile([P, 5, P], F32, name="held_pack", tag="after_pack", align_bytes=64)
-        nc.scalar.copy(words_of(z_c)[:, :, 0], turned_high[:, 2, :])
-        add_up(census(3, HALF, P, held_pack[:, 0:2, :], held_pack[:, 2, :]), back_b, 1)
-        project(0, *packed_a, False)
-        part2 = keep.tile([P, P], F32, name="part2")
-        far_sum(soft2[:, :, P:HALF], part2[:])
-        weigh(back_b, gain_b, [turned_high[:, 1, :]], "rows_b")
-        nc.scalar.copy(words_of(z_b), turned_high[:, 0:2, :].rearrange("p u j -> p j u"))
-        near_b = keep.tile([P, P], F32, name="near_b", tag="rows_b")
-        soft3 = census(3, HALF + P, P, held_pack[:, 3:5, :], near_b[:])
-        parts = keep.tile([P, 3, P], F32, name="parts", tag="after_b")
-        far_sum(soft3, parts[:, 0, :])
-        far_weigh(2, part2[:], parts[:, 1, :])
-        far_weigh(3, parts[:, 0, :], parts[:, 2, :])
-        finish(2, soft2[:, :, P:HALF], parts[:, 1, :], z_c)
         packed_b = pack(z_b)
-        finish(3, soft3, parts[:, 2, :], z_c)
-        project(HALF, *packed_b, False)
-        project(HALF + P, *pack(z_c), True)
+        far_c = keep.tile([P, 2, P], F32, name="far_c", tag="after_b")
+        near_c = keep.tile([P, P], F32, name="near_c", tag="after_pack", align_bytes=64)
+        soft3 = census(3, HALF + P, P, far_c[:], near_c[:])
+        parts = keep.tile([P, 2, P], F32, name="parts")
+        far_sum(soft3, parts[:, 0, :])
+        far_weigh(3, parts[:, 0, :], parts[:, 1, :])
+        finish(3, soft3, parts[:, 1, :], z_c)
+        packed_c = pack(z_c)
+        project(0, *packed_a, 2, [(acc, "acc")] * 2, [nc.scalar.copy] * 2, ("after_pack", ""))
+        project(HALF, *packed_b, 2, [(sums, "bank")] * 2, [nc.scalar.copy, nc.vector.tensor_copy])
+        project(HALF + P, *packed_c, 2, [(sums, "bank")] * 2, [nc.scalar.copy, nc.vector.tensor_copy])

@@ -20,7 +20,8 @@ P = 128
 PACK = 4
 HALF = S // 2
 SCALAR_SHARE = 44
-WIDE = 3
+HELD = 2
+WIDE = 4
 
 
 def tile_picked_census8_none_p_kernel(tc, x_words, x_scales, w1, gn, w2, offs, p1, p2, p3, out):
@@ -105,72 +106,60 @@ def tile_picked_census8_none_p_kernel(tc, x_words, x_scales, w1, gn, w2, offs, p
             nc.scalar.copy(windows[t][:, 0:S], y_ps[:])
             nc.sync.dma_start(centres[t], windows[t][:, 0:S])
 
-        gain_rows = keep.tile([P, P, PACK], F32, name="gain_rows")
-        gain_a = keep.tile([P, P, PACK], F32, name="gain_a", tag="after_a")
-        gain_b = keep.tile([P, P, PACK], F32, name="gain_b", tag="after_b")
-        gain_half = keep.tile([P, PACK], F32, name="gain_half")
+        gain_rows = keep.tile([P, P, PACK], F32, name="gain_rows", tag="after_c", align_bytes=64)
+        gain_held = keep.tile([P, P, PACK], F32, name="gain_held", tag="after_held", align_bytes=64)
 
         def spread_gain():
             gain_ps = turn.tile([P, PACK, P], F32, name="gain_ps", tag="turned")
             for t in range(PACK):
                 nc.tensor.transpose(gain_ps[:, t, :], gain[:, t : t + 1].to_broadcast([P, P]), ident[:])
             nc.scalar.activation(gain_rows[:], gain_ps[:].rearrange("j t p -> j p t"), ACT.Copy, scale=0.5)
-            nc.sync.dma_start(gain_a[:], gain_rows[:])
-            nc.sync.dma_start(gain_b[:], gain_rows[:])
-            nc.scalar.activation(gain_half[:], gain[:], ACT.Copy, scale=0.5)
+            nc.sync.dma_start(gain_held[:], gain_rows[:])
 
+        w2_codes = [keep.tile([P, HALF], U32, name="w2_low", align_bytes=64), keep.tile([P, HALF], U32, name="w2_high", tag="after_held", align_bytes=64)]
         w2_bf = keep.tile([P, N, PACK], BF16, name="w2_bf", align_bytes=64)
-        w2_codes = keep.tile([P, N], U32, name="w2_codes", align_bytes=64)
         w2_scales = keep.tile([P, N], U8, name="w2_scales", align_bytes=64)
         w2_src = w2_raw[:].rearrange("p j (c i) -> p c j i", i=4)
         w2_dst = w2_bf[:].rearrange("p (c i) j -> p c j i", i=4)
 
+        def pack_w2(half):
+            cols = slice(half * HALF, (half + 1) * HALF)
+            nc.vector.quantize_mx(w2_codes[half][:].bitcast(FP8X4), w2_scales[:, cols], w2_bf[:, cols].rearrange("p n j -> p (n j)"))
+
         def round_w2(quarter):
             nc.scalar.copy(w2_dst[:, 32 * quarter : 32 * (quarter + 1)], w2_src[:, 32 * quarter : 32 * (quarter + 1)])
 
-        def census(t, c0, width, far=None, near=None, near_first=False):
-            if far is None:
-                far = ring.tile([P, 2, width], F32, name="far", tag="far")[:]
-            if near is None:
-                near = ring.tile([P, width], F32, name="near", tag="near")[:]
-            soft = ring.tile([P, 3, width], F32, name="soft", tag="soft", bufs=3)
+        def differences(t, c0, plane, l, step):
+            width = plane.shape[1]
+            for s0 in range(0, width, step):
+                entries = slice((c0 + s0) // 16, (c0 + s0 + step) // 16)
+                nc.vector.tensor_tensor(plane[:, s0 : s0 + step], windows[t][:].indirect(lists[l][:, entries]), centres[t][:, c0 + s0 : c0 + s0 + step], ALU.subtract)
 
-            def differences(plane, l, step):
-                for s0 in range(0, width, step):
-                    entries = slice((c0 + s0) // 16, (c0 + s0 + step) // 16)
-                    nc.vector.tensor_tensor(plane[:, s0 : s0 + step], windows[t][:].indirect(lists[l][:, entries]), centres[t][:, c0 + s0 : c0 + s0 + step], ALU.subtract)
-
-            def far_pair():
-                differences(far[:, 0, :], 0, HALF if t == 0 else width)
+        def far_terms(t, c0, far, soft):
+            width = far.shape[2]
+            for l in range(2):
+                differences(t, c0, far[:, l, :], l, HALF if (t, l) == (0, 0) else width)
                 if width > P:
-                    nc.scalar.activation(soft[:, 0, :], far[:, 0, :], ACT.Tanh, scale=2.0)
-                differences(far[:, 1, :], 1, width)
-                if width > P:
-                    nc.scalar.activation(soft[:, 1, :], far[:, 1, :], ACT.Tanh, scale=2.0)
-                else:
-                    nc.scalar.activation(soft[:, 0:2, :], far, ACT.Tanh, scale=2.0)
+                    nc.scalar.activation(soft[:, l, :], far[:, l, :], ACT.Tanh, scale=2.0)
+            if width == P:
+                nc.scalar.activation(soft[:, 0:2, :], far, ACT.Tanh, scale=2.0)
 
-            if not near_first:
-                far_pair()
-            differences(near, 2, width)
+        def near_term(t, c0, near, soft):
+            differences(t, c0, near, 2, near.shape[1])
             nc.scalar.activation(soft[:, 2, :], near, ACT.Sigmoid, scale=4.0)
-            if near_first:
-                far_pair()
+
+        def census(t, c0, width):
+            far = ring.tile([P, 2, width], F32, name="far", tag="far")
+            near = ring.tile([P, width], F32, name="near", tag="near")
+            soft = ring.tile([P, 3, width], F32, name="soft", tag="soft", bufs=3)
+            far_terms(t, c0, far[:], soft)
+            near_term(t, c0, near[:], soft)
             return soft
 
-        def add_up(soft, t, first, count, terms=(0, 0, 1, 2)):
+        def add_up(soft, t, first, count, terms=(0, 0, 1, 2), opening=True, close=True):
             for i, l in enumerate(terms):
                 for b in range(count):
-                    nc.tensor.matmul(banks[first + b][:, t, :], soft[:, l, b * P : (b + 1) * P], ident[:], start=(i == 0), stop=(i == len(terms) - 1), is_transpose=True)
-
-        def far_sum(soft, part):
-            nc.vector.scalar_tensor_tensor(part, soft[:, 0, :], 2.0, soft[:, 1, :], ALU.mult, ALU.add)
-
-        def far_weigh(t, part, weighed):
-            nc.vector.tensor_scalar(weighed, part, -0.5, gain_half[:, t : t + 1], ALU.add, ALU.mult)
-
-        def finish(t, soft, weighed, z_bf):
-            nc.vector.scalar_tensor_tensor(z_bf[:, :, t], soft[:, 2, :], gain_half[:, t : t + 1], weighed, ALU.mult, ALU.add)
+                    nc.tensor.matmul(banks[first + b][:, t, :], soft[:, l, b * P : (b + 1) * P], ident[:], start=(opening and i == 0), stop=(close and i == len(terms) - 1), is_transpose=True)
 
         def weigh(b, gains, target, tag):
             z_rows = keep.tile([P, P, PACK], BF16, name="z_rows", tag=tag)
@@ -179,20 +168,13 @@ def tile_picked_census8_none_p_kernel(tc, x_words, x_scales, w1, gn, w2, offs, p
             for u in range(2):
                 nc.tensor.transpose(target[:, u, :], pairs[:, :, u], ident[:])
 
-        def weigh_three(b, target):
-            z_rows = keep.tile([P, 2, P, 2], BF16, name="z_rows_three", tag="after_a")
-            nc.vector.scalar_tensor_tensor(z_rows[:, 0], banks[b][:, 0:2, :].rearrange("j t p -> j p t"), -0.5, gain_rows[:, :, 0:2], ALU.add, ALU.mult)
-            nc.vector.scalar_tensor_tensor(z_rows[:, 1], banks[b][:, 2, :].unsqueeze(2).to_broadcast([P, P, 2]), -0.5, gain_rows[:, :, 2:3].to_broadcast([P, P, 2]), ALU.add, ALU.mult)
-            for u in range(2):
-                nc.tensor.transpose(target[:, u, :], z_rows[:, u].rearrange("j p e -> j (p e)").bitcast(F32), ident[:])
-
         def words_of(z_bf):
             return z_bf[:].rearrange("p j t -> p (j t)").bitcast(F32).rearrange("p (j u) -> p j u", u=2)
 
         def pack(z_bf):
             width = z_bf.shape[1]
-            z_codes = ring.tile([P, width], U32, name="z_codes", tag="z_codes", align_bytes=64, bufs=3)
-            z_scales = ring.tile([P, width], U8, name="z_scales", tag="z_scales", align_bytes=64, bufs=3)
+            z_codes = ring.tile([P, width], U32, name="z_codes", tag="z_codes", align_bytes=64, bufs=4)
+            z_scales = ring.tile([P, width], U8, name="z_scales", tag="z_scales", align_bytes=64, bufs=4)
             nc.vector.quantize_mx(z_codes[:].bitcast(FP8X4), z_scales[:], z_bf[:].rearrange("p j t -> p (j t)"))
             return z_codes, z_scales
 
@@ -203,14 +185,17 @@ def tile_picked_census8_none_p_kernel(tc, x_words, x_scales, w1, gn, w2, offs, p
                 o_ps = pool.tile([P, rows, width], F32, name="o_ps", tag=tag)
                 for i in range(rows):
                     cols = slice((rows * h + i) * P, (rows * h + i + 1) * P)
-                    nc.tensor.matmul_mx(o_ps[:, i, :], w2_codes[:, cols].bitcast(FP8X4), w2_scales[:, cols], z_codes[:].bitcast(FP8X4), z_scales[:], start=True, stop=True)
+                    nc.tensor.matmul_mx(o_ps[:, i, :], w2_codes[h][:, i * P : (i + 1) * P].bitcast(FP8X4), w2_scales[:, cols], z_codes[:].bitcast(FP8X4), z_scales[:], start=True, stop=True)
                 result = keep.tile([P, rows, width], F32, name="result%d_%d" % (c0, h), tag=tags[h % 2] or "result%d_%d" % (c0, h), align_bytes=64)
                 movers[h](result[:], o_ps[:])
                 nc.sync.dma_start(out[rows * h * P : rows * (h + 1) * P, c0 : c0 + width].rearrange("(i p) j -> p i j", p=P), result[:])
 
-        z_a = keep.tile([P, HALF, PACK], BF16, name="z_a", tag="after_pack", align_bytes=64)
-        z_b = keep.tile([P, P, PACK], BF16, name="z_b", align_bytes=64)
-        z_c = keep.tile([P, P, PACK], BF16, name="z_c", align_bytes=64)
+        def interleave(turned, name):
+            blocks = turned.shape[1]
+            z_bf = keep.tile([P, blocks * P, PACK], BF16, name=name, align_bytes=64)
+            nc.scalar.copy(words_of(z_bf).rearrange("p (b j) u -> p b j u", b=blocks), turned.rearrange("p b u j -> p b j u"))
+            return z_bf
+
         later_tile(1)
         later_tile(2)
         later_tile(3)
@@ -219,30 +204,27 @@ def tile_picked_census8_none_p_kernel(tc, x_words, x_scales, w1, gn, w2, offs, p
         for t in range(3):
             add_up(census(t, 0, S), t, 0, 4)
             if t < 2:
-                round_w2(2 * t)
-                round_w2(2 * t + 1)
-        turned_low = turn.tile([P, 2, 2, P], F32, name="turned_low", tag="turned")
-        turned_high = turn.tile([P, 2, 2, P], F32, name="turned_high", tag="turned")
-        add_up(census(3, 0, HALF), 3, 0, 2)
-        add_up(census(3, HALF, P), 3, 2, 1)
-        nc.vector.quantize_mx(w2_codes[:].bitcast(FP8X4), w2_scales[:], w2_bf[:].rearrange("p n j -> p (n j)"))
-        for b in range(2):
-            weigh(b, gain_a, turned_low[:, b], "rows_a%d" % b)
-        weigh(2, gain_b, turned_high[:, 0], "rows_b")
-        weigh_three(3, turned_high[:, 1])
-        nc.scalar.copy(words_of(z_a).rearrange("p (b j) u -> p b j u", b=2), turned_low[:].rearrange("p b u j -> p b j u"))
-        nc.scalar.copy(words_of(z_b), turned_high[:, 0].rearrange("p u j -> p j u"))
-        nc.scalar.copy(words_of(z_c), turned_high[:, 1].rearrange("p u j -> p j u"))
-        packed_a = pack(z_a)
-        packed_b = pack(z_b)
-        far_c = keep.tile([P, 2, P], F32, name="far_c", tag="after_b")
-        near_c = keep.tile([P, P], F32, name="near_c", tag="after_pack", align_bytes=64)
-        soft3 = census(3, HALF + P, P, far_c[:], near_c[:])
-        parts = keep.tile([P, 2, P], F32, name="parts")
-        far_sum(soft3, parts[:, 0, :])
-        far_weigh(3, parts[:, 0, :], parts[:, 1, :])
-        finish(3, soft3, parts[:, 1, :], z_c)
-        packed_c = pack(z_c)
-        project(0, *packed_a, 2, [(acc, "acc")] * 2, [nc.scalar.copy] * 2, ("after_pack", ""))
-        project(HALF, *packed_b, 2, [(sums, "bank")] * 2, [nc.scalar.copy, nc.vector.tensor_copy])
-        project(HALF + P, *packed_c, 2, [(sums, "bank")] * 2, [nc.scalar.copy, nc.vector.tensor_copy])
+                round_w2(2 - 2 * t)
+                round_w2(3 - 2 * t)
+        far = ring.tile([P, 2, S], F32, name="far", tag="far")
+        near = ring.tile([P, S], F32, name="near", tag="near")
+        soft = ring.tile([P, 3, S], F32, name="soft", tag="soft", bufs=3)
+        differences(3, 0, far[:, 0, :], 0, S)
+        nc.scalar.activation(soft[:, 0, :], far[:, 0, :], ACT.Tanh, scale=2.0)
+        for h in range(2):
+            cells = slice(h * HALF, (h + 1) * HALF)
+            differences(3, h * HALF, far[:, 1, cells], 1, HALF)
+            nc.scalar.activation(soft[:, 1, cells], far[:, 1, cells], ACT.Tanh, scale=2.0)
+            near_term(3, h * HALF, near[:, cells], soft[:, :, cells])
+            add_up(soft[:, :, cells], 3, 2 * h, 2)
+        z_tiles = []
+        for b in range(4):
+            turned = turn.tile([P, 1, 2, P], F32, name="turned", tag="turned")
+            weigh(b, gain_held if b == HELD else gain_rows, turned[:, 0], "rows%d" % b)
+            z_tiles.append(interleave(turned[:], "z%d" % b))
+        pack_w2(0)
+        packed = [pack(z_tiles[b]) for b in range(3)]
+        pack_w2(1)
+        packed.append(pack(z_tiles[3]))
+        for b in range(4):
+            project(b * P, *packed[b], 2, [(acc, "acc"), (sums, "bank")], [nc.scalar.copy, nc.vector.tensor_copy])

@@ -47,18 +47,15 @@ def tile_picked_census8_none_p_kernel(tc, x_words, x_scales, w1, gn, w2, offs, p
         w1_rows = w1.rearrange("(p j) c -> p j c", j=PACK)
         w1_raw = keep.tile([P, PACK, H], F32, name="w1_raw", tag="raw")
         nc.sync.dma_start(w1_raw[:, 0:2, :], w1_rows[:, 0:2, :])
-        nc.sync.dma_start(scale_table[0:P:8, :].bitcast(I32), x_scales[0].bitcast(I32))
+        for r in range(4):
+            nc.sync.dma_start(scale_table[r:P:32, :].bitcast(I32), x_scales[0, r:16:4, :].bitcast(I32))
         nc.sync.dma_start(w1_raw[:, 2:4, :], w1_rows[:, 2:4, :])
         word_table = keep.tile([P, T], U32, name="word_table", align_bytes=64)
         nc.sync.dma_start(word_table[:].bitcast(I32), x_words[0].rearrange("p n t -> p (n t)").bitcast(I32))
         lists = (load_list("list3", p3), load_list("list2", p2), load_list("list1", p1))
 
         x_bytes = keep.tile([P, S], U8, name="x_bytes", align_bytes=64)
-        nc.gpsimd.memset(x_bytes[:].bitcast(I32), 0)
-        picked_bytes = keep.tile([P, S], U8, name="picked_bytes", tag="staged", align_bytes=64)
-        nc.vector.tensor_copy(picked_bytes[:], scale_table[:].indirect(picks[:]))
-        for r in range(4):
-            nc.sync.dma_start(x_bytes[r:P:32, :].bitcast(I32), picked_bytes[8 * r : P : 32, :].bitcast(I32))
+        nc.vector.tensor_copy(x_bytes[:], scale_table[:].indirect(picks[:]))
 
         nc.scalar.activation(warm[:], warm[:], ACT.Sigmoid)
         ident = keep.tile([P, P], F32, name="ident")
@@ -71,7 +68,7 @@ def tile_picked_census8_none_p_kernel(tc, x_words, x_scales, w1, gn, w2, offs, p
         nc.vector.tensor_copy(w1_dst[:, SCALAR_SHARE:P], w1_src[:, SCALAR_SHARE:P])
         w2_raw = keep.tile([P, PACK, N], F32, name="w2_raw", tag="raw")
         nc.sync.dma_start(w2_raw[:], w2.rearrange("(p j) c -> p j c", j=PACK))
-        gain = keep.tile([P, PACK], F32, name="gain", tag="staged", align_bytes=64)
+        gain = keep.tile([P, PACK], F32, name="gain")
         nc.sync.dma_start(gain[:], gn.rearrange("(p t) o -> p (t o)", t=PACK))
 
         w1_codes = keep.tile([P, H], U32, name="w1_codes", align_bytes=64)

@@ -20,7 +20,6 @@ P = 128
 PACK = 4
 HALF = S // 2
 SCALAR_SHARE = 44
-HELD = 2
 WIDE = 4
 
 
@@ -68,7 +67,7 @@ def tile_picked_census8_none_p_kernel(tc, x_words, x_scales, w1, gn, w2, offs, p
         nc.vector.tensor_copy(w1_dst[:, SCALAR_SHARE:P], w1_src[:, SCALAR_SHARE:P])
         w2_raw = keep.tile([P, PACK, N], F32, name="w2_raw", tag="raw")
         nc.sync.dma_start(w2_raw[:], w2.rearrange("(p j) c -> p j c", j=PACK))
-        gain = keep.tile([P, PACK], F32, name="gain")
+        gain = keep.tile([P, PACK], F32, name="gain", tag="w1_bf", align_bytes=64)
         nc.sync.dma_start(gain[:], gn.rearrange("(p t) o -> p (t o)", t=PACK))
 
         w1_codes = keep.tile([P, H], U32, name="w1_codes", align_bytes=64)
@@ -103,17 +102,15 @@ def tile_picked_census8_none_p_kernel(tc, x_words, x_scales, w1, gn, w2, offs, p
             nc.scalar.copy(windows[t][:, 0:S], y_ps[:])
             nc.sync.dma_start(centres[t], windows[t][:, 0:S])
 
-        gain_rows = keep.tile([P, P, PACK], F32, name="gain_rows", tag="after_c", align_bytes=64)
-        gain_held = keep.tile([P, P, PACK], F32, name="gain_held", tag="after_held", align_bytes=64)
+        gain_rows = keep.tile([P, 2, P, 2], F32, name="gain_rows")
 
         def spread_gain():
             gain_ps = turn.tile([P, PACK, P], F32, name="gain_ps", tag="turned")
             for t in range(PACK):
                 nc.tensor.transpose(gain_ps[:, t, :], gain[:, t : t + 1].to_broadcast([P, P]), ident[:])
-            nc.scalar.activation(gain_rows[:], gain_ps[:].rearrange("j t p -> j p t"), ACT.Copy, scale=0.5)
-            nc.sync.dma_start(gain_held[:], gain_rows[:])
+            nc.scalar.activation(gain_rows[:], gain_ps[:].rearrange("j (u e) p -> j u p e", e=2), ACT.Copy, scale=0.5)
 
-        w2_codes = [keep.tile([P, HALF], U32, name="w2_low", align_bytes=64), keep.tile([P, HALF], U32, name="w2_high", tag="after_held", align_bytes=64)]
+        w2_codes = [keep.tile([P, HALF], U32, name="w2_low", align_bytes=64)]
         w2_bf = keep.tile([P, N, PACK], BF16, name="w2_bf", align_bytes=64)
         w2_scales = keep.tile([P, N], U8, name="w2_scales", align_bytes=64)
         w2_src = w2_raw[:].rearrange("p j (c i) -> p c j i", i=4)
@@ -156,14 +153,13 @@ def tile_picked_census8_none_p_kernel(tc, x_words, x_scales, w1, gn, w2, offs, p
         def add_up(soft, t, first, count, terms=(0, 0, 1, 2), opening=True, close=True):
             for i, l in enumerate(terms):
                 for b in range(count):
-                    nc.tensor.matmul(banks[first + b][:, t, :], soft[:, l, b * P : (b + 1) * P], ident[:], start=(opening and i == 0), stop=(close and i == len(terms) - 1), is_transpose=True)
+                    nc.tensor.matmul(banks[first + b][:, t % 2, t // 2, :], soft[:, l, b * P : (b + 1) * P], ident[:], start=(opening and i == 0), stop=(close and i == len(terms) - 1), is_transpose=True)
 
-        def weigh(b, gains, target, tag):
-            z_rows = keep.tile([P, P, PACK], BF16, name="z_rows", tag=tag)
-            nc.vector.scalar_tensor_tensor(z_rows[:], banks[b][:].rearrange("j t p -> j p t"), -0.5, gains[:], ALU.add, ALU.mult)
-            pairs = z_rows[:].rearrange("j p t -> j (p t)").bitcast(F32).rearrange("j (p u) -> j p u", u=2)
+        def weigh(b, gains, target):
+            z_rows = keep.tile([P, 2, P, 2], BF16, name="z_rows%d" % b, align_bytes=64)
+            nc.vector.scalar_tensor_tensor(z_rows[:].rearrange("j u p e -> j (u p) e"), banks[b][:].rearrange("j e u p -> j (u p) e"), -0.5, gains[:].rearrange("j u p e -> j (u p) e"), ALU.add, ALU.mult)
             for u in range(2):
-                nc.tensor.transpose(target[:, u, :], pairs[:, :, u], ident[:])
+                nc.tensor.transpose(target[:, u, :], z_rows[:, u].rearrange("j p e -> j (p e)").bitcast(F32), ident[:])
 
         def words_of(z_bf):
             return z_bf[:].rearrange("p j t -> p (j t)").bitcast(F32).rearrange("p (j u) -> p j u", u=2)
@@ -175,7 +171,7 @@ def tile_picked_census8_none_p_kernel(tc, x_words, x_scales, w1, gn, w2, offs, p
             nc.vector.quantize_mx(z_codes[:].bitcast(FP8X4), z_scales[:], z_bf[:].rearrange("p j t -> p (j t)"))
             return z_codes, z_scales
 
-        def project(c0, z_codes, z_scales, rows, banks, movers, tags=("", "")):
+        def project(c0, z_codes, z_scales, rows, banks, movers, results):
             width = z_codes.shape[1]
             for h in range(PACK // rows):
                 pool, tag = banks[h]
@@ -183,9 +179,9 @@ def tile_picked_census8_none_p_kernel(tc, x_words, x_scales, w1, gn, w2, offs, p
                 for i in range(rows):
                     cols = slice((rows * h + i) * P, (rows * h + i + 1) * P)
                     nc.tensor.matmul_mx(o_ps[:, i, :], w2_codes[h][:, i * P : (i + 1) * P].bitcast(FP8X4), w2_scales[:, cols], z_codes[:].bitcast(FP8X4), z_scales[:], start=True, stop=True)
-                result = keep.tile([P, rows, width], F32, name="result%d_%d" % (c0, h), tag=tags[h % 2] or "result%d_%d" % (c0, h), align_bytes=64)
-                movers[h](result[:], o_ps[:])
-                nc.sync.dma_start(out[rows * h * P : rows * (h + 1) * P, c0 : c0 + width].rearrange("(i p) j -> p i j", p=P), result[:])
+                movers[h](results[h][:, :, c0 % HALF : c0 % HALF + width], o_ps[:])
+                if c0 % HALF:
+                    nc.sync.dma_start(out[rows * h * P : rows * (h + 1) * P, c0 - P : c0 + P].rearrange("(i p) j -> p i j", p=P), results[h][:])
 
         def interleave(turned, name):
             blocks = turned.shape[1]
@@ -197,7 +193,7 @@ def tile_picked_census8_none_p_kernel(tc, x_words, x_scales, w1, gn, w2, offs, p
         later_tile(2)
         later_tile(3)
         spread_gain()
-        banks = [sums.tile([P, PACK, P], F32, name="bank", tag="bank") for b in range(4)]
+        banks = [sums.tile([P, 2, 2, P], F32, name="bank", tag="bank") for b in range(4)]
         for t in range(3):
             add_up(census(t, 0, S), t, 0, 4)
             if t < 2:
@@ -214,14 +210,18 @@ def tile_picked_census8_none_p_kernel(tc, x_words, x_scales, w1, gn, w2, offs, p
             nc.scalar.activation(soft[:, 1, cells], far[:, 1, cells], ACT.Tanh, scale=2.0)
             near_term(3, h * HALF, near[:, cells], soft[:, :, cells])
             add_up(soft[:, :, cells], 3, 2 * h, 2)
-        z_tiles = []
-        for b in range(4):
+        def leave(b):
             turned = turn.tile([P, 1, 2, P], F32, name="turned", tag="turned")
-            weigh(b, gain_held if b == HELD else gain_rows, turned[:, 0], "rows%d" % b)
-            z_tiles.append(interleave(turned[:], "z%d" % b))
+            weigh(b, gain_rows, turned[:, 0])
+            return interleave(turned[:], "z%d" % b)
+
+        z_tiles = [leave(b) for b in range(4)]
         pack_w2(0)
         packed = [pack(z_tiles[b]) for b in range(3)]
+        w2_codes.append(keep.tile([P, HALF], U32, name="w2_high", tag="z_rows1", align_bytes=64))
         pack_w2(1)
         packed.append(pack(z_tiles[3]))
         for b in range(4):
-            project(b * P, *packed[b], 2, [(acc, "acc"), (sums, "bank")], [nc.scalar.copy, nc.vector.tensor_copy])
+            if b % 2 == 0:
+                results = [keep.tile([P, 2, HALF], F32, name="result%d_%d" % (b, h)) for h in range(2)]
+            project(b * P, *packed[b], 2, [(acc, "acc"), (sums, "bank")], [nc.scalar.copy, nc.vector.tensor_copy], results)

@@ -20,7 +20,6 @@ P = 128
 PACK = 4
 HALF = S // 2
 SCALAR_SHARE = 44
-WIDE = 4
 
 
 def tile_picked_census8_none_p_kernel(tc, x_words, x_scales, w1, gn, w2, offs, p1, p2, p3, out):
@@ -43,6 +42,8 @@ def tile_picked_census8_none_p_kernel(tc, x_words, x_scales, w1, gn, w2, offs, p
         nc.gpsimd.memset(scale_table[:].bitcast(I32), 0)
 
         picks = load_list("picks", offs)
+        gain = keep.tile([P, PACK], F32, name="gain")
+        nc.sync.dma_start(gain[:], gn.rearrange("(p t) o -> p (t o)", t=PACK))
         w1_rows = w1.rearrange("(p j) c -> p j c", j=PACK)
         w1_raw = keep.tile([P, PACK, H], F32, name="w1_raw", tag="raw")
         nc.sync.dma_start(w1_raw[:, 0:2, :], w1_rows[:, 0:2, :])
@@ -51,6 +52,9 @@ def tile_picked_census8_none_p_kernel(tc, x_words, x_scales, w1, gn, w2, offs, p
         nc.sync.dma_start(w1_raw[:, 2:4, :], w1_rows[:, 2:4, :])
         word_table = keep.tile([P, T], U32, name="word_table", align_bytes=64)
         nc.sync.dma_start(word_table[:].bitcast(I32), x_words[0].rearrange("p n t -> p (n t)").bitcast(I32))
+        w2_rows = w2.rearrange("(p j) c -> p j c", j=PACK)
+        w2_raw = [keep.tile([P, PACK, HALF], F32, name="w2_raw_low")]
+        nc.sync.dma_start(w2_raw[0][:], w2_rows[:, :, 0:HALF])
         lists = (load_list("list3", p3), load_list("list2", p2), load_list("list1", p1))
 
         x_bytes = keep.tile([P, S], U8, name="x_bytes", align_bytes=64)
@@ -60,15 +64,19 @@ def tile_picked_census8_none_p_kernel(tc, x_words, x_scales, w1, gn, w2, offs, p
         ident = keep.tile([P, P], F32, name="ident")
         make_identity(nc, ident[:])
 
+        gain_rows = keep.tile([P, 2, P, 2], F32, name="gain_rows")
+        gain_ps = turn.tile([P, PACK, P], F32, name="gain_ps", tag="turned")
+        for t in range(PACK):
+            nc.tensor.transpose(gain_ps[:, t, :], gain[:, t : t + 1].to_broadcast([P, P]), ident[:])
+        nc.scalar.activation(gain_rows[:], gain_ps[:].rearrange("j (u e) p -> j u p e", e=2), ACT.Copy, scale=0.5)
+
         w1_bf = keep.tile([P, PACK, P, PACK], BF16, name="w1_bf", align_bytes=64)
         w1_dst = w1_bf[:].rearrange("p t m j -> p m j t")
         w1_src = w1_raw[:].rearrange("p j (m t) -> p m j t", t=PACK)
         nc.scalar.copy(w1_dst[:, 0:SCALAR_SHARE], w1_src[:, 0:SCALAR_SHARE])
         nc.vector.tensor_copy(w1_dst[:, SCALAR_SHARE:P], w1_src[:, SCALAR_SHARE:P])
-        w2_raw = keep.tile([P, PACK, N], F32, name="w2_raw", tag="raw")
-        nc.sync.dma_start(w2_raw[:], w2.rearrange("(p j) c -> p j c", j=PACK))
-        gain = keep.tile([P, PACK], F32, name="gain", tag="w1_bf", align_bytes=64)
-        nc.sync.dma_start(gain[:], gn.rearrange("(p t) o -> p (t o)", t=PACK))
+        w2_raw.append(keep.tile([P, PACK, HALF], F32, name="w2_raw_high", tag="raw"))
+        nc.sync.dma_start(w2_raw[1][:], w2_rows[:, :, HALF:N])
 
         w1_codes = keep.tile([P, H], U32, name="w1_codes", align_bytes=64)
         w1_scales = keep.tile([P, H], U8, name="w1_scales", align_bytes=64)
@@ -82,78 +90,69 @@ def tile_picked_census8_none_p_kernel(tc, x_words, x_scales, w1, gn, w2, offs, p
             cols = slice(t * P, (t + 1) * P)
             nc.tensor.matmul_mx(y_ps, w1_codes[:, cols].bitcast(FP8X4), w1_scales[:, cols], x_codes[:, cells].bitcast(FP8X4), x_bytes[:, cells], start=True, stop=True)
 
-        windows = [keep.tile([P, 2 * S if t < WIDE else S], F32, name="window%d" % t) for t in range(PACK)]
+        windows = [keep.tile([P, 2 * S], F32, name="window%d" % t) for t in range(PACK)]
         nc.gpsimd.memset(windows[0][:, S : 2 * S], 0.0)
-        centres = [windows[t + 1][:, S : 2 * S] if t + 1 < WIDE else keep.tile([P, S], F32, name="centre%d" % t)[:] for t in range(PACK)]
+        last_centre = keep.tile([P, S], F32, name="last_centre", tag="last_centre", align_bytes=64)
+        centres = [windows[t + 1][:, S : 2 * S] for t in range(PACK - 1)] + [last_centre[:]]
 
-        low, high = slice(0, HALF), slice(HALF, S)
+        def round_w2(half, tag):
+            rounded = keep.tile([P, HALF, PACK], BF16, name="w2_bf", tag=tag, align_bytes=64)
+            nc.gpsimd.tensor_scalar(rounded[:], w2_raw[half][:].rearrange("p j n -> p n j"), 1.0, 0.0, ALU.mult, ALU.add)
+            return rounded
+
+        w2_low_bf = round_w2(0, "w2_low_bf")
+
+        low, high, whole = slice(0, HALF), slice(HALF, S), slice(0, S)
         y_low = acc.tile([P, HALF], F32, name="y_low", tag="acc")
         y_high = acc.tile([P, HALF], F32, name="y_high", tag="acc")
         first_product(0, low, y_low[:])
         first_product(0, high, y_high[:])
+        later = {}
+        for t, (pool, tag) in ((1, (turn, "turned")), (2, (turn, "turned")), (3, (acc, "acc"))):
+            later[t] = pool.tile([P, S], F32, name="y_ps", tag=tag)
+            first_product(t, whole, later[t][:])
         nc.scalar.copy(windows[0][:, low], y_low[:])
         nc.vector.tensor_copy(windows[0][:, high], y_high[:])
         nc.scalar.copy(centres[0][:, low], y_low[:])
         nc.scalar.copy(centres[0][:, high], y_high[:])
 
-        def later_tile(t):
-            y_ps = acc.tile([P, S], F32, name="y_ps", tag="acc")
-            first_product(t, slice(0, S), y_ps[:])
-            nc.scalar.copy(windows[t][:, 0:S], y_ps[:])
-            nc.sync.dma_start(centres[t], windows[t][:, 0:S])
+        def open_window(t):
+            nc.scalar.copy(windows[t][:, whole], later[t][:])
+            nc.sync.dma_start(centres[t], windows[t][:, whole])
 
-        gain_rows = keep.tile([P, 2, P, 2], F32, name="gain_rows")
+        gaps = [keep.tile([P, 3, S], F32, name="gaps%d" % t) for t in range(PACK)]
+        softs = [keep.tile([P, 3, S], F32, name="soft%d" % t) for t in range(PACK)]
+        fetched = {}
+        banks = [sums.tile([P, 2, 2, P], F32, name="bank", tag="bank") for b in range(4)]
 
-        def spread_gain():
-            gain_ps = turn.tile([P, PACK, P], F32, name="gain_ps", tag="turned")
-            for t in range(PACK):
-                nc.tensor.transpose(gain_ps[:, t, :], gain[:, t : t + 1].to_broadcast([P, P]), ident[:])
-            nc.scalar.activation(gain_rows[:], gain_ps[:].rearrange("j (u e) p -> j u p e", e=2), ACT.Copy, scale=0.5)
+        def fetch(t):
+            fetched[t] = keep.tile([P, S], F32, name="fetched", tag="fetched%d" % t, align_bytes=64)
+            nc.scalar.activation(fetched[t][:], windows[t][:].indirect(lists[0][:]), ACT.Copy)
 
-        w2_codes = [keep.tile([P, HALF], U32, name="w2_low", align_bytes=64)]
-        w2_bf = keep.tile([P, N, PACK], BF16, name="w2_bf", align_bytes=64)
+        def difference(t, l, cells):
+            if l == 0 and t in fetched:
+                nc.vector.tensor_tensor(gaps[t][:, l, cells], fetched[t][:, cells], windows[t][:, cells], ALU.subtract)
+            else:
+                entries = slice(cells.start // 16, cells.stop // 16)
+                nc.vector.tensor_tensor(gaps[t][:, l, cells], windows[t][:].indirect(lists[l][:, entries]), centres[t][:, cells], ALU.subtract)
+
+        def term(t, l, cells):
+            difference(t, l, cells)
+            if l < 2:
+                nc.scalar.activation(softs[t][:, l, cells], gaps[t][:, l, cells], ACT.Tanh, scale=2.0)
+            else:
+                nc.scalar.activation(softs[t][:, l, cells], gaps[t][:, l, cells], ACT.Sigmoid, scale=4.0)
+            for b in range(cells.start // P, cells.stop // P):
+                for again in range(2 if l == 0 else 1):
+                    nc.tensor.matmul(banks[b][:, t % 2, t // 2, :], softs[t][:, l, b * P : (b + 1) * P], ident[:], start=(l == 0 and again == 0), stop=(l == 2), is_transpose=True)
+
+        w2_codes = []
         w2_scales = keep.tile([P, N], U8, name="w2_scales", align_bytes=64)
-        w2_src = w2_raw[:].rearrange("p j (c i) -> p c j i", i=4)
-        w2_dst = w2_bf[:].rearrange("p (c i) j -> p c j i", i=4)
 
-        def pack_w2(half):
+        def pack_w2(half, rounded, codes):
             cols = slice(half * HALF, (half + 1) * HALF)
-            nc.vector.quantize_mx(w2_codes[half][:].bitcast(FP8X4), w2_scales[:, cols], w2_bf[:, cols].rearrange("p n j -> p (n j)"))
-
-        def round_w2(quarter):
-            nc.scalar.copy(w2_dst[:, 32 * quarter : 32 * (quarter + 1)], w2_src[:, 32 * quarter : 32 * (quarter + 1)])
-
-        def differences(t, c0, plane, l, step):
-            width = plane.shape[1]
-            for s0 in range(0, width, step):
-                entries = slice((c0 + s0) // 16, (c0 + s0 + step) // 16)
-                nc.vector.tensor_tensor(plane[:, s0 : s0 + step], windows[t][:].indirect(lists[l][:, entries]), centres[t][:, c0 + s0 : c0 + s0 + step], ALU.subtract)
-
-        def far_terms(t, c0, far, soft):
-            width = far.shape[2]
-            for l in range(2):
-                differences(t, c0, far[:, l, :], l, HALF if (t, l) == (0, 0) else width)
-                if width > P:
-                    nc.scalar.activation(soft[:, l, :], far[:, l, :], ACT.Tanh, scale=2.0)
-            if width == P:
-                nc.scalar.activation(soft[:, 0:2, :], far, ACT.Tanh, scale=2.0)
-
-        def near_term(t, c0, near, soft):
-            differences(t, c0, near, 2, near.shape[1])
-            nc.scalar.activation(soft[:, 2, :], near, ACT.Sigmoid, scale=4.0)
-
-        def census(t, c0, width):
-            far = ring.tile([P, 2, width], F32, name="far", tag="far")
-            near = ring.tile([P, width], F32, name="near", tag="near")
-            soft = ring.tile([P, 3, width], F32, name="soft", tag="soft", bufs=3)
-            far_terms(t, c0, far[:], soft)
-            near_term(t, c0, near[:], soft)
-            return soft
-
-        def add_up(soft, t, first, count, terms=(0, 0, 1, 2), opening=True, close=True):
-            for i, l in enumerate(terms):
-                for b in range(count):
-                    nc.tensor.matmul(banks[first + b][:, t % 2, t // 2, :], soft[:, l, b * P : (b + 1) * P], ident[:], start=(opening and i == 0), stop=(close and i == len(terms) - 1), is_transpose=True)
+            nc.vector.quantize_mx(codes[:].bitcast(FP8X4), w2_scales[:, cols], rounded[:].rearrange("p n j -> p (n j)"))
+            w2_codes.append(codes)
 
         def weigh(b, gains, target):
             z_rows = keep.tile([P, 2, P, 2], BF16, name="z_rows%d" % b, align_bytes=64)
@@ -171,17 +170,13 @@ def tile_picked_census8_none_p_kernel(tc, x_words, x_scales, w1, gn, w2, offs, p
             nc.vector.quantize_mx(z_codes[:].bitcast(FP8X4), z_scales[:], z_bf[:].rearrange("p j t -> p (j t)"))
             return z_codes, z_scales
 
-        def project(c0, z_codes, z_scales, rows, banks, movers, results):
-            width = z_codes.shape[1]
-            for h in range(PACK // rows):
-                pool, tag = banks[h]
-                o_ps = pool.tile([P, rows, width], F32, name="o_ps", tag=tag)
-                for i in range(rows):
-                    cols = slice((rows * h + i) * P, (rows * h + i + 1) * P)
-                    nc.tensor.matmul_mx(o_ps[:, i, :], w2_codes[h][:, i * P : (i + 1) * P].bitcast(FP8X4), w2_scales[:, cols], z_codes[:].bitcast(FP8X4), z_scales[:], start=True, stop=True)
-                movers[h](results[h][:, :, c0 % HALF : c0 % HALF + width], o_ps[:])
-                if c0 % HALF:
-                    nc.sync.dma_start(out[rows * h * P : rows * (h + 1) * P, c0 - P : c0 + P].rearrange("(i p) j -> p i j", p=P), results[h][:])
+        def project(h, z_codes, z_scales, o_ps):
+            for i in range(2):
+                cols = slice((2 * h + i) * P, (2 * h + i + 1) * P)
+                nc.tensor.matmul_mx(o_ps[:, i, :], w2_codes[h][:, i * P : (i + 1) * P].bitcast(FP8X4), w2_scales[:, cols], z_codes[:].bitcast(FP8X4), z_scales[:], start=True, stop=True)
+
+        def store(h, cells, result):
+            nc.sync.dma_start(out[h * HALF : (h + 1) * HALF, cells].rearrange("(i p) j -> p i j", p=P), result[:])
 
         def interleave(turned, name):
             blocks = turned.shape[1]
@@ -189,39 +184,52 @@ def tile_picked_census8_none_p_kernel(tc, x_words, x_scales, w1, gn, w2, offs, p
             nc.scalar.copy(words_of(z_bf).rearrange("p (b j) u -> p b j u", b=blocks), turned.rearrange("p b u j -> p b j u"))
             return z_bf
 
-        later_tile(1)
-        later_tile(2)
-        later_tile(3)
-        spread_gain()
-        banks = [sums.tile([P, 2, 2, P], F32, name="bank", tag="bank") for b in range(4)]
-        for t in range(3):
-            add_up(census(t, 0, S), t, 0, 4)
-            if t < 2:
-                round_w2(2 - 2 * t)
-                round_w2(3 - 2 * t)
-        far = ring.tile([P, 2, S], F32, name="far", tag="far")
-        near = ring.tile([P, S], F32, name="near", tag="near")
-        soft = ring.tile([P, 3, S], F32, name="soft", tag="soft", bufs=3)
-        differences(3, 0, far[:, 0, :], 0, S)
-        nc.scalar.activation(soft[:, 0, :], far[:, 0, :], ACT.Tanh, scale=2.0)
-        for h in range(2):
-            cells = slice(h * HALF, (h + 1) * HALF)
-            differences(3, h * HALF, far[:, 1, cells], 1, HALF)
-            nc.scalar.activation(soft[:, 1, cells], far[:, 1, cells], ACT.Tanh, scale=2.0)
-            near_term(3, h * HALF, near[:, cells], soft[:, :, cells])
-            add_up(soft[:, :, cells], 3, 2 * h, 2)
+        open_window(1)
+        term(0, 0, low)
+        term(0, 0, high)
+        fetch(1)
+        term(0, 1, whole)
+        open_window(2)
+        term(0, 2, whole)
+        term(1, 0, whole)
+        pack_w2(0, w2_low_bf, keep.tile([P, HALF], U32, name="w2_low", tag="fetched1", align_bytes=64))
+        fetch(2)
+        term(1, 1, whole)
+        open_window(3)
+        term(1, 2, whole)
+        term(2, 0, whole)
+        fetch(3)
+        term(2, 1, whole)
+        term(2, 2, whole)
+        for cells in (low, high):
+            for l in range(3):
+                term(3, l, cells)
+
+        w2_high_bf = round_w2(1, "last_centre")
+
         def leave(b):
             turned = turn.tile([P, 1, 2, P], F32, name="turned", tag="turned")
             weigh(b, gain_rows, turned[:, 0])
             return interleave(turned[:], "z%d" % b)
 
         z_tiles = [leave(b) for b in range(4)]
-        pack_w2(0)
-        packed = [pack(z_tiles[b]) for b in range(3)]
-        w2_codes.append(keep.tile([P, HALF], U32, name="w2_high", tag="z_rows1", align_bytes=64))
-        pack_w2(1)
-        packed.append(pack(z_tiles[3]))
-        for b in range(4):
-            if b % 2 == 0:
-                results = [keep.tile([P, 2, HALF], F32, name="result%d_%d" % (b, h)) for h in range(2)]
-            project(b * P, *packed[b], 2, [(acc, "acc"), (sums, "bank")], [nc.scalar.copy, nc.vector.tensor_copy], results)
+        packed = [pack(z_tiles[0])]
+        pack_w2(1, w2_high_bf, keep.tile([P, HALF], U32, name="w2_high", align_bytes=64))
+        packed.extend(pack(z_tiles[b]) for b in range(1, 4))
+        movers = (nc.scalar.copy, nc.vector.tensor_copy)
+        early = [sums.tile([P, 2, HALF], F32, name="early", tag="bank") for h in range(2)]
+        for b in range(2):
+            for h in range(2):
+                project(h, *packed[b], early[h][:, :, b * P : (b + 1) * P])
+        for h in range(2):
+            result = keep.tile([P, 2, HALF], F32, name="early_result%d" % h)
+            movers[h](result[:], early[h][:])
+            store(h, low, result)
+        results = [keep.tile([P, 2, HALF], F32, name="late_result%d" % h) for h in range(2)]
+        for b, (pool, tag) in ((2, (acc, "acc")), (3, (sums, "bank"))):
+            for h in range(2):
+                late = pool.tile([P, 2, P], F32, name="late", tag=tag)
+                project(h, *packed[b], late[:])
+                movers[h](results[h][:, :, (b - 2) * P : (b - 1) * P], late[:])
+        for h in range(2):
+            store(h, high, results[h])

@@ -52,9 +52,6 @@ def tile_picked_census8_none_p_kernel(tc, x_words, x_scales, w1, gn, w2, offs, p
         nc.sync.dma_start(w1_raw[:, 2:4, :], w1_rows[:, 2:4, :])
         word_table = keep.tile([P, T], U32, name="word_table", align_bytes=64)
         nc.sync.dma_start(word_table[:].bitcast(I32), x_words[0].rearrange("p n t -> p (n t)").bitcast(I32))
-        w2_rows = w2.rearrange("(p j) c -> p j c", j=PACK)
-        w2_raw = [keep.tile([P, PACK, HALF], F32, name="w2_raw_low")]
-        nc.sync.dma_start(w2_raw[0][:], w2_rows[:, :, 0:HALF])
         lists = (load_list("list3", p3), load_list("list2", p2), load_list("list1", p1))
 
         x_bytes = keep.tile([P, S], U8, name="x_bytes", align_bytes=64)
@@ -75,8 +72,8 @@ def tile_picked_census8_none_p_kernel(tc, x_words, x_scales, w1, gn, w2, offs, p
         w1_src = w1_raw[:].rearrange("p j (m t) -> p m j t", t=PACK)
         nc.scalar.copy(w1_dst[:, 0:SCALAR_SHARE], w1_src[:, 0:SCALAR_SHARE])
         nc.vector.tensor_copy(w1_dst[:, SCALAR_SHARE:P], w1_src[:, SCALAR_SHARE:P])
-        w2_raw.append(keep.tile([P, PACK, HALF], F32, name="w2_raw_high", tag="raw"))
-        nc.sync.dma_start(w2_raw[1][:], w2_rows[:, :, HALF:N])
+        w2_raw = keep.tile([P, PACK, N], F32, name="w2_raw", tag="raw")
+        nc.sync.dma_start(w2_raw[:], w2.rearrange("(p j) c -> p j c", j=PACK))
 
         w1_codes = keep.tile([P, H], U32, name="w1_codes", align_bytes=64)
         w1_scales = keep.tile([P, H], U8, name="w1_scales", align_bytes=64)
@@ -95,12 +92,12 @@ def tile_picked_census8_none_p_kernel(tc, x_words, x_scales, w1, gn, w2, offs, p
         last_centre = keep.tile([P, S], F32, name="last_centre", tag="last_centre", align_bytes=64)
         centres = [windows[t + 1][:, S : 2 * S] for t in range(PACK - 1)] + [last_centre[:]]
 
-        def round_w2(half, tag):
-            rounded = keep.tile([P, HALF, PACK], BF16, name="w2_bf", tag=tag, align_bytes=64)
-            nc.gpsimd.tensor_scalar(rounded[:], w2_raw[half][:].rearrange("p j n -> p n j"), 1.0, 0.0, ALU.mult, ALU.add)
-            return rounded
+        w2_low_bf = keep.tile([P, HALF, PACK], BF16, name="w2_low_bf", align_bytes=64)
+        w2_src = w2_raw[:].rearrange("p j (c i) -> p c j i", i=4)
+        w2_dst = w2_low_bf[:].rearrange("p (c i) j -> p c j i", i=4)
 
-        w2_low_bf = round_w2(0, "w2_low_bf")
+        def round_w2(quarter):
+            nc.scalar.copy(w2_dst[:, 32 * quarter : 32 * (quarter + 1)], w2_src[:, 32 * quarter : 32 * (quarter + 1)])
 
         low, high, whole = slice(0, HALF), slice(HALF, S), slice(0, S)
         y_low = acc.tile([P, HALF], F32, name="y_low", tag="acc")
@@ -120,7 +117,7 @@ def tile_picked_census8_none_p_kernel(tc, x_words, x_scales, w1, gn, w2, offs, p
             nc.scalar.copy(windows[t][:, whole], later[t][:])
             nc.sync.dma_start(centres[t], windows[t][:, whole])
 
-        gaps = [keep.tile([P, 3, S], F32, name="gaps%d" % t) for t in range(PACK)]
+        gaps = {}
         softs = [keep.tile([P, 3, S], F32, name="soft%d" % t) for t in range(PACK)]
         fetched = {}
         banks = [sums.tile([P, 2, 2, P], F32, name="bank", tag="bank") for b in range(4)]
@@ -130,18 +127,20 @@ def tile_picked_census8_none_p_kernel(tc, x_words, x_scales, w1, gn, w2, offs, p
             nc.scalar.activation(fetched[t][:], windows[t][:].indirect(lists[0][:]), ACT.Copy)
 
         def difference(t, l, cells):
+            if (t, l) not in gaps:
+                gaps[t, l] = keep.tile([P, S], F32, name="gap", tag="gap%d_%d" % (min(t, 1) if l else t, l))
             if l == 0 and t in fetched:
-                nc.vector.tensor_tensor(gaps[t][:, l, cells], fetched[t][:, cells], windows[t][:, cells], ALU.subtract)
+                nc.vector.tensor_tensor(gaps[t, l][:, cells], fetched[t][:, cells], windows[t][:, cells], ALU.subtract)
             else:
                 entries = slice(cells.start // 16, cells.stop // 16)
-                nc.vector.tensor_tensor(gaps[t][:, l, cells], windows[t][:].indirect(lists[l][:, entries]), centres[t][:, cells], ALU.subtract)
+                nc.vector.tensor_tensor(gaps[t, l][:, cells], windows[t][:].indirect(lists[l][:, entries]), centres[t][:, cells], ALU.subtract)
 
         def term(t, l, cells):
             difference(t, l, cells)
             if l < 2:
-                nc.scalar.activation(softs[t][:, l, cells], gaps[t][:, l, cells], ACT.Tanh, scale=2.0)
+                nc.scalar.activation(softs[t][:, l, cells], gaps[t, l][:, cells], ACT.Tanh, scale=2.0)
             else:
-                nc.scalar.activation(softs[t][:, l, cells], gaps[t][:, l, cells], ACT.Sigmoid, scale=4.0)
+                nc.scalar.activation(softs[t][:, l, cells], gaps[t, l][:, cells], ACT.Sigmoid, scale=4.0)
             for b in range(cells.start // P, cells.stop // P):
                 for again in range(2 if l == 0 else 1):
                     nc.tensor.matmul(banks[b][:, t % 2, t // 2, :], softs[t][:, l, b * P : (b + 1) * P], ident[:], start=(l == 0 and again == 0), stop=(l == 2), is_transpose=True)
@@ -185,27 +184,30 @@ def tile_picked_census8_none_p_kernel(tc, x_words, x_scales, w1, gn, w2, offs, p
             return z_bf
 
         open_window(1)
+        open_window(2)
         term(0, 0, low)
         term(0, 0, high)
-        fetch(1)
+        open_window(3)
         term(0, 1, whole)
-        open_window(2)
+        round_w2(0)
         term(0, 2, whole)
+        round_w2(1)
         term(1, 0, whole)
-        pack_w2(0, w2_low_bf, keep.tile([P, HALF], U32, name="w2_low", tag="fetched1", align_bytes=64))
         fetch(2)
         term(1, 1, whole)
-        open_window(3)
         term(1, 2, whole)
         term(2, 0, whole)
+        pack_w2(0, w2_low_bf, keep.tile([P, HALF], U32, name="w2_low", tag="fetched2", align_bytes=64))
         fetch(3)
         term(2, 1, whole)
         term(2, 2, whole)
+        term(3, 0, whole)
         for cells in (low, high):
-            for l in range(3):
+            for l in (1, 2):
                 term(3, l, cells)
 
-        w2_high_bf = round_w2(1, "last_centre")
+        w2_high_bf = keep.tile([P, HALF, PACK], BF16, name="w2_high_bf", tag="last_centre", align_bytes=64)
+        nc.gpsimd.tensor_scalar(w2_high_bf[:], w2_raw[:, :, HALF:N].rearrange("p j n -> p n j"), 1.0, 0.0, ALU.mult, ALU.add)
 
         def leave(b):
             turned = turn.tile([P, 1, 2, P], F32, name="turned", tag="turned")

@@ -87,16 +87,15 @@ def tile_picked_census8_none_p_kernel(tc, x_words, x_scales, w1, gn, w2, offs, p
             cols = slice(t * P, (t + 1) * P)
             nc.tensor.matmul_mx(y_ps, w1_codes[:, cols].bitcast(FP8X4), w1_scales[:, cols], x_codes[:, cells].bitcast(FP8X4), x_bytes[:, cells], start=True, stop=True)
 
-        windows = [keep.tile([P, 2 * S], F32, name="window%d" % t) for t in range(PACK)]
+        windows = [keep.tile([P, 2 * S], F32, name="window", tag="window%d" % t, align_bytes=64) for t in range(PACK)]
         nc.gpsimd.memset(windows[0][:, S : 2 * S], 0.0)
-        last_centre = keep.tile([P, S], F32, name="last_centre", tag="last_centre", align_bytes=64)
-        centres = [windows[t + 1][:, S : 2 * S] for t in range(PACK - 1)] + [last_centre[:]]
+        lone_centre = keep.tile([P, S], F32, name="lone_centre")
+        centres = [windows[1][:, S : 2 * S], windows[3][:, S : 2 * S], lone_centre[:], windows[2][:, S : 2 * S]]
 
-        w2_low_bf = keep.tile([P, HALF, PACK], BF16, name="w2_low_bf", align_bytes=64)
         w2_src = w2_raw[:].rearrange("p j (c i) -> p c j i", i=4)
-        w2_dst = w2_low_bf[:].rearrange("p (c i) j -> p c j i", i=4)
 
-        def round_w2(quarter):
+        def round_w2(quarter, rounded):
+            w2_dst = rounded[:].rearrange("p (c i) j -> p c j i", i=4)
             nc.scalar.copy(w2_dst[:, 32 * quarter : 32 * (quarter + 1)], w2_src[:, 32 * quarter : 32 * (quarter + 1)])
 
         low, high, whole = slice(0, HALF), slice(HALF, S), slice(0, S)
@@ -127,10 +126,13 @@ def tile_picked_census8_none_p_kernel(tc, x_words, x_scales, w1, gn, w2, offs, p
             nc.scalar.activation(fetched[t][:], windows[t][:].indirect(lists[0][:]), ACT.Copy)
 
         def difference(t, l, cells):
+            if (t, l, cells) == (3, 1, low):
+                last_gaps = keep.tile([P, 2, S], F32, name="last_gaps", tag="gap2")
+                gaps[3, 1], gaps[3, 2] = last_gaps[:, 0, :], last_gaps[:, 1, :]
             if (t, l) not in gaps:
-                gaps[t, l] = keep.tile([P, S], F32, name="gap", tag="gap%d_%d" % (min(t, 1) if l else t, l))
+                gaps[t, l] = keep.tile([P, S], F32, name="gap", tag="gap%d" % l if l else "gap0_%d" % min(t, 2))[:]
             if l == 0 and t in fetched:
-                nc.vector.tensor_tensor(gaps[t, l][:, cells], fetched[t][:, cells], windows[t][:, cells], ALU.subtract)
+                nc.vector.tensor_tensor(gaps[t, l][:, cells], fetched[t][:, cells], centres[t][:, cells], ALU.subtract)
             else:
                 entries = slice(cells.start // 16, cells.stop // 16)
                 nc.vector.tensor_tensor(gaps[t, l][:, cells], windows[t][:].indirect(lists[l][:, entries]), centres[t][:, cells], ALU.subtract)
@@ -143,7 +145,7 @@ def tile_picked_census8_none_p_kernel(tc, x_words, x_scales, w1, gn, w2, offs, p
                 nc.scalar.activation(softs[t][:, l, cells], gaps[t, l][:, cells], ACT.Sigmoid, scale=4.0)
             for b in range(cells.start // P, cells.stop // P):
                 for again in range(2 if l == 0 else 1):
-                    nc.tensor.matmul(banks[b][:, t % 2, t // 2, :], softs[t][:, l, b * P : (b + 1) * P], ident[:], start=(l == 0 and again == 0), stop=(l == 2), is_transpose=True)
+                    nc.tensor.matmul(banks[b][:, t % 2, t // 2, :], softs[t][:, l, b * P : (b + 1) * P], ident[:], start=(l == (1 if t in fetched else 0) and again == 0), stop=(l == 2), is_transpose=True)
 
         w2_codes = []
         w2_scales = keep.tile([P, N], U8, name="w2_scales", align_bytes=64)
@@ -189,24 +191,25 @@ def tile_picked_census8_none_p_kernel(tc, x_words, x_scales, w1, gn, w2, offs, p
         term(0, 0, high)
         open_window(3)
         term(0, 1, whole)
-        round_w2(0)
+        fetch(1)
         term(0, 2, whole)
-        round_w2(1)
+        term(1, 1, whole)
         term(1, 0, whole)
         fetch(2)
-        term(1, 1, whole)
         term(1, 2, whole)
-        term(2, 0, whole)
-        pack_w2(0, w2_low_bf, keep.tile([P, HALF], U32, name="w2_low", tag="fetched2", align_bytes=64))
-        fetch(3)
         term(2, 1, whole)
+        term(2, 0, whole)
+        w2_low_bf = keep.tile([P, HALF, PACK], BF16, name="w2_low_bf", tag="fetched2", align_bytes=64)
+        round_w2(0, w2_low_bf)
         term(2, 2, whole)
+        round_w2(1, w2_low_bf)
         term(3, 0, whole)
+        pack_w2(0, w2_low_bf, keep.tile([P, HALF], U32, name="w2_low", align_bytes=64))
         for cells in (low, high):
             for l in (1, 2):
                 term(3, l, cells)
 
-        w2_high_bf = keep.tile([P, HALF, PACK], BF16, name="w2_high_bf", tag="last_centre", align_bytes=64)
+        w2_high_bf = keep.tile([P, HALF, PACK], BF16, name="w2_high_bf", tag="window3", align_bytes=64)
         nc.gpsimd.tensor_scalar(w2_high_bf[:], w2_raw[:, :, HALF:N].rearrange("p j n -> p n j"), 1.0, 0.0, ALU.mult, ALU.add)
 
         def leave(b):
@@ -216,7 +219,7 @@ def tile_picked_census8_none_p_kernel(tc, x_words, x_scales, w1, gn, w2, offs, p
 
         z_tiles = [leave(b) for b in range(4)]
         packed = [pack(z_tiles[0])]
-        pack_w2(1, w2_high_bf, keep.tile([P, HALF], U32, name="w2_high", align_bytes=64))
+        pack_w2(1, w2_high_bf, keep.tile([P, HALF], U32, name="w2_high", tag="z_rows2", align_bytes=64))
         packed.extend(pack(z_tiles[b]) for b in range(1, 4))
         movers = (nc.scalar.copy, nc.vector.tensor_copy)
         early = [sums.tile([P, 2, HALF], F32, name="early", tag="bank") for h in range(2)]

@@ -96,7 +96,7 @@ def tile_picked_census8_none_p_kernel(tc, x_words, x_scales, w1, gn, w2, offs, p
 
         def round_w2(quarter, rounded):
             w2_dst = rounded[:].rearrange("p (c i) j -> p c j i", i=4)
-            nc.scalar.copy(w2_dst[:, 32 * quarter : 32 * (quarter + 1)], w2_src[:, 32 * quarter : 32 * (quarter + 1)])
+            nc.scalar.copy(w2_dst[:, 32 * (quarter % 2) : 32 * (quarter % 2 + 1)], w2_src[:, 32 * quarter : 32 * (quarter + 1)])
 
         low, high, whole = slice(0, HALF), slice(HALF, S), slice(0, S)
         y_low = acc.tile([P, HALF], F32, name="y_low", tag="acc")
@@ -210,7 +210,8 @@ def tile_picked_census8_none_p_kernel(tc, x_words, x_scales, w1, gn, w2, offs, p
                 term(3, l, cells)
 
         w2_high_bf = keep.tile([P, HALF, PACK], BF16, name="w2_high_bf", tag="window3", align_bytes=64)
-        nc.gpsimd.tensor_scalar(w2_high_bf[:], w2_raw[:, :, HALF:N].rearrange("p j n -> p n j"), 1.0, 0.0, ALU.mult, ALU.add)
+        round_w2(2, w2_high_bf)
+        round_w2(3, w2_high_bf)
 
         def leave(b):
             turned = turn.tile([P, 1, 2, P], F32, name="turned", tag="turned")

@@ -42,8 +42,6 @@ def tile_picked_census8_none_p_kernel(tc, x_words, x_scales, w1, gn, w2, offs, p
         nc.gpsimd.memset(scale_table[:].bitcast(I32), 0)
 
         picks = load_list("picks", offs)
-        gain = keep.tile([P, PACK], F32, name="gain")
-        nc.sync.dma_start(gain[:], gn.rearrange("(p t) o -> p (t o)", t=PACK))
         w1_rows = w1.rearrange("(p j) c -> p j c", j=PACK)
         w1_raw = keep.tile([P, PACK, H], F32, name="w1_raw", tag="raw")
         nc.sync.dma_start(w1_raw[:, 0:2, :], w1_rows[:, 0:2, :])
@@ -61,12 +59,6 @@ def tile_picked_census8_none_p_kernel(tc, x_words, x_scales, w1, gn, w2, offs, p
         ident = keep.tile([P, P], F32, name="ident")
         make_identity(nc, ident[:])
 
-        gain_rows = keep.tile([P, 2, P, 2], F32, name="gain_rows")
-        gain_ps = turn.tile([P, PACK, P], F32, name="gain_ps", tag="turned")
-        for t in range(PACK):
-            nc.tensor.transpose(gain_ps[:, t, :], gain[:, t : t + 1].to_broadcast([P, P]), ident[:])
-        nc.scalar.activation(gain_rows[:], gain_ps[:].rearrange("j (u e) p -> j u p e", e=2), ACT.Copy, scale=0.5)
-
         w1_bf = keep.tile([P, PACK, P, PACK], BF16, name="w1_bf", align_bytes=64)
         w1_dst = w1_bf[:].rearrange("p t m j -> p m j t")
         w1_src = w1_raw[:].rearrange("p j (m t) -> p m j t", t=PACK)
@@ -74,14 +66,18 @@ def tile_picked_census8_none_p_kernel(tc, x_words, x_scales, w1, gn, w2, offs, p
         nc.vector.tensor_copy(w1_dst[:, SCALAR_SHARE:P], w1_src[:, SCALAR_SHARE:P])
         w2_raw = keep.tile([P, PACK, N], F32, name="w2_raw", tag="raw")
         nc.sync.dma_start(w2_raw[:], w2.rearrange("(p j) c -> p j c", j=PACK))
+        gain = keep.tile([P, PACK], F32, name="gain", tag="w1_bf", align_bytes=64)
+        nc.sync.dma_start(gain[:], gn.rearrange("(p t) o -> p (t o)", t=PACK))
 
         w1_codes = keep.tile([P, H], U32, name="w1_codes", align_bytes=64)
         w1_scales = keep.tile([P, H], U8, name="w1_scales", align_bytes=64)
         nc.vector.quantize_mx(w1_codes[:].bitcast(FP8X4), w1_scales[:], w1_bf[:].rearrange("p t m j -> p (t m j)"))
 
         x_codes = keep.tile([P, S], U32, name="x_codes", align_bytes=64)
-        for h in range(2):
-            nc.vector.tensor_copy(x_codes[:, h * HALF : (h + 1) * HALF], word_table[:].indirect(picks[:, h * 16 : (h + 1) * 16]))
+        low, high, whole = slice(0, HALF), slice(HALF, S), slice(0, S)
+        third, fourth = slice(HALF, HALF + P), slice(HALF + P, S)
+        for cells in (low, third, fourth):
+            nc.vector.tensor_copy(x_codes[:, cells], word_table[:].indirect(picks[:, cells.start // 16 : cells.stop // 16]))
 
         def first_product(t, cells, y_ps):
             cols = slice(t * P, (t + 1) * P)
@@ -89,8 +85,8 @@ def tile_picked_census8_none_p_kernel(tc, x_words, x_scales, w1, gn, w2, offs, p
 
         windows = [keep.tile([P, 2 * S], F32, name="window", tag="window%d" % t, align_bytes=64) for t in range(PACK)]
         nc.gpsimd.memset(windows[0][:, S : 2 * S], 0.0)
-        lone_centre = keep.tile([P, S], F32, name="lone_centre")
-        centres = [windows[1][:, S : 2 * S], windows[3][:, S : 2 * S], lone_centre[:], windows[2][:, S : 2 * S]]
+        last_centre = keep.tile([P, S], F32, name="last_centre", tag="last_centre", align_bytes=64)
+        centres = [windows[t + 1][:, S : 2 * S] for t in range(PACK - 1)] + [last_centre[:]]
 
         w2_src = w2_raw[:].rearrange("p j (c i) -> p c j i", i=4)
 
@@ -98,19 +94,22 @@ def tile_picked_census8_none_p_kernel(tc, x_words, x_scales, w1, gn, w2, offs, p
             w2_dst = rounded[:].rearrange("p (c i) j -> p c j i", i=4)
             nc.scalar.copy(w2_dst[:, 32 * (quarter % 2) : 32 * (quarter % 2 + 1)], w2_src[:, 32 * quarter : 32 * (quarter + 1)])
 
-        low, high, whole = slice(0, HALF), slice(HALF, S), slice(0, S)
         y_low = acc.tile([P, HALF], F32, name="y_low", tag="acc")
-        y_high = acc.tile([P, HALF], F32, name="y_high", tag="acc")
+        y_third = acc.tile([P, P], F32, name="y_third", tag="acc")
+        y_fourth = sums.tile([P, P], F32, name="y_fourth", tag="bank")
         first_product(0, low, y_low[:])
-        first_product(0, high, y_high[:])
+        first_product(0, third, y_third[:])
+        first_product(0, fourth, y_fourth[:])
         later = {}
         for t, (pool, tag) in ((1, (turn, "turned")), (2, (turn, "turned")), (3, (acc, "acc"))):
             later[t] = pool.tile([P, S], F32, name="y_ps", tag=tag)
             first_product(t, whole, later[t][:])
         nc.scalar.copy(windows[0][:, low], y_low[:])
-        nc.vector.tensor_copy(windows[0][:, high], y_high[:])
         nc.scalar.copy(centres[0][:, low], y_low[:])
-        nc.scalar.copy(centres[0][:, high], y_high[:])
+        nc.vector.tensor_copy(windows[0][:, third], y_third[:])
+        nc.vector.tensor_copy(windows[0][:, fourth], y_fourth[:])
+        nc.scalar.copy(centres[0][:, third], y_third[:])
+        nc.scalar.copy(centres[0][:, fourth], y_fourth[:])
 
         def open_window(t):
             nc.scalar.copy(windows[t][:, whole], later[t][:])
@@ -145,7 +144,7 @@ def tile_picked_census8_none_p_kernel(tc, x_words, x_scales, w1, gn, w2, offs, p
                 nc.scalar.activation(softs[t][:, l, cells], gaps[t, l][:, cells], ACT.Sigmoid, scale=4.0)
             for b in range(cells.start // P, cells.stop // P):
                 for again in range(2 if l == 0 else 1):
-                    nc.tensor.matmul(banks[b][:, t % 2, t // 2, :], softs[t][:, l, b * P : (b + 1) * P], ident[:], start=(l == (1 if t in fetched else 0) and again == 0), stop=(l == 2), is_transpose=True)
+                    nc.tensor.matmul(banks[b][:, t % 2, t // 2, :], softs[t][:, l, b * P : (b + 1) * P], ident[:], start=(l == 0 and again == 0), stop=(l == 2), is_transpose=True)
 
         w2_codes = []
         w2_scales = keep.tile([P, N], U8, name="w2_scales", align_bytes=64)
@@ -174,7 +173,7 @@ def tile_picked_census8_none_p_kernel(tc, x_words, x_scales, w1, gn, w2, offs, p
         def project(h, z_codes, z_scales, o_ps):
             for i in range(2):
                 cols = slice((2 * h + i) * P, (2 * h + i + 1) * P)
-                nc.tensor.matmul_mx(o_ps[:, i, :], w2_codes[h][:, i * P : (i + 1) * P].bitcast(FP8X4), w2_scales[:, cols], z_codes[:].bitcast(FP8X4), z_scales[:], start=True, stop=True)
+                nc.tensor.matmul_mx(o_ps[i][:], w2_codes[h][:, i * P : (i + 1) * P].bitcast(FP8X4), w2_scales[:, cols], z_codes[:].bitcast(FP8X4), z_scales[:], start=True, stop=True)
 
         def store(h, cells, result):
             nc.sync.dma_start(out[h * HALF : (h + 1) * HALF, cells].rearrange("(i p) j -> p i j", p=P), result[:])
@@ -191,24 +190,27 @@ def tile_picked_census8_none_p_kernel(tc, x_words, x_scales, w1, gn, w2, offs, p
         term(0, 0, high)
         open_window(3)
         term(0, 1, whole)
-        fetch(1)
         term(0, 2, whole)
-        term(1, 1, whole)
-        term(1, 0, whole)
+        gain_rows = keep.tile([P, 2, P, 2], F32, name="gain_rows")
+        gain_ps = turn.tile([P, PACK, P], F32, name="gain_ps", tag="turned")
+        for t in range(PACK):
+            nc.tensor.transpose(gain_ps[:, t, :], gain[:, t : t + 1].to_broadcast([P, P]), ident[:])
+        nc.scalar.activation(gain_rows[:], gain_ps[:].rearrange("j (u e) p -> j u p e", e=2), ACT.Copy, scale=0.5)
         fetch(2)
-        term(1, 2, whole)
-        term(2, 1, whole)
+        for l in range(3):
+            term(1, l, whole)
         term(2, 0, whole)
         w2_low_bf = keep.tile([P, HALF, PACK], BF16, name="w2_low_bf", tag="fetched2", align_bytes=64)
         round_w2(0, w2_low_bf)
-        term(2, 2, whole)
+        term(2, 1, whole)
         round_w2(1, w2_low_bf)
+        term(2, 2, whole)
         term(3, 0, whole)
-        pack_w2(0, w2_low_bf, keep.tile([P, HALF], U32, name="w2_low", align_bytes=64))
         for cells in (low, high):
             for l in (1, 2):
                 term(3, l, cells)
 
+        pack_w2(0, w2_low_bf, keep.tile([P, HALF], U32, name="w2_low", tag="last_centre", align_bytes=64))
         w2_high_bf = keep.tile([P, HALF, PACK], BF16, name="w2_high_bf", tag="window3", align_bytes=64)
         round_w2(2, w2_high_bf)
         round_w2(3, w2_high_bf)
@@ -219,23 +221,26 @@ def tile_picked_census8_none_p_kernel(tc, x_words, x_scales, w1, gn, w2, offs, p
             return interleave(turned[:], "z%d" % b)
 
         z_tiles = [leave(b) for b in range(4)]
-        packed = [pack(z_tiles[0])]
+        packed = [pack(z_tiles[b]) for b in range(2)]
         pack_w2(1, w2_high_bf, keep.tile([P, HALF], U32, name="w2_high", tag="z_rows2", align_bytes=64))
-        packed.extend(pack(z_tiles[b]) for b in range(1, 4))
+        packed.extend(pack(z_tiles[b]) for b in range(2, 4))
         movers = (nc.scalar.copy, nc.vector.tensor_copy)
         early = [sums.tile([P, 2, HALF], F32, name="early", tag="bank") for h in range(2)]
-        for b in range(2):
-            for h in range(2):
-                project(h, *packed[b], early[h][:, :, b * P : (b + 1) * P])
         for h in range(2):
+            for b in range(2):
+                project(h, *packed[b], [early[h][:, i, b * P : (b + 1) * P] for i in range(2)])
             result = keep.tile([P, 2, HALF], F32, name="early_result%d" % h)
             movers[h](result[:], early[h][:])
             store(h, low, result)
         results = [keep.tile([P, 2, HALF], F32, name="late_result%d" % h) for h in range(2)]
-        for b, (pool, tag) in ((2, (acc, "acc")), (3, (sums, "bank"))):
-            for h in range(2):
-                late = pool.tile([P, 2, P], F32, name="late", tag=tag)
-                project(h, *packed[b], late[:])
-                movers[h](results[h][:, :, (b - 2) * P : (b - 1) * P], late[:])
+        for h in range(2):
+            late = acc.tile([P, 2, P], F32, name="late", tag="acc")
+            project(h, *packed[2], [late[:, i, :] for i in range(2)])
+            movers[h](results[h][:, :, 0:P], late[:])
+        for h, (pool, tag) in enumerate(((sums, "bank"), (turn, "turned"))):
+            last = [pool.tile([P, P], F32, name="last", tag=tag) for i in range(2)]
+            project(h, *packed[3], last)
+            for i in range(2):
+                movers[i](results[h][:, i, P:HALF], last[i][:])
         for h in range(2):
             store(h, high, results[h])

@@ -41,10 +41,10 @@ def tile_picked_census8_none_p_kernel(tc, x_words, x_scales, w1, gn, w2, offs, p
         scale_table = keep.tile([P, T], U8, name="scale_table", align_bytes=64)
         nc.gpsimd.memset(scale_table[:].bitcast(I32), 0)
 
-        picks = load_list("picks", offs)
         w1_rows = w1.rearrange("(p j) c -> p j c", j=PACK)
         w1_raw = keep.tile([P, PACK, H], F32, name="w1_raw", tag="raw")
         nc.sync.dma_start(w1_raw[:, 0:2, :], w1_rows[:, 0:2, :])
+        picks = load_list("picks", offs)
         for r in range(4):
             nc.sync.dma_start(scale_table[r:P:32, :].bitcast(I32), x_scales[0, r:16:4, :].bitcast(I32))
         nc.sync.dma_start(w1_raw[:, 2:4, :], w1_rows[:, 2:4, :])
@@ -84,9 +84,11 @@ def tile_picked_census8_none_p_kernel(tc, x_words, x_scales, w1, gn, w2, offs, p
             nc.tensor.matmul_mx(y_ps, w1_codes[:, cols].bitcast(FP8X4), w1_scales[:, cols], x_codes[:, cells].bitcast(FP8X4), x_bytes[:, cells], start=True, stop=True)
 
         windows = [keep.tile([P, 2 * S], F32, name="window", tag="window%d" % t, align_bytes=64) for t in range(PACK)]
-        nc.gpsimd.memset(windows[0][:, S : 2 * S], 0.0)
+        for t in (0, 2):
+            nc.gpsimd.memset(windows[t][:, S : 2 * S], 0.0)
+        second_centre = keep.tile([P, S], F32, name="second_centre")
         last_centre = keep.tile([P, S], F32, name="last_centre", tag="last_centre", align_bytes=64)
-        centres = [windows[t + 1][:, S : 2 * S] for t in range(PACK - 1)] + [last_centre[:]]
+        centres = [windows[1][:, S : 2 * S], second_centre[:], windows[3][:, S : 2 * S], last_centre[:]]
 
         w2_src = w2_raw[:].rearrange("p j (c i) -> p c j i", i=4)
 
@@ -129,7 +131,7 @@ def tile_picked_census8_none_p_kernel(tc, x_words, x_scales, w1, gn, w2, offs, p
                 last_gaps = keep.tile([P, 2, S], F32, name="last_gaps", tag="gap2")
                 gaps[3, 1], gaps[3, 2] = last_gaps[:, 0, :], last_gaps[:, 1, :]
             if (t, l) not in gaps:
-                gaps[t, l] = keep.tile([P, S], F32, name="gap", tag="gap%d" % l if l else "gap0_%d" % min(t, 2))[:]
+                gaps[t, l] = keep.tile([P, S], F32, name="gap", tag="gap%d" % l if l and t else "gap%d_%d" % (l, min(t, 2)))[:]
             if l == 0 and t in fetched:
                 nc.vector.tensor_tensor(gaps[t, l][:, cells], fetched[t][:, cells], centres[t][:, cells], ALU.subtract)
             else:
@@ -189,16 +191,17 @@ def tile_picked_census8_none_p_kernel(tc, x_words, x_scales, w1, gn, w2, offs, p
         term(0, 0, low)
         term(0, 0, high)
         open_window(3)
+        fetch(2)
         term(0, 1, whole)
         term(0, 2, whole)
-        gain_rows = keep.tile([P, 2, P, 2], F32, name="gain_rows")
+        term(1, 0, whole)
+        gain_rows = keep.tile([P, 2, P, 2], F32, name="gain_rows", tag="gap0_1")
         gain_ps = turn.tile([P, PACK, P], F32, name="gain_ps", tag="turned")
         for t in range(PACK):
             nc.tensor.transpose(gain_ps[:, t, :], gain[:, t : t + 1].to_broadcast([P, P]), ident[:])
         nc.scalar.activation(gain_rows[:], gain_ps[:].rearrange("j (u e) p -> j u p e", e=2), ACT.Copy, scale=0.5)
-        fetch(2)
-        for l in range(3):
-            term(1, l, whole)
+        term(1, 1, whole)
+        term(1, 2, whole)
         term(2, 0, whole)
         w2_low_bf = keep.tile([P, HALF, PACK], BF16, name="w2_low_bf", tag="fetched2", align_bytes=64)
         round_w2(0, w2_low_bf)

@@ -138,12 +138,18 @@ def tile_picked_census8_none_p_kernel(tc, x_words, x_scales, w1, gn, w2, offs, p
                 entries = slice(cells.start // 16, cells.stop // 16)
                 nc.vector.tensor_tensor(gaps[t, l][:, cells], windows[t][:].indirect(lists[l][:, entries]), centres[t][:, cells], ALU.subtract)
 
-        def term(t, l, cells):
+        def soften(t, l, cells):
             difference(t, l, cells)
             if l < 2:
                 nc.scalar.activation(softs[t][:, l, cells], gaps[t, l][:, cells], ACT.Tanh, scale=2.0)
             else:
                 nc.scalar.activation(softs[t][:, l, cells], gaps[t, l][:, cells], ACT.Sigmoid, scale=4.0)
+
+        def term(t, l, cells):
+            soften(t, l, cells)
+            add_up(t, l, cells)
+
+        def add_up(t, l, cells):
             for b in range(cells.start // P, cells.stop // P):
                 for again in range(2 if l == 0 else 1):
                     nc.tensor.matmul(banks[b][:, t % 2, t // 2, :], softs[t][:, l, b * P : (b + 1) * P], ident[:], start=(l == 0 and again == 0), stop=(l == 2), is_transpose=True)
@@ -151,9 +157,10 @@ def tile_picked_census8_none_p_kernel(tc, x_words, x_scales, w1, gn, w2, offs, p
         w2_codes = []
         w2_scales = keep.tile([P, N], U8, name="w2_scales", align_bytes=64)
 
-        def pack_w2(half, rounded, codes):
-            cols = slice(half * HALF, (half + 1) * HALF)
-            nc.vector.quantize_mx(codes[:].bitcast(FP8X4), w2_scales[:, cols], rounded[:].rearrange("p n j -> p (n j)"))
+        def pack_w2(quarter, rounded):
+            codes = keep.tile([P, P], U32, name="w2_codes", tag="z_rows%d" % quarter if quarter else "last_centre", align_bytes=64)
+            part = rounded[:, quarter % 2 * P : (quarter % 2 + 1) * P]
+            nc.vector.quantize_mx(codes[:].bitcast(FP8X4), w2_scales[:, quarter * P : (quarter + 1) * P], part.rearrange("p n j -> p (n j)"))
             w2_codes.append(codes)
 
         def weigh(b, gains, target):
@@ -175,7 +182,7 @@ def tile_picked_census8_none_p_kernel(tc, x_words, x_scales, w1, gn, w2, offs, p
         def project(h, z_codes, z_scales, o_ps):
             for i in range(2):
                 cols = slice((2 * h + i) * P, (2 * h + i + 1) * P)
-                nc.tensor.matmul_mx(o_ps[i][:], w2_codes[h][:, i * P : (i + 1) * P].bitcast(FP8X4), w2_scales[:, cols], z_codes[:].bitcast(FP8X4), z_scales[:], start=True, stop=True)
+                nc.tensor.matmul_mx(o_ps[i][:], w2_codes[2 * h + i][:].bitcast(FP8X4), w2_scales[:, cols], z_codes[:].bitcast(FP8X4), z_scales[:], start=True, stop=True)
 
         def store(h, cells, result):
             nc.sync.dma_start(out[h * HALF : (h + 1) * HALF, cells].rearrange("(i p) j -> p i j", p=P), result[:])
@@ -208,12 +215,13 @@ def tile_picked_census8_none_p_kernel(tc, x_words, x_scales, w1, gn, w2, offs, p
         term(2, 1, whole)
         round_w2(1, w2_low_bf)
         term(2, 2, whole)
-        term(3, 0, whole)
+        soften(3, 0, whole)
         for cells in (low, high):
+            add_up(3, 0, cells)
             for l in (1, 2):
                 term(3, l, cells)
 
-        pack_w2(0, w2_low_bf, keep.tile([P, HALF], U32, name="w2_low", tag="last_centre", align_bytes=64))
+        pack_w2(0, w2_low_bf)
         w2_high_bf = keep.tile([P, HALF, PACK], BF16, name="w2_high_bf", tag="window3", align_bytes=64)
         round_w2(2, w2_high_bf)
         round_w2(3, w2_high_bf)
@@ -224,8 +232,11 @@ def tile_picked_census8_none_p_kernel(tc, x_words, x_scales, w1, gn, w2, offs, p
             return interleave(turned[:], "z%d" % b)
 
         z_tiles = [leave(b) for b in range(4)]
-        packed = [pack(z_tiles[b]) for b in range(2)]
-        pack_w2(1, w2_high_bf, keep.tile([P, HALF], U32, name="w2_high", tag="z_rows2", align_bytes=64))
+        packed = [pack(z_tiles[0])]
+        pack_w2(1, w2_low_bf)
+        packed.append(pack(z_tiles[1]))
+        pack_w2(2, w2_high_bf)
+        pack_w2(3, w2_high_bf)
         packed.extend(pack(z_tiles[b]) for b in range(2, 4))
         movers = (nc.scalar.copy, nc.vector.tensor_copy)
         early = [sums.tile([P, 2, HALF], F32, name="early", tag="bank") for h in range(2)]

@@ -86,9 +86,9 @@ def tile_picked_census8_none_p_kernel(tc, x_words, x_scales, w1, gn, w2, offs, p
         windows = [keep.tile([P, 2 * S], F32, name="window", tag="window%d" % t, align_bytes=64) for t in range(PACK)]
         for t in (0, 2):
             nc.gpsimd.memset(windows[t][:, S : 2 * S], 0.0)
-        second_centre = keep.tile([P, S], F32, name="second_centre")
+        third_centre = keep.tile([P, S], F32, name="third_centre")
         last_centre = keep.tile([P, S], F32, name="last_centre", tag="last_centre", align_bytes=64)
-        centres = [windows[1][:, S : 2 * S], second_centre[:], windows[3][:, S : 2 * S], last_centre[:]]
+        centres = [windows[1][:, S : 2 * S], windows[3][:, S : 2 * S], third_centre[:], last_centre[:]]
 
         w2_src = w2_raw[:].rearrange("p j (c i) -> p c j i", i=4)
 
@@ -122,18 +122,15 @@ def tile_picked_census8_none_p_kernel(tc, x_words, x_scales, w1, gn, w2, offs, p
         fetched = {}
         banks = [sums.tile([P, 2, 2, P], F32, name="bank", tag="bank") for b in range(4)]
 
-        def fetch(t):
-            fetched[t] = keep.tile([P, S], F32, name="fetched", tag="fetched%d" % t, align_bytes=64)
-            nc.scalar.activation(fetched[t][:], windows[t][:].indirect(lists[0][:]), ACT.Copy)
+        def fetch(t, cells, tag):
+            fetched[t, cells.start] = keep.tile([P, cells.stop - cells.start], F32, name="fetched", tag=tag)
+            nc.scalar.activation(fetched[t, cells.start][:], windows[t][:].indirect(lists[0][:, cells.start // 16 : cells.stop // 16]), ACT.Copy)
 
         def difference(t, l, cells):
-            if (t, l, cells) == (3, 1, low):
-                last_gaps = keep.tile([P, 2, S], F32, name="last_gaps", tag="gap2")
-                gaps[3, 1], gaps[3, 2] = last_gaps[:, 0, :], last_gaps[:, 1, :]
             if (t, l) not in gaps:
-                gaps[t, l] = keep.tile([P, S], F32, name="gap", tag="gap%d" % l if l and t else "gap%d_%d" % (l, min(t, 2)))[:]
-            if l == 0 and t in fetched:
-                nc.vector.tensor_tensor(gaps[t, l][:, cells], fetched[t][:, cells], centres[t][:, cells], ALU.subtract)
+                gaps[t, l] = keep.tile([P, S], F32, name="gap", tag="gap%d_%d" % (t, l))
+            if l == 0 and (t, cells.start) in fetched:
+                nc.vector.tensor_tensor(gaps[t, l][:, cells], fetched[t, cells.start][:], centres[t][:, cells], ALU.subtract)
             else:
                 entries = slice(cells.start // 16, cells.stop // 16)
                 nc.vector.tensor_tensor(gaps[t, l][:, cells], windows[t][:].indirect(lists[l][:, entries]), centres[t][:, cells], ALU.subtract)
@@ -157,10 +154,9 @@ def tile_picked_census8_none_p_kernel(tc, x_words, x_scales, w1, gn, w2, offs, p
         w2_codes = []
         w2_scales = keep.tile([P, N], U8, name="w2_scales", align_bytes=64)
 
-        def pack_w2(quarter, rounded):
-            codes = keep.tile([P, P], U32, name="w2_codes", tag="z_rows%d" % quarter if quarter else "last_centre", align_bytes=64)
-            part = rounded[:, quarter % 2 * P : (quarter % 2 + 1) * P]
-            nc.vector.quantize_mx(codes[:].bitcast(FP8X4), w2_scales[:, quarter * P : (quarter + 1) * P], part.rearrange("p n j -> p (n j)"))
+        def pack_w2(half, rounded):
+            codes = keep.tile([P, HALF], U32, name="w2_codes", tag="z_rows%d" % (1 + half), align_bytes=64)
+            nc.vector.quantize_mx(codes[:].bitcast(FP8X4), w2_scales[:, half * HALF : (half + 1) * HALF], rounded[:].rearrange("p n j -> p (n j)"))
             w2_codes.append(codes)
 
         def weigh(b, gains, target):
@@ -182,7 +178,7 @@ def tile_picked_census8_none_p_kernel(tc, x_words, x_scales, w1, gn, w2, offs, p
         def project(h, z_codes, z_scales, o_ps):
             for i in range(2):
                 cols = slice((2 * h + i) * P, (2 * h + i + 1) * P)
-                nc.tensor.matmul_mx(o_ps[i][:], w2_codes[2 * h + i][:].bitcast(FP8X4), w2_scales[:, cols], z_codes[:].bitcast(FP8X4), z_scales[:], start=True, stop=True)
+                nc.tensor.matmul_mx(o_ps[i][:], w2_codes[h][:, i * P : (i + 1) * P].bitcast(FP8X4), w2_scales[:, cols], z_codes[:].bitcast(FP8X4), z_scales[:], start=True, stop=True)
 
         def store(h, cells, result):
             nc.sync.dma_start(out[h * HALF : (h + 1) * HALF, cells].rearrange("(i p) j -> p i j", p=P), result[:])
@@ -198,33 +194,34 @@ def tile_picked_census8_none_p_kernel(tc, x_words, x_scales, w1, gn, w2, offs, p
         term(0, 0, low)
         term(0, 0, high)
         open_window(3)
-        fetch(2)
+        fetch(2, whole, "fetched2")
         term(0, 1, whole)
         term(0, 2, whole)
+        fetch(3, low, "fetched3")
         term(1, 0, whole)
-        gain_rows = keep.tile([P, 2, P, 2], F32, name="gain_rows", tag="gap0_1")
+        term(1, 1, whole)
+        fetch(3, high, "gap1_0")
+        term(1, 2, whole)
+        term(2, 0, whole)
+        term(2, 1, whole)
+        gain_rows = keep.tile([P, 2, P, 2], F32, name="gain_rows", tag="fetched2")
         gain_ps = turn.tile([P, PACK, P], F32, name="gain_ps", tag="turned")
         for t in range(PACK):
             nc.tensor.transpose(gain_ps[:, t, :], gain[:, t : t + 1].to_broadcast([P, P]), ident[:])
         nc.scalar.activation(gain_rows[:], gain_ps[:].rearrange("j (u e) p -> j u p e", e=2), ACT.Copy, scale=0.5)
-        term(1, 1, whole)
-        term(1, 2, whole)
-        term(2, 0, whole)
-        w2_low_bf = keep.tile([P, HALF, PACK], BF16, name="w2_low_bf", tag="fetched2", align_bytes=64)
-        round_w2(0, w2_low_bf)
-        term(2, 1, whole)
-        round_w2(1, w2_low_bf)
         term(2, 2, whole)
-        soften(3, 0, whole)
+        for cells in (low, high):
+            soften(3, 0, cells)
         for cells in (low, high):
             add_up(3, 0, cells)
             for l in (1, 2):
                 term(3, l, cells)
 
-        pack_w2(0, w2_low_bf)
-        w2_high_bf = keep.tile([P, HALF, PACK], BF16, name="w2_high_bf", tag="window3", align_bytes=64)
-        round_w2(2, w2_high_bf)
-        round_w2(3, w2_high_bf)
+        w2_low_bf = keep.tile([P, HALF, PACK], BF16, name="w2_low_bf", tag="window3", align_bytes=64)
+        round_w2(0, w2_low_bf)
+        round_w2(1, w2_low_bf)
+        w2_high_bf = keep.tile([P, HALF, PACK], BF16, name="w2_high_bf", tag="last_centre", align_bytes=64)
+        nc.gpsimd.tensor_scalar(w2_high_bf[:], w2_raw[:, :, HALF:N].rearrange("p j n -> p n j"), 1.0, 0.0, ALU.mult, ALU.add)
 
         def leave(b):
             turned = turn.tile([P, 1, 2, P], F32, name="turned", tag="turned")
@@ -233,10 +230,9 @@ def tile_picked_census8_none_p_kernel(tc, x_words, x_scales, w1, gn, w2, offs, p
 
         z_tiles = [leave(b) for b in range(4)]
         packed = [pack(z_tiles[0])]
-        pack_w2(1, w2_low_bf)
+        pack_w2(0, w2_low_bf)
         packed.append(pack(z_tiles[1]))
-        pack_w2(2, w2_high_bf)
-        pack_w2(3, w2_high_bf)
+        pack_w2(1, w2_high_bf)
         packed.extend(pack(z_tiles[b]) for b in range(2, 4))
         movers = (nc.scalar.copy, nc.vector.tensor_copy)
         early = [sums.tile([P, 2, HALF], F32, name="early", tag="bank") for h in range(2)]

@@ -20,6 +20,9 @@ P = 128
 PACK = 4
 HALF = S // 2
 SCALAR_SHARE = 44
+FETCHED_TILE = 2
+LAST_TILE = PACK - 1
+DOUBLED, SINGLE, NEAR = 0, 1, 2
 
 
 def tile_picked_census8_none_p_kernel(tc, x_words, x_scales, w1, gn, w2, offs, p1, p2, p3, out):
@@ -73,9 +76,9 @@ def tile_picked_census8_none_p_kernel(tc, x_words, x_scales, w1, gn, w2, offs, p
         w1_scales = keep.tile([P, H], U8, name="w1_scales", align_bytes=64)
         nc.vector.quantize_mx(w1_codes[:].bitcast(FP8X4), w1_scales[:], w1_bf[:].rearrange("p t m j -> p (t m j)"))
 
-        x_codes = keep.tile([P, S], U32, name="x_codes", align_bytes=64)
         low, high, whole = slice(0, HALF), slice(HALF, S), slice(0, S)
         third, fourth = slice(HALF, HALF + P), slice(HALF + P, S)
+        x_codes = keep.tile([P, S], U32, name="x_codes", align_bytes=64)
         for cells in (low, third, fourth):
             nc.vector.tensor_copy(x_codes[:, cells], word_table[:].indirect(picks[:, cells.start // 16 : cells.stop // 16]))
 
@@ -84,17 +87,11 @@ def tile_picked_census8_none_p_kernel(tc, x_words, x_scales, w1, gn, w2, offs, p
             nc.tensor.matmul_mx(y_ps, w1_codes[:, cols].bitcast(FP8X4), w1_scales[:, cols], x_codes[:, cells].bitcast(FP8X4), x_bytes[:, cells], start=True, stop=True)
 
         windows = [keep.tile([P, 2 * S], F32, name="window", tag="window%d" % t, align_bytes=64) for t in range(PACK)]
-        for t in (0, 2):
+        for t in (0, FETCHED_TILE):
             nc.gpsimd.memset(windows[t][:, S : 2 * S], 0.0)
         third_centre = keep.tile([P, S], F32, name="third_centre")
         last_centre = keep.tile([P, S], F32, name="last_centre", tag="last_centre", align_bytes=64)
         centres = [windows[1][:, S : 2 * S], windows[3][:, S : 2 * S], third_centre[:], last_centre[:]]
-
-        w2_src = w2_raw[:].rearrange("p j (c i) -> p c j i", i=4)
-
-        def round_w2(quarter, rounded):
-            w2_dst = rounded[:].rearrange("p (c i) j -> p c j i", i=4)
-            nc.scalar.copy(w2_dst[:, 32 * (quarter % 2) : 32 * (quarter % 2 + 1)], w2_src[:, 32 * quarter : 32 * (quarter + 1)])
 
         y_low = acc.tile([P, HALF], F32, name="y_low", tag="acc")
         y_third = acc.tile([P, P], F32, name="y_third", tag="acc")
@@ -117,39 +114,73 @@ def tile_picked_census8_none_p_kernel(tc, x_words, x_scales, w1, gn, w2, offs, p
             nc.scalar.copy(windows[t][:, whole], later[t][:])
             nc.sync.dma_start(centres[t], windows[t][:, whole])
 
-        gaps = {}
         softs = [keep.tile([P, 3, S], F32, name="soft%d" % t) for t in range(PACK)]
-        fetched = {}
         banks = [sums.tile([P, 2, 2, P], F32, name="bank", tag="bank") for b in range(4)]
 
-        def fetch(t, cells, tag):
-            fetched[t, cells.start] = keep.tile([P, cells.stop - cells.start], F32, name="fetched", tag=tag)
-            nc.scalar.activation(fetched[t, cells.start][:], windows[t][:].indirect(lists[0][:, cells.start // 16 : cells.stop // 16]), ACT.Copy)
+        def difference(t, term, cells, tag):
+            gap = keep.tile([P, cells.stop - cells.start], F32, name="gap", tag=tag, align_bytes=64)
+            entries = slice(cells.start // 16, cells.stop // 16)
+            nc.vector.tensor_tensor(gap[:], windows[t][:].indirect(lists[term][:, entries]), centres[t][:, cells], ALU.subtract)
+            return gap[:]
 
-        def difference(t, l, cells):
-            if (t, l) not in gaps:
-                gaps[t, l] = keep.tile([P, S], F32, name="gap", tag="gap%d_%d" % (t, l))
-            if l == 0 and (t, cells.start) in fetched:
-                nc.vector.tensor_tensor(gaps[t, l][:, cells], fetched[t, cells.start][:], centres[t][:, cells], ALU.subtract)
-            else:
-                entries = slice(cells.start // 16, cells.stop // 16)
-                nc.vector.tensor_tensor(gaps[t, l][:, cells], windows[t][:].indirect(lists[l][:, entries]), centres[t][:, cells], ALU.subtract)
-
-        def soften(t, l, cells):
-            difference(t, l, cells)
-            if l < 2:
-                nc.scalar.activation(softs[t][:, l, cells], gaps[t, l][:, cells], ACT.Tanh, scale=2.0)
-            else:
-                nc.scalar.activation(softs[t][:, l, cells], gaps[t, l][:, cells], ACT.Sigmoid, scale=4.0)
-
-        def term(t, l, cells):
-            soften(t, l, cells)
-            add_up(t, l, cells)
-
-        def add_up(t, l, cells):
+        def add_up(t, term, cells, gap):
+            func, scale = (ACT.Sigmoid, 4.0) if term == NEAR else (ACT.Tanh, 2.0)
+            nc.scalar.activation(softs[t][:, term, cells], gap, func, scale=scale)
             for b in range(cells.start // P, cells.stop // P):
-                for again in range(2 if l == 0 else 1):
-                    nc.tensor.matmul(banks[b][:, t % 2, t // 2, :], softs[t][:, l, b * P : (b + 1) * P], ident[:], start=(l == 0 and again == 0), stop=(l == 2), is_transpose=True)
+                for again in range(2 if term == DOUBLED else 1):
+                    nc.tensor.matmul(banks[b][:, t % 2, t // 2, :], softs[t][:, term, b * P : (b + 1) * P], ident[:], start=(term == DOUBLED and again == 0), stop=(term == NEAR), is_transpose=True)
+
+        def census(t, term, cells):
+            add_up(t, term, cells, difference(t, term, cells, "gap%d_%d_%d" % (t, term, cells.start)))
+
+        open_window(1)
+        open_window(2)
+        census(0, DOUBLED, low)
+        census(0, DOUBLED, high)
+        open_window(3)
+        fetched = keep.tile([P, S], F32, name="fetched", align_bytes=64)
+        nc.scalar.activation(fetched[:], windows[FETCHED_TILE][:].indirect(lists[DOUBLED][:]), ACT.Copy)
+        census(0, SINGLE, whole)
+        census(0, NEAR, whole)
+        for term in (DOUBLED, SINGLE, NEAR):
+            census(1, term, whole)
+        fetched_gap = keep.tile([P, S], F32, name="fetched_gap")
+        nc.vector.tensor_tensor(fetched_gap[:], fetched[:], centres[FETCHED_TILE], ALU.subtract)
+        add_up(FETCHED_TILE, DOUBLED, whole, fetched_gap[:])
+        census(FETCHED_TILE, SINGLE, whole)
+
+        gain_rows = keep.tile([P, 2, P, 2], F32, name="gain_rows", tag="fetched", align_bytes=64)
+        gain_ps = turn.tile([P, PACK, P], F32, name="gain_ps", tag="turned")
+        for t in range(PACK):
+            nc.tensor.transpose(gain_ps[:, t, :], gain[:, t : t + 1].to_broadcast([P, P]), ident[:])
+        nc.scalar.activation(gain_rows[:], gain_ps[:].rearrange("j (u e) p -> j u p e", e=2), ACT.Copy, scale=0.5)
+        census(FETCHED_TILE, NEAR, whole)
+
+        doubled_gap = difference(LAST_TILE, DOUBLED, whole, "doubled_gap")
+        for cells, single_tag in ((low, "single_gap"), (high, "z_rows0")):
+            add_up(LAST_TILE, DOUBLED, cells, doubled_gap[:, cells])
+            add_up(LAST_TILE, SINGLE, cells, difference(LAST_TILE, SINGLE, cells, single_tag))
+            census(LAST_TILE, NEAR, cells)
+
+        w2_low_bf = keep.tile([P, HALF, PACK], BF16, name="w2_low_bf", tag="window%d" % LAST_TILE, align_bytes=64)
+        w2_src = w2_raw[:].rearrange("p j (c i) -> p c j i", i=4)
+        w2_dst = w2_low_bf[:].rearrange("p (c i) j -> p c j i", i=4)
+        for groups in (slice(0, HALF // 8), slice(HALF // 8, HALF // 4)):
+            nc.scalar.copy(w2_dst[:, groups], w2_src[:, groups])
+        w2_high_bf = keep.tile([P, HALF, PACK], BF16, name="w2_high_bf", tag="last_centre", align_bytes=64)
+        nc.gpsimd.tensor_scalar(w2_high_bf[:], w2_raw[:, :, HALF:N].rearrange("p j n -> p n j"), 1.0, 0.0, ALU.mult, ALU.add)
+
+        def leave(b):
+            pool, tag = (acc, "acc") if b == 2 else (turn, "turned")
+            turned = pool.tile([P, 2, P], F32, name="turned", tag=tag)
+            z_rows = keep.tile([P, 2, P, 2], BF16, name="z_rows%d" % b, align_bytes=64)
+            nc.vector.scalar_tensor_tensor(z_rows[:].rearrange("j u p e -> j (u p) e"), banks[b][:].rearrange("j e u p -> j (u p) e"), -0.5, gain_rows[:].rearrange("j u p e -> j (u p) e"), ALU.add, ALU.mult)
+            for u in range(2):
+                nc.tensor.transpose(turned[:, u, :], z_rows[:, u].rearrange("j p e -> j (p e)").bitcast(F32), ident[:])
+            z_bf = keep.tile([P, P, PACK], BF16, name="z%d" % b, align_bytes=64)
+            z_words = z_bf[:].rearrange("p j t -> p (j t)").bitcast(F32).rearrange("p (j u) -> p j u", u=2)
+            nc.scalar.copy(z_words, turned[:].rearrange("p u j -> p j u"))
+            return z_bf
 
         w2_codes = []
         w2_scales = keep.tile([P, N], U8, name="w2_scales", align_bytes=64)
@@ -159,81 +190,26 @@ def tile_picked_census8_none_p_kernel(tc, x_words, x_scales, w1, gn, w2, offs, p
             nc.vector.quantize_mx(codes[:].bitcast(FP8X4), w2_scales[:, half * HALF : (half + 1) * HALF], rounded[:].rearrange("p n j -> p (n j)"))
             w2_codes.append(codes)
 
-        def weigh(b, gains, target):
-            z_rows = keep.tile([P, 2, P, 2], BF16, name="z_rows%d" % b, align_bytes=64)
-            nc.vector.scalar_tensor_tensor(z_rows[:].rearrange("j u p e -> j (u p) e"), banks[b][:].rearrange("j e u p -> j (u p) e"), -0.5, gains[:].rearrange("j u p e -> j (u p) e"), ALU.add, ALU.mult)
-            for u in range(2):
-                nc.tensor.transpose(target[:, u, :], z_rows[:, u].rearrange("j p e -> j (p e)").bitcast(F32), ident[:])
-
-        def words_of(z_bf):
-            return z_bf[:].rearrange("p j t -> p (j t)").bitcast(F32).rearrange("p (j u) -> p j u", u=2)
-
         def pack(z_bf):
-            width = z_bf.shape[1]
-            z_codes = ring.tile([P, width], U32, name="z_codes", tag="z_codes", align_bytes=64, bufs=4)
-            z_scales = ring.tile([P, width], U8, name="z_scales", tag="z_scales", align_bytes=64, bufs=4)
+            z_codes = ring.tile([P, P], U32, name="z_codes", tag="z_codes", align_bytes=64, bufs=4)
+            z_scales = ring.tile([P, P], U8, name="z_scales", tag="z_scales", align_bytes=64, bufs=4)
             nc.vector.quantize_mx(z_codes[:].bitcast(FP8X4), z_scales[:], z_bf[:].rearrange("p j t -> p (j t)"))
             return z_codes, z_scales
 
         def project(h, z_codes, z_scales, o_ps):
             for i in range(2):
                 cols = slice((2 * h + i) * P, (2 * h + i + 1) * P)
-                nc.tensor.matmul_mx(o_ps[i][:], w2_codes[h][:, i * P : (i + 1) * P].bitcast(FP8X4), w2_scales[:, cols], z_codes[:].bitcast(FP8X4), z_scales[:], start=True, stop=True)
+                nc.tensor.matmul_mx(o_ps[i], w2_codes[h][:, i * P : (i + 1) * P].bitcast(FP8X4), w2_scales[:, cols], z_codes[:].bitcast(FP8X4), z_scales[:], start=True, stop=True)
 
         def store(h, cells, result):
             nc.sync.dma_start(out[h * HALF : (h + 1) * HALF, cells].rearrange("(i p) j -> p i j", p=P), result[:])
 
-        def interleave(turned, name):
-            blocks = turned.shape[1]
-            z_bf = keep.tile([P, blocks * P, PACK], BF16, name=name, align_bytes=64)
-            nc.scalar.copy(words_of(z_bf).rearrange("p (b j) u -> p b j u", b=blocks), turned.rearrange("p b u j -> p b j u"))
-            return z_bf
-
-        open_window(1)
-        open_window(2)
-        term(0, 0, low)
-        term(0, 0, high)
-        open_window(3)
-        fetch(2, whole, "fetched2")
-        term(0, 1, whole)
-        term(0, 2, whole)
-        fetch(3, low, "fetched3")
-        term(1, 0, whole)
-        term(1, 1, whole)
-        fetch(3, high, "gap1_0")
-        term(1, 2, whole)
-        term(2, 0, whole)
-        term(2, 1, whole)
-        gain_rows = keep.tile([P, 2, P, 2], F32, name="gain_rows", tag="fetched2")
-        gain_ps = turn.tile([P, PACK, P], F32, name="gain_ps", tag="turned")
-        for t in range(PACK):
-            nc.tensor.transpose(gain_ps[:, t, :], gain[:, t : t + 1].to_broadcast([P, P]), ident[:])
-        nc.scalar.activation(gain_rows[:], gain_ps[:].rearrange("j (u e) p -> j u p e", e=2), ACT.Copy, scale=0.5)
-        term(2, 2, whole)
-        for cells in (low, high):
-            soften(3, 0, cells)
-        for cells in (low, high):
-            add_up(3, 0, cells)
-            for l in (1, 2):
-                term(3, l, cells)
-
-        w2_low_bf = keep.tile([P, HALF, PACK], BF16, name="w2_low_bf", tag="window3", align_bytes=64)
-        round_w2(0, w2_low_bf)
-        round_w2(1, w2_low_bf)
-        w2_high_bf = keep.tile([P, HALF, PACK], BF16, name="w2_high_bf", tag="last_centre", align_bytes=64)
-        nc.gpsimd.tensor_scalar(w2_high_bf[:], w2_raw[:, :, HALF:N].rearrange("p j n -> p n j"), 1.0, 0.0, ALU.mult, ALU.add)
-
-        def leave(b):
-            turned = turn.tile([P, 1, 2, P], F32, name="turned", tag="turned")
-            weigh(b, gain_rows, turned[:, 0])
-            return interleave(turned[:], "z%d" % b)
-
         z_tiles = [leave(b) for b in range(4)]
-        packed = [pack(z_tiles[0])]
         pack_w2(0, w2_low_bf)
-        packed.append(pack(z_tiles[1]))
+        packed = [pack(z_tiles[b]) for b in range(2)]
         pack_w2(1, w2_high_bf)
         packed.extend(pack(z_tiles[b]) for b in range(2, 4))
+
         movers = (nc.scalar.copy, nc.vector.tensor_copy)
         early = [sums.tile([P, 2, HALF], F32, name="early", tag="bank") for h in range(2)]
         for h in range(2):
@@ -249,7 +225,7 @@ def tile_picked_census8_none_p_kernel(tc, x_words, x_scales, w1, gn, w2, offs, p
             movers[h](results[h][:, :, 0:P], late[:])
         for h, (pool, tag) in enumerate(((sums, "bank"), (turn, "turned"))):
             last = [pool.tile([P, P], F32, name="last", tag=tag) for i in range(2)]
-            project(h, *packed[3], last)
+            project(h, *packed[3], [bank[:] for bank in last])
             for i in range(2):
                 movers[i](results[h][:, i, P:HALF], last[i][:])
         for h in range(2):

@@ -142,8 +142,11 @@ def tile_picked_census8_none_p_kernel(tc, x_words, x_scales, w1, gn, w2, offs, p
         nc.scalar.activation(fetched[:], windows[FETCHED_TILE][:].indirect(lists[DOUBLED][:]), ACT.Copy)
         census(0, SINGLE, whole)
         census(0, NEAR, whole)
-        for term in (DOUBLED, SINGLE, NEAR):
-            census(1, term, whole)
+        census(1, DOUBLED, whole)
+        census(1, SINGLE, whole)
+        fetched_half = keep.tile([P, HALF], F32, name="fetched_half", tag="gap1_%d_0" % DOUBLED, align_bytes=64)
+        nc.scalar.activation(fetched_half[:], windows[LAST_TILE][:].indirect(lists[DOUBLED][:, HALF // 16 : S // 16]), ACT.Copy)
+        census(1, NEAR, whole)
         fetched_gap = keep.tile([P, S], F32, name="fetched_gap")
         nc.vector.tensor_tensor(fetched_gap[:], fetched[:], centres[FETCHED_TILE], ALU.subtract)
         add_up(FETCHED_TILE, DOUBLED, whole, fetched_gap[:])
@@ -156,11 +159,13 @@ def tile_picked_census8_none_p_kernel(tc, x_words, x_scales, w1, gn, w2, offs, p
         nc.scalar.activation(gain_rows[:], gain_ps[:].rearrange("j (u e) p -> j u p e", e=2), ACT.Copy, scale=0.5)
         census(FETCHED_TILE, NEAR, whole)
 
-        doubled_gap = difference(LAST_TILE, DOUBLED, whole, "doubled_gap")
-        for cells, single_tag in ((low, "single_gap"), (high, "z_rows0")):
-            add_up(LAST_TILE, DOUBLED, cells, doubled_gap[:, cells])
-            add_up(LAST_TILE, SINGLE, cells, difference(LAST_TILE, SINGLE, cells, single_tag))
-            census(LAST_TILE, NEAR, cells)
+        for term in (DOUBLED, SINGLE, NEAR):
+            census(LAST_TILE, term, low)
+        half_gap = keep.tile([P, HALF], F32, name="half_gap")
+        nc.vector.tensor_tensor(half_gap[:], fetched_half[:], centres[LAST_TILE][:, high], ALU.subtract)
+        add_up(LAST_TILE, DOUBLED, high, half_gap[:])
+        add_up(LAST_TILE, SINGLE, high, difference(LAST_TILE, SINGLE, high, "z_rows0"))
+        census(LAST_TILE, NEAR, high)
 
         w2_low_bf = keep.tile([P, HALF, PACK], BF16, name="w2_low_bf", tag="window%d" % LAST_TILE, align_bytes=64)
         w2_src = w2_raw[:].rearrange("p j (c i) -> p c j i", i=4)
@@ -196,13 +201,13 @@ def tile_picked_census8_none_p_kernel(tc, x_words, x_scales, w1, gn, w2, offs, p
             nc.vector.quantize_mx(z_codes[:].bitcast(FP8X4), z_scales[:], z_bf[:].rearrange("p j t -> p (j t)"))
             return z_codes, z_scales
 
-        def project(h, z_codes, z_scales, o_ps):
-            for i in range(2):
-                cols = slice((2 * h + i) * P, (2 * h + i + 1) * P)
-                nc.tensor.matmul_mx(o_ps[i], w2_codes[h][:, i * P : (i + 1) * P].bitcast(FP8X4), w2_scales[:, cols], z_codes[:].bitcast(FP8X4), z_scales[:], start=True, stop=True)
+        def project(m, z_codes, z_scales, o_ps):
+            codes = w2_codes[m // 2][:, m % 2 * P : (m % 2 + 1) * P]
+            nc.tensor.matmul_mx(o_ps, codes.bitcast(FP8X4), w2_scales[:, m * P : (m + 1) * P], z_codes[:].bitcast(FP8X4), z_scales[:], start=True, stop=True)
 
-        def store(h, cells, result):
-            nc.sync.dma_start(out[h * HALF : (h + 1) * HALF, cells].rearrange("(i p) j -> p i j", p=P), result[:])
+        def store(first, cells, result):
+            rows = slice(first * P, (first + result.shape[1]) * P)
+            nc.sync.dma_start(out[rows, cells].rearrange("(i p) j -> p i j", p=P), result[:])
 
         z_tiles = [leave(b) for b in range(4)]
         pack_w2(0, w2_low_bf)
@@ -211,22 +216,23 @@ def tile_picked_census8_none_p_kernel(tc, x_words, x_scales, w1, gn, w2, offs, p
         packed.extend(pack(z_tiles[b]) for b in range(2, 4))
 
         movers = (nc.scalar.copy, nc.vector.tensor_copy)
-        early = [sums.tile([P, 2, HALF], F32, name="early", tag="bank") for h in range(2)]
-        for h in range(2):
-            for b in range(2):
-                project(h, *packed[b], [early[h][:, i, b * P : (b + 1) * P] for i in range(2)])
-            result = keep.tile([P, 2, HALF], F32, name="early_result%d" % h)
-            movers[h](result[:], early[h][:])
-            store(h, low, result)
+        for first, count, mover in ((0, 1, movers[0]), (1, 1, movers[0]), (2, 2, movers[1])):
+            early = sums.tile([P, count, HALF], F32, name="early", tag="bank")
+            for i in range(count):
+                for b in range(2):
+                    project(first + i, *packed[b], early[:, i, b * P : (b + 1) * P])
+            result = keep.tile([P, count, HALF], F32, name="early_result%d" % first)
+            mover(result[:], early[:])
+            store(first, low, result)
         results = [keep.tile([P, 2, HALF], F32, name="late_result%d" % h) for h in range(2)]
         for h in range(2):
             late = acc.tile([P, 2, P], F32, name="late", tag="acc")
-            project(h, *packed[2], [late[:, i, :] for i in range(2)])
-            movers[h](results[h][:, :, 0:P], late[:])
-        for h, (pool, tag) in enumerate(((sums, "bank"), (turn, "turned"))):
-            last = [pool.tile([P, P], F32, name="last", tag=tag) for i in range(2)]
-            project(h, *packed[3], [bank[:] for bank in last])
             for i in range(2):
-                movers[i](results[h][:, i, P:HALF], last[i][:])
-        for h in range(2):
-            store(h, high, results[h])
+                project(2 * h + i, *packed[2], late[:, i, :])
+            movers[h](results[h][:, :, 0:P], late[:])
+        for h, (pool, tag) in enumerate(((turn, "turned"), (sums, "bank"))):
+            for i in range(2):
+                last = pool.tile([P, P], F32, name="last", tag=tag)
+                project(2 * h + i, *packed[3], last[:])
+                movers[i](results[h][:, i, P:HALF], last[:])
+            store(2 * h, high, results[h])

@@ -20,16 +20,16 @@ P = 128
 PACK = 4
 HALF = S // 2
 SCALAR_SHARE = 44
-FETCHED_TILE = 2
-LAST_TILE = PACK - 1
 DOUBLED, SINGLE, NEAR = 0, 1, 2
+RING = 4
+ADDS = 4 * PACK
 
 
 def tile_picked_census8_none_p_kernel(tc, x_words, x_scales, w1, gn, w2, offs, p1, p2, p3, out):
     nc = tc.nc
     with ExitStack() as ctx:
         keep = ctx.enter_context(tc.tile_pool(name="keep", bufs=1))
-        ring = ctx.enter_context(tc.tile_pool(name="ring", bufs=2))
+        ring = ctx.enter_context(tc.tile_pool(name="ring", bufs=RING))
         acc = ctx.enter_context(tc.psum_pool(name="acc", bufs=2))
         sums = ctx.enter_context(tc.psum_pool(name="sums", bufs=4))
         turn = ctx.enter_context(tc.psum_pool(name="turn", bufs=2))
@@ -61,6 +61,8 @@ def tile_picked_census8_none_p_kernel(tc, x_words, x_scales, w1, gn, w2, offs, p
         nc.scalar.activation(warm[:], warm[:], ACT.Sigmoid)
         ident = keep.tile([P, P], F32, name="ident")
         make_identity(nc, ident[:])
+        gain = keep.tile([P, PACK], F32, name="gain")
+        nc.gpsimd.dma_start(gain[:], gn.rearrange("(p t) o -> p (t o)", t=PACK))
 
         w1_bf = keep.tile([P, PACK, P, PACK], BF16, name="w1_bf", align_bytes=64)
         w1_dst = w1_bf[:].rearrange("p t m j -> p m j t")
@@ -69,12 +71,16 @@ def tile_picked_census8_none_p_kernel(tc, x_words, x_scales, w1, gn, w2, offs, p
         nc.vector.tensor_copy(w1_dst[:, SCALAR_SHARE:P], w1_src[:, SCALAR_SHARE:P])
         w2_raw = keep.tile([P, PACK, N], F32, name="w2_raw", tag="raw")
         nc.sync.dma_start(w2_raw[:], w2.rearrange("(p j) c -> p j c", j=PACK))
-        gain = keep.tile([P, PACK], F32, name="gain", tag="w1_bf", align_bytes=64)
-        nc.sync.dma_start(gain[:], gn.rearrange("(p t) o -> p (t o)", t=PACK))
 
         w1_codes = keep.tile([P, H], U32, name="w1_codes", align_bytes=64)
         w1_scales = keep.tile([P, H], U8, name="w1_scales", align_bytes=64)
         nc.vector.quantize_mx(w1_codes[:].bitcast(FP8X4), w1_scales[:], w1_bf[:].rearrange("p t m j -> p (t m j)"))
+
+        gain_rows = keep.tile([P, 2, P, 2], F32, name="gain_rows", tag="w1_bf", align_bytes=64)
+        gain_ps = turn.tile([P, PACK, P], F32, name="gain_ps", tag="turned")
+        for t in range(PACK):
+            nc.tensor.transpose(gain_ps[:, t, :], gain[:, t : t + 1].to_broadcast([P, P]), ident[:])
+        nc.scalar.activation(gain_rows[:], gain_ps[:].rearrange("j (u e) p -> j u p e", e=2), ACT.Copy, scale=0.5)
 
         low, high, whole = slice(0, HALF), slice(HALF, S), slice(0, S)
         third, fourth = slice(HALF, HALF + P), slice(HALF + P, S)
@@ -86,12 +92,11 @@ def tile_picked_census8_none_p_kernel(tc, x_words, x_scales, w1, gn, w2, offs, p
             cols = slice(t * P, (t + 1) * P)
             nc.tensor.matmul_mx(y_ps, w1_codes[:, cols].bitcast(FP8X4), w1_scales[:, cols], x_codes[:, cells].bitcast(FP8X4), x_bytes[:, cells], start=True, stop=True)
 
-        windows = [keep.tile([P, 2 * S], F32, name="window", tag="window%d" % t, align_bytes=64) for t in range(PACK)]
-        for t in (0, FETCHED_TILE):
-            nc.gpsimd.memset(windows[t][:, S : 2 * S], 0.0)
-        third_centre = keep.tile([P, S], F32, name="third_centre")
-        last_centre = keep.tile([P, S], F32, name="last_centre", tag="last_centre", align_bytes=64)
-        centres = [windows[1][:, S : 2 * S], windows[3][:, S : 2 * S], third_centre[:], last_centre[:]]
+        windows = [keep.tile([P, S if t == 3 else 2 * S], F32, name="window%d" % t, align_bytes=64) for t in range(PACK)]
+        nc.gpsimd.memset(windows[0][:, S : 2 * S], 0.0)
+        centre2 = keep.tile([P, S], F32, name="centre2")
+        centre3 = keep.tile([P, S], F32, name="centre3", align_bytes=64)
+        centres = [windows[1][:, S : 2 * S], windows[2][:, S : 2 * S], centre2[:], centre3[:]]
 
         y_low = acc.tile([P, HALF], F32, name="y_low", tag="acc")
         y_third = acc.tile([P, P], F32, name="y_third", tag="acc")
@@ -116,69 +121,67 @@ def tile_picked_census8_none_p_kernel(tc, x_words, x_scales, w1, gn, w2, offs, p
 
         softs = [keep.tile([P, 3, S], F32, name="soft%d" % t) for t in range(PACK)]
         banks = [sums.tile([P, 2, 2, P], F32, name="bank", tag="bank") for b in range(4)]
+        added = [[] for b in range(4)]
 
-        def difference(t, term, cells, tag):
-            gap = keep.tile([P, cells.stop - cells.start], F32, name="gap", tag=tag, align_bytes=64)
-            entries = slice(cells.start // 16, cells.stop // 16)
-            nc.vector.tensor_tensor(gap[:], windows[t][:].indirect(lists[term][:, entries]), centres[t][:, cells], ALU.subtract)
-            return gap[:]
+        def looked_up(t, term, cells):
+            return windows[t][:].indirect(lists[term][:, cells.start // 16 : cells.stop // 16])
 
-        def add_up(t, term, cells, gap):
+        def add_up(t, term, cells, neighbours):
+            gap = ring.tile([P, cells.stop - cells.start], F32, name="gap", tag="work", align_bytes=64)
+            nc.vector.tensor_tensor(gap[:], neighbours, centres[t][:, cells], ALU.subtract)
             func, scale = (ACT.Sigmoid, 4.0) if term == NEAR else (ACT.Tanh, 2.0)
-            nc.scalar.activation(softs[t][:, term, cells], gap, func, scale=scale)
+            nc.scalar.activation(softs[t][:, term, cells], gap[:], func, scale=scale)
             for b in range(cells.start // P, cells.stop // P):
                 for again in range(2 if term == DOUBLED else 1):
-                    nc.tensor.matmul(banks[b][:, t % 2, t // 2, :], softs[t][:, term, b * P : (b + 1) * P], ident[:], start=(term == DOUBLED and again == 0), stop=(term == NEAR), is_transpose=True)
+                    added[b].append(term)
+                    nc.tensor.matmul(banks[b][:, t % 2, t // 2, :], softs[t][:, term, b * P : (b + 1) * P], ident[:], start=len(added[b]) == 1, stop=len(added[b]) == ADDS, is_transpose=True)
 
         def census(t, term, cells):
-            add_up(t, term, cells, difference(t, term, cells, "gap%d_%d_%d" % (t, term, cells.start)))
+            add_up(t, term, cells, looked_up(t, term, cells))
+
+        fetched = {t: keep.tile([P, S], F32, name="fetched%d" % t, align_bytes=64) for t in (1, 2)}
+
+        def fetch(t, cells):
+            nc.scalar.activation(fetched[t][:, cells], looked_up(t, NEAR, cells), ACT.Copy)
 
         open_window(1)
-        open_window(2)
         census(0, DOUBLED, low)
+        open_window(2)
         census(0, DOUBLED, high)
         open_window(3)
-        fetched = keep.tile([P, S], F32, name="fetched", align_bytes=64)
-        nc.scalar.activation(fetched[:], windows[FETCHED_TILE][:].indirect(lists[DOUBLED][:]), ACT.Copy)
         census(0, SINGLE, whole)
+        fetch(1, low)
         census(0, NEAR, whole)
+        fetch(1, high)
         census(1, DOUBLED, whole)
+        fetch(2, low)
+        census(2, DOUBLED, whole)
+        fetch(2, high)
+        census(3, DOUBLED, low)
+        census(3, DOUBLED, high)
+        add_up(1, NEAR, whole, fetched[1][:])
         census(1, SINGLE, whole)
-        fetched_half = keep.tile([P, HALF], F32, name="fetched_half", tag="gap1_%d_0" % DOUBLED, align_bytes=64)
-        nc.scalar.activation(fetched_half[:], windows[LAST_TILE][:].indirect(lists[DOUBLED][:, HALF // 16 : S // 16]), ACT.Copy)
-        census(1, NEAR, whole)
-        fetched_gap = keep.tile([P, S], F32, name="fetched_gap")
-        nc.vector.tensor_tensor(fetched_gap[:], fetched[:], centres[FETCHED_TILE], ALU.subtract)
-        add_up(FETCHED_TILE, DOUBLED, whole, fetched_gap[:])
-        census(FETCHED_TILE, SINGLE, whole)
+        add_up(2, NEAR, whole, fetched[2][:])
+        for t, term in ((2, SINGLE), (3, SINGLE), (3, NEAR)):
+            census(t, term, low)
+        census(2, SINGLE, high)
+        census(3, SINGLE, third)
+        census(3, NEAR, third)
+        census(3, SINGLE, fourth)
+        census(3, NEAR, fourth)
 
-        gain_rows = keep.tile([P, 2, P, 2], F32, name="gain_rows", tag="fetched", align_bytes=64)
-        gain_ps = turn.tile([P, PACK, P], F32, name="gain_ps", tag="turned")
-        for t in range(PACK):
-            nc.tensor.transpose(gain_ps[:, t, :], gain[:, t : t + 1].to_broadcast([P, P]), ident[:])
-        nc.scalar.activation(gain_rows[:], gain_ps[:].rearrange("j (u e) p -> j u p e", e=2), ACT.Copy, scale=0.5)
-        census(FETCHED_TILE, NEAR, whole)
-
-        for term in (DOUBLED, SINGLE, NEAR):
-            census(LAST_TILE, term, low)
-        half_gap = keep.tile([P, HALF], F32, name="half_gap")
-        nc.vector.tensor_tensor(half_gap[:], fetched_half[:], centres[LAST_TILE][:, high], ALU.subtract)
-        add_up(LAST_TILE, DOUBLED, high, half_gap[:])
-        add_up(LAST_TILE, SINGLE, high, difference(LAST_TILE, SINGLE, high, "z_rows0"))
-        census(LAST_TILE, NEAR, high)
-
-        w2_low_bf = keep.tile([P, HALF, PACK], BF16, name="w2_low_bf", tag="window%d" % LAST_TILE, align_bytes=64)
+        w2_low_bf = keep.tile([P, HALF, PACK], BF16, name="w2_low_bf", tag="window3", align_bytes=64)
         w2_src = w2_raw[:].rearrange("p j (c i) -> p c j i", i=4)
         w2_dst = w2_low_bf[:].rearrange("p (c i) j -> p c j i", i=4)
         for groups in (slice(0, HALF // 8), slice(HALF // 8, HALF // 4)):
             nc.scalar.copy(w2_dst[:, groups], w2_src[:, groups])
-        w2_high_bf = keep.tile([P, HALF, PACK], BF16, name="w2_high_bf", tag="last_centre", align_bytes=64)
+        w2_high_bf = keep.tile([P, HALF, PACK], BF16, name="w2_high_bf", tag="centre3", align_bytes=64)
         nc.gpsimd.tensor_scalar(w2_high_bf[:], w2_raw[:, :, HALF:N].rearrange("p j n -> p n j"), 1.0, 0.0, ALU.mult, ALU.add)
 
         def leave(b):
             pool, tag = (acc, "acc") if b == 2 else (turn, "turned")
             turned = pool.tile([P, 2, P], F32, name="turned", tag=tag)
-            z_rows = keep.tile([P, 2, P, 2], BF16, name="z_rows%d" % b, align_bytes=64)
+            z_rows = ring.tile([P, 2, P, 2], BF16, name="z_rows", tag="work", align_bytes=64)
             nc.vector.scalar_tensor_tensor(z_rows[:].rearrange("j u p e -> j (u p) e"), banks[b][:].rearrange("j e u p -> j (u p) e"), -0.5, gain_rows[:].rearrange("j u p e -> j (u p) e"), ALU.add, ALU.mult)
             for u in range(2):
                 nc.tensor.transpose(turned[:, u, :], z_rows[:, u].rearrange("j p e -> j (p e)").bitcast(F32), ident[:])
@@ -191,48 +194,32 @@ def tile_picked_census8_none_p_kernel(tc, x_words, x_scales, w1, gn, w2, offs, p
         w2_scales = keep.tile([P, N], U8, name="w2_scales", align_bytes=64)
 
         def pack_w2(half, rounded):
-            codes = keep.tile([P, HALF], U32, name="w2_codes", tag="z_rows%d" % (1 + half), align_bytes=64)
+            codes = ring.tile([P, HALF], U32, name="w2_codes", tag="work", align_bytes=64)
             nc.vector.quantize_mx(codes[:].bitcast(FP8X4), w2_scales[:, half * HALF : (half + 1) * HALF], rounded[:].rearrange("p n j -> p (n j)"))
             w2_codes.append(codes)
 
-        def pack(z_bf):
-            z_codes = ring.tile([P, P], U32, name="z_codes", tag="z_codes", align_bytes=64, bufs=4)
-            z_scales = ring.tile([P, P], U8, name="z_scales", tag="z_scales", align_bytes=64, bufs=4)
-            nc.vector.quantize_mx(z_codes[:].bitcast(FP8X4), z_scales[:], z_bf[:].rearrange("p j t -> p (j t)"))
-            return z_codes, z_scales
+        z_codes = keep.tile([P, S], U32, name="z_codes", align_bytes=64)
+        z_scales = keep.tile([P, S], U8, name="z_scales", align_bytes=64)
 
-        def project(m, z_codes, z_scales, o_ps):
-            codes = w2_codes[m // 2][:, m % 2 * P : (m % 2 + 1) * P]
-            nc.tensor.matmul_mx(o_ps, codes.bitcast(FP8X4), w2_scales[:, m * P : (m + 1) * P], z_codes[:].bitcast(FP8X4), z_scales[:], start=True, stop=True)
-
-        def store(first, cells, result):
-            rows = slice(first * P, (first + result.shape[1]) * P)
-            nc.sync.dma_start(out[rows, cells].rearrange("(i p) j -> p i j", p=P), result[:])
+        def pack(b, z_bf):
+            cells = slice(b * P, (b + 1) * P)
+            nc.vector.quantize_mx(z_codes[:, cells].bitcast(FP8X4), z_scales[:, cells], z_bf[:].rearrange("p j t -> p (j t)"))
 
         z_tiles = [leave(b) for b in range(4)]
         pack_w2(0, w2_low_bf)
-        packed = [pack(z_tiles[b]) for b in range(2)]
+        pack(0, z_tiles[0])
+        pack(1, z_tiles[1])
         pack_w2(1, w2_high_bf)
-        packed.extend(pack(z_tiles[b]) for b in range(2, 4))
+        pack(2, z_tiles[2])
+        pack(3, z_tiles[3])
 
         movers = (nc.scalar.copy, nc.vector.tensor_copy)
-        for first, count, mover in ((0, 1, movers[0]), (1, 1, movers[0]), (2, 2, movers[1])):
-            early = sums.tile([P, count, HALF], F32, name="early", tag="bank")
-            for i in range(count):
-                for b in range(2):
-                    project(first + i, *packed[b], early[:, i, b * P : (b + 1) * P])
-            result = keep.tile([P, count, HALF], F32, name="early_result%d" % first)
-            mover(result[:], early[:])
-            store(first, low, result)
-        results = [keep.tile([P, 2, HALF], F32, name="late_result%d" % h) for h in range(2)]
-        for h in range(2):
-            late = acc.tile([P, 2, P], F32, name="late", tag="acc")
-            for i in range(2):
-                project(2 * h + i, *packed[2], late[:, i, :])
-            movers[h](results[h][:, :, 0:P], late[:])
-        for h, (pool, tag) in enumerate(((turn, "turned"), (sums, "bank"))):
-            for i in range(2):
-                last = pool.tile([P, P], F32, name="last", tag=tag)
-                project(2 * h + i, *packed[3], last[:])
-                movers[i](results[h][:, i, P:HALF], last[:])
-            store(2 * h, high, results[h])
+        for cells, places in ((low, [(sums, "bank")] * 4), (high, [(acc, "acc")] * 2 + [(turn, "turned")] * 2)):
+            for m, (pool, tag) in enumerate(places):
+                rows = slice(m * P, (m + 1) * P)
+                o_ps = pool.tile([P, HALF], F32, name="o_ps", tag=tag)
+                codes = w2_codes[m // 2][:, m % 2 * P : (m % 2 + 1) * P]
+                nc.tensor.matmul_mx(o_ps[:], codes.bitcast(FP8X4), w2_scales[:, rows], z_codes[:, cells].bitcast(FP8X4), z_scales[:, cells], start=True, stop=True)
+                result = keep.tile([P, HALF], F32, name="result%d_%d" % (m, cells.start))
+                movers[m % 2](result[:], o_ps[:])
+                nc.sync.dma_start(out[rows, cells], result[:])

@@ -21,7 +21,7 @@ PACK = 4
 HALF = S // 2
 SCALAR_SHARE = 44
 DOUBLED, SINGLE, NEAR = 0, 1, 2
-RING = 4
+RING = 5
 ADDS = 4 * PACK
 
 
@@ -39,10 +39,10 @@ def tile_picked_census8_none_p_kernel(tc, x_words, x_scales, w1, gn, w2, offs, p
             nc.sync.dma_start(held[:], source)
             return held
 
-        warm = keep.tile([P, 1], F32, name="warm")
-        nc.gpsimd.memset(warm[:], 0.0)
         scale_table = keep.tile([P, T], U8, name="scale_table", align_bytes=64)
         nc.gpsimd.memset(scale_table[:].bitcast(I32), 0)
+        warm = keep.tile([P, 1], F32, name="warm")
+        nc.gpsimd.memset(warm[:], 0.0)
 
         w1_rows = w1.rearrange("(p j) c -> p j c", j=PACK)
         w1_raw = keep.tile([P, PACK, H], F32, name="w1_raw", tag="raw")
@@ -126,8 +126,8 @@ def tile_picked_census8_none_p_kernel(tc, x_words, x_scales, w1, gn, w2, offs, p
         def looked_up(t, term, cells):
             return windows[t][:].indirect(lists[term][:, cells.start // 16 : cells.stop // 16])
 
-        def add_up(t, term, cells, neighbours):
-            gap = ring.tile([P, cells.stop - cells.start], F32, name="gap", tag="work", align_bytes=64)
+        def add_up(t, term, cells, neighbours, pool=ring, tag="work"):
+            gap = pool.tile([P, cells.stop - cells.start], F32, name="gap", tag=tag, align_bytes=64)
             nc.vector.tensor_tensor(gap[:], neighbours, centres[t][:, cells], ALU.subtract)
             func, scale = (ACT.Sigmoid, 4.0) if term == NEAR else (ACT.Tanh, 2.0)
             nc.scalar.activation(softs[t][:, term, cells], gap[:], func, scale=scale)
@@ -136,41 +136,43 @@ def tile_picked_census8_none_p_kernel(tc, x_words, x_scales, w1, gn, w2, offs, p
                     added[b].append(term)
                     nc.tensor.matmul(banks[b][:, t % 2, t // 2, :], softs[t][:, term, b * P : (b + 1) * P], ident[:], start=len(added[b]) == 1, stop=len(added[b]) == ADDS, is_transpose=True)
 
-        def census(t, term, cells):
-            add_up(t, term, cells, looked_up(t, term, cells))
+        def census(t, term, cells, *place):
+            add_up(t, term, cells, looked_up(t, term, cells), *place)
 
-        fetched = {t: keep.tile([P, S], F32, name="fetched%d" % t, align_bytes=64) for t in (1, 2)}
-
-        def fetch(t, cells):
-            nc.scalar.activation(fetched[t][:, cells], looked_up(t, NEAR, cells), ACT.Copy)
+        def fetch(t, term, cells, into):
+            nc.scalar.activation(into, looked_up(t, term, cells), ACT.Copy)
 
         open_window(1)
-        census(0, DOUBLED, low)
+        census(0, DOUBLED, low, keep, "near1")
         open_window(2)
         census(0, DOUBLED, high)
         open_window(3)
-        census(0, SINGLE, whole)
-        fetch(1, low)
+        near1 = keep.tile([P, S], F32, name="near1", align_bytes=64)
+        fetch(1, NEAR, low, near1[:, low])
+        census(0, SINGLE, whole, keep, "single2")
+        fetch(1, NEAR, high, near1[:, high])
         census(0, NEAR, whole)
-        fetch(1, high)
-        census(1, DOUBLED, whole)
-        fetch(2, low)
+        single2 = keep.tile([P, HALF], F32, name="single2", align_bytes=64)
+        fetch(2, SINGLE, high, single2[:])
+        census(1, DOUBLED, whole, keep, "near2")
         census(2, DOUBLED, whole)
-        fetch(2, high)
+        near2 = keep.tile([P, S], F32, name="near2", align_bytes=64)
+        fetch(2, NEAR, whole, near2[:])
         census(3, DOUBLED, low)
         census(3, DOUBLED, high)
-        add_up(1, NEAR, whole, fetched[1][:])
+        add_up(1, NEAR, whole, near1[:])
         census(1, SINGLE, whole)
-        add_up(2, NEAR, whole, fetched[2][:])
-        for t, term in ((2, SINGLE), (3, SINGLE), (3, NEAR)):
-            census(t, term, low)
-        census(2, SINGLE, high)
+        census(2, SINGLE, low)
+        add_up(2, NEAR, whole, near2[:])
+        census(3, SINGLE, low)
+        census(3, NEAR, low)
+        add_up(2, SINGLE, high, single2[:])
         census(3, SINGLE, third)
         census(3, NEAR, third)
         census(3, SINGLE, fourth)
         census(3, NEAR, fourth)
 
-        w2_low_bf = keep.tile([P, HALF, PACK], BF16, name="w2_low_bf", tag="window3", align_bytes=64)
+        w2_low_bf = ring.tile([P, HALF, PACK], BF16, name="w2_low_bf", tag="work", align_bytes=64)
         w2_src = w2_raw[:].rearrange("p j (c i) -> p c j i", i=4)
         w2_dst = w2_low_bf[:].rearrange("p (c i) j -> p c j i", i=4)
         for groups in (slice(0, HALF // 8), slice(HALF // 8, HALF // 4)):

@@ -20,6 +20,7 @@ P = 128
 PACK = 4
 HALF = S // 2
 SCALAR_SHARE = 44
+W2_SPLIT = 192
 DOUBLED, SINGLE, NEAR = 0, 1, 2
 RING = 5
 ADDS = 4 * PACK
@@ -161,30 +162,32 @@ def tile_picked_census8_none_p_kernel(tc, x_words, x_scales, w1, gn, w2, offs, p
         census(3, DOUBLED, low)
         census(3, DOUBLED, high)
         add_up(1, NEAR, whole, near1[:])
-        census(1, SINGLE, whole)
+        census(1, SINGLE, low)
         census(2, SINGLE, low)
         add_up(2, NEAR, whole, near2[:])
         census(3, SINGLE, low)
         census(3, NEAR, low)
+        census(1, SINGLE, high)
         add_up(2, SINGLE, high, single2[:])
         census(3, SINGLE, third)
         census(3, NEAR, third)
         census(3, SINGLE, fourth)
         census(3, NEAR, fourth)
 
-        w2_low_bf = ring.tile([P, HALF, PACK], BF16, name="w2_low_bf", tag="work", align_bytes=64)
+        w2_first = ring.tile([P, W2_SPLIT, PACK], BF16, name="w2_first", tag="work", align_bytes=64)
         w2_src = w2_raw[:].rearrange("p j (c i) -> p c j i", i=4)
-        w2_dst = w2_low_bf[:].rearrange("p (c i) j -> p c j i", i=4)
-        for groups in (slice(0, HALF // 8), slice(HALF // 8, HALF // 4)):
+        w2_dst = w2_first[:].rearrange("p (c i) j -> p c j i", i=4)
+        for groups in (slice(0, P // 4), slice(P // 4, W2_SPLIT // 4)):
             nc.scalar.copy(w2_dst[:, groups], w2_src[:, groups])
-        w2_high_bf = keep.tile([P, HALF, PACK], BF16, name="w2_high_bf", tag="centre3", align_bytes=64)
-        nc.gpsimd.tensor_scalar(w2_high_bf[:], w2_raw[:, :, HALF:N].rearrange("p j n -> p n j"), 1.0, 0.0, ALU.mult, ALU.add)
+        w2_rest = keep.tile([P, N - W2_SPLIT, PACK], BF16, name="w2_rest", tag="centre3", align_bytes=64)
+        nc.gpsimd.tensor_scalar(w2_rest[:], w2_raw[:, :, W2_SPLIT:N].rearrange("p j n -> p n j"), 1.0, 0.0, ALU.mult, ALU.add)
 
         def leave(b):
             pool, tag = (acc, "acc") if b == 2 else (turn, "turned")
             turned = pool.tile([P, 2, P], F32, name="turned", tag=tag)
             z_rows = ring.tile([P, 2, P, 2], BF16, name="z_rows", tag="work", align_bytes=64)
-            nc.vector.scalar_tensor_tensor(z_rows[:].rearrange("j u p e -> j (u p) e"), banks[b][:].rearrange("j e u p -> j (u p) e"), -0.5, gain_rows[:].rearrange("j u p e -> j (u p) e"), ALU.add, ALU.mult)
+            for us in (slice(0, 1), slice(1, 2)) if b % 2 else (slice(0, 2),):
+                nc.vector.scalar_tensor_tensor(z_rows[:, us].rearrange("j u p e -> j (u p) e"), banks[b][:, :, us].rearrange("j e u p -> j (u p) e"), -0.5, gain_rows[:, us].rearrange("j u p e -> j (u p) e"), ALU.add, ALU.mult)
             for u in range(2):
                 nc.tensor.transpose(turned[:, u, :], z_rows[:, u].rearrange("j p e -> j (p e)").bitcast(F32), ident[:])
             z_bf = keep.tile([P, P, PACK], BF16, name="z%d" % b, align_bytes=64)
@@ -192,13 +195,10 @@ def tile_picked_census8_none_p_kernel(tc, x_words, x_scales, w1, gn, w2, offs, p
             nc.scalar.copy(z_words, turned[:].rearrange("p u j -> p j u"))
             return z_bf
 
-        w2_codes = []
         w2_scales = keep.tile([P, N], U8, name="w2_scales", align_bytes=64)
 
-        def pack_w2(half, rounded):
-            codes = ring.tile([P, HALF], U32, name="w2_codes", tag="work", align_bytes=64)
-            nc.vector.quantize_mx(codes[:].bitcast(FP8X4), w2_scales[:, half * HALF : (half + 1) * HALF], rounded[:].rearrange("p n j -> p (n j)"))
-            w2_codes.append(codes)
+        def pack_w2(columns, rounded):
+            nc.vector.quantize_mx(w2_codes[:, columns].bitcast(FP8X4), w2_scales[:, columns], rounded.rearrange("p n j -> p (n j)"))
 
         z_codes = keep.tile([P, S], U32, name="z_codes", align_bytes=64)
         z_scales = keep.tile([P, S], U8, name="z_scales", align_bytes=64)
@@ -208,10 +208,13 @@ def tile_picked_census8_none_p_kernel(tc, x_words, x_scales, w1, gn, w2, offs, p
             nc.vector.quantize_mx(z_codes[:, cells].bitcast(FP8X4), z_scales[:, cells], z_bf[:].rearrange("p j t -> p (j t)"))
 
         z_tiles = [leave(b) for b in range(4)]
-        pack_w2(0, w2_low_bf)
+        w2_codes = ring.tile([P, N], U32, name="w2_codes", tag="work", align_bytes=64)
+        pack_w2(slice(0, P), w2_first[:, 0:P])
         pack(0, z_tiles[0])
         pack(1, z_tiles[1])
-        pack_w2(1, w2_high_bf)
+        pack_w2(slice(P, W2_SPLIT), w2_first[:, P:W2_SPLIT])
+        pack_w2(slice(W2_SPLIT, HALF), w2_rest[:, 0 : HALF - W2_SPLIT])
+        pack_w2(high, w2_rest[:, HALF - W2_SPLIT : N - W2_SPLIT])
         pack(2, z_tiles[2])
         pack(3, z_tiles[3])
 
@@ -220,8 +223,7 @@ def tile_picked_census8_none_p_kernel(tc, x_words, x_scales, w1, gn, w2, offs, p
             for m, (pool, tag) in enumerate(places):
                 rows = slice(m * P, (m + 1) * P)
                 o_ps = pool.tile([P, HALF], F32, name="o_ps", tag=tag)
-                codes = w2_codes[m // 2][:, m % 2 * P : (m % 2 + 1) * P]
-                nc.tensor.matmul_mx(o_ps[:], codes.bitcast(FP8X4), w2_scales[:, rows], z_codes[:, cells].bitcast(FP8X4), z_scales[:, cells], start=True, stop=True)
+                nc.tensor.matmul_mx(o_ps[:], w2_codes[:, rows].bitcast(FP8X4), w2_scales[:, rows], z_codes[:, cells].bitcast(FP8X4), z_scales[:, cells], start=True, stop=True)
                 result = keep.tile([P, HALF], F32, name="result%d_%d" % (m, cells.start))
                 movers[m % 2](result[:], o_ps[:])
                 nc.sync.dma_start(out[rows, cells], result[:])

@@ -159,15 +159,17 @@ def tile_picked_census8_none_p_kernel(tc, x_words, x_scales, w1, gn, w2, offs, p
         census(2, DOUBLED, whole)
         near2 = keep.tile([P, S], F32, name="near2", align_bytes=64)
         fetch(2, NEAR, whole, near2[:])
-        census(3, DOUBLED, low)
+        census(3, DOUBLED, low, keep, "single1")
         census(3, DOUBLED, high)
+        single1 = keep.tile([P, HALF], F32, name="single1", align_bytes=64)
+        fetch(1, SINGLE, high, single1[:])
         add_up(1, NEAR, whole, near1[:])
         census(1, SINGLE, low)
         census(2, SINGLE, low)
         add_up(2, NEAR, whole, near2[:])
         census(3, SINGLE, low)
         census(3, NEAR, low)
-        census(1, SINGLE, high)
+        add_up(1, SINGLE, high, single1[:])
         add_up(2, SINGLE, high, single2[:])
         census(3, SINGLE, third)
         census(3, NEAR, third)
@@ -218,12 +220,28 @@ def tile_picked_census8_none_p_kernel(tc, x_words, x_scales, w1, gn, w2, offs, p
         pack(2, z_tiles[2])
         pack(3, z_tiles[3])
 
+        results = [keep.tile([P, PACK, HALF], F32, name="result%d" % h) for h in range(2)]
+
+        def held(m, cells):
+            return results[cells.start // HALF][:, m, cells.start % HALF : (cells.stop - 1) % HALF + 1]
+
+        def project(m, cells, place, mover):
+            rows = slice(m * P, (m + 1) * P)
+            o_ps = place[0].tile([P, cells.stop - cells.start], F32, name="o_ps", tag=place[1])
+            nc.tensor.matmul_mx(o_ps[:], w2_codes[:, rows].bitcast(FP8X4), w2_scales[:, rows], z_codes[:, cells].bitcast(FP8X4), z_scales[:, cells], start=True, stop=True)
+            mover(held(m, cells), o_ps[:])
+
+        def store(m, cells):
+            nc.sync.dma_start(out[m * P : (m + 1) * P, cells], held(m, cells))
+
+        in_sums, in_acc, in_turn = (sums, "bank"), (acc, "acc"), (turn, "turned")
         movers = (nc.scalar.copy, nc.vector.tensor_copy)
-        for cells, places in ((low, [(sums, "bank")] * 4), (high, [(acc, "acc")] * 2 + [(turn, "turned")] * 2)):
-            for m, (pool, tag) in enumerate(places):
-                rows = slice(m * P, (m + 1) * P)
-                o_ps = pool.tile([P, HALF], F32, name="o_ps", tag=tag)
-                nc.tensor.matmul_mx(o_ps[:], w2_codes[:, rows].bitcast(FP8X4), w2_scales[:, rows], z_codes[:, cells].bitcast(FP8X4), z_scales[:, cells], start=True, stop=True)
-                result = keep.tile([P, HALF], F32, name="result%d_%d" % (m, cells.start))
-                movers[m % 2](result[:], o_ps[:])
-                nc.sync.dma_start(out[rows, cells], result[:])
+        project(0, slice(0, P), in_sums, movers[0])
+        project(0, slice(P, HALF), in_sums, movers[0])
+        store(0, low)
+        for m, cells, place in ((1, low, in_sums), (2, low, in_sums), (3, low, in_acc), (0, high, in_acc), (1, high, in_turn), (2, high, in_turn)):
+            project(m, cells, place, movers[m % 2])
+            store(m, cells)
+        project(3, third, in_sums, movers[1])
+        project(3, fourth, in_sums, movers[0])
+        store(3, high)

@@ -93,11 +93,10 @@ def tile_picked_census8_none_p_kernel(tc, x_words, x_scales, w1, gn, w2, offs, p
             cols = slice(t * P, (t + 1) * P)
             nc.tensor.matmul_mx(y_ps, w1_codes[:, cols].bitcast(FP8X4), w1_scales[:, cols], x_codes[:, cells].bitcast(FP8X4), x_bytes[:, cells], start=True, stop=True)
 
-        windows = [keep.tile([P, S if t == 3 else 2 * S], F32, name="window%d" % t, align_bytes=64) for t in range(PACK)]
+        windows = [keep.tile([P, 2 * S], F32, name="window%d" % t, align_bytes=64) for t in range(PACK)]
         nc.gpsimd.memset(windows[0][:, S : 2 * S], 0.0)
-        centre2 = keep.tile([P, S], F32, name="centre2")
         centre3 = keep.tile([P, S], F32, name="centre3", align_bytes=64)
-        centres = [windows[1][:, S : 2 * S], windows[2][:, S : 2 * S], centre2[:], centre3[:]]
+        centres = [windows[1][:, S : 2 * S], windows[2][:, S : 2 * S], windows[3][:, S : 2 * S], centre3[:]]
 
         y_low = acc.tile([P, HALF], F32, name="y_low", tag="acc")
         y_third = acc.tile([P, P], F32, name="y_third", tag="acc")
@@ -127,9 +126,9 @@ def tile_picked_census8_none_p_kernel(tc, x_words, x_scales, w1, gn, w2, offs, p
         def looked_up(t, term, cells):
             return windows[t][:].indirect(lists[term][:, cells.start // 16 : cells.stop // 16])
 
-        def add_up(t, term, cells, neighbours, pool=ring, tag="work"):
+        def add_up(t, term, cells, neighbours, pool=ring, tag="work", own=None):
             gap = pool.tile([P, cells.stop - cells.start], F32, name="gap", tag=tag, align_bytes=64)
-            nc.vector.tensor_tensor(gap[:], neighbours, centres[t][:, cells], ALU.subtract)
+            nc.vector.tensor_tensor(gap[:], neighbours, (own or centres)[t][:, cells], ALU.subtract)
             func, scale = (ACT.Sigmoid, 4.0) if term == NEAR else (ACT.Tanh, 2.0)
             nc.scalar.activation(softs[t][:, term, cells], gap[:], func, scale=scale)
             for b in range(cells.start // P, cells.stop // P):
@@ -156,11 +155,10 @@ def tile_picked_census8_none_p_kernel(tc, x_words, x_scales, w1, gn, w2, offs, p
         single2 = keep.tile([P, HALF], F32, name="single2", align_bytes=64)
         fetch(2, SINGLE, high, single2[:])
         census(1, DOUBLED, whole, keep, "near2")
-        census(2, DOUBLED, whole)
+        census(2, DOUBLED, whole, keep, "single1")
         near2 = keep.tile([P, S], F32, name="near2", align_bytes=64)
         fetch(2, NEAR, whole, near2[:])
-        census(3, DOUBLED, low, keep, "single1")
-        census(3, DOUBLED, high)
+        census(3, DOUBLED, whole)
         single1 = keep.tile([P, HALF], F32, name="single1", align_bytes=64)
         fetch(1, SINGLE, high, single1[:])
         add_up(1, NEAR, whole, near1[:])
@@ -171,10 +169,9 @@ def tile_picked_census8_none_p_kernel(tc, x_words, x_scales, w1, gn, w2, offs, p
         census(3, NEAR, low)
         add_up(1, SINGLE, high, single1[:])
         add_up(2, SINGLE, high, single2[:])
-        census(3, SINGLE, third)
-        census(3, NEAR, third)
-        census(3, SINGLE, fourth)
-        census(3, NEAR, fourth)
+        for cells in (third, fourth):
+            for term in (SINGLE, NEAR):
+                add_up(3, term, cells, centre3[:].indirect(lists[term][:, cells.start // 16 : cells.stop // 16]), own=windows)
 
         w2_first = ring.tile([P, W2_SPLIT, PACK], BF16, name="w2_first", tag="work", align_bytes=64)
         w2_src = w2_raw[:].rearrange("p j (c i) -> p c j i", i=4)
@@ -239,9 +236,15 @@ def tile_picked_census8_none_p_kernel(tc, x_words, x_scales, w1, gn, w2, offs, p
         project(0, slice(0, P), in_sums, movers[0])
         project(0, slice(P, HALF), in_sums, movers[0])
         store(0, low)
-        for m, cells, place in ((1, low, in_sums), (2, low, in_sums), (3, low, in_acc), (0, high, in_acc), (1, high, in_turn), (2, high, in_turn)):
-            project(m, cells, place, movers[m % 2])
-            store(m, cells)
-        project(3, third, in_sums, movers[1])
-        project(3, fourth, in_sums, movers[0])
+        for m, place in ((1, in_sums), (2, in_sums), (3, in_acc)):
+            project(m, low, place, movers[m // 3])
+            store(m, low)
+        project(0, third, in_acc, movers[1])
+        project(0, fourth, in_sums, movers[0])
+        store(0, high)
+        for m in (1, 2):
+            project(m, high, in_turn, movers[m % 2])
+            store(m, high)
+        project(3, third, in_sums, movers[0])
+        project(3, fourth, in_sums, movers[1])
         store(3, high)

@@ -20,7 +20,6 @@ P = 128
 PACK = 4
 HALF = S // 2
 SCALAR_SHARE = 44
-W2_SPLIT = 192
 DOUBLED, SINGLE, NEAR = 0, 1, 2
 RING = 5
 ADDS = 4 * PACK
@@ -173,13 +172,13 @@ def tile_picked_census8_none_p_kernel(tc, x_words, x_scales, w1, gn, w2, offs, p
             for term in (SINGLE, NEAR):
                 add_up(3, term, cells, centre3[:].indirect(lists[term][:, cells.start // 16 : cells.stop // 16]), own=windows)
 
-        w2_first = ring.tile([P, W2_SPLIT, PACK], BF16, name="w2_first", tag="work", align_bytes=64)
+        w2_first = ring.tile([P, HALF, PACK], BF16, name="w2_first", tag="work", align_bytes=64)
         w2_src = w2_raw[:].rearrange("p j (c i) -> p c j i", i=4)
         w2_dst = w2_first[:].rearrange("p (c i) j -> p c j i", i=4)
-        for groups in (slice(0, P // 4), slice(P // 4, W2_SPLIT // 4)):
+        for groups in (slice(0, P // 4), slice(P // 4, HALF // 4)):
             nc.scalar.copy(w2_dst[:, groups], w2_src[:, groups])
-        w2_rest = keep.tile([P, N - W2_SPLIT, PACK], BF16, name="w2_rest", tag="centre3", align_bytes=64)
-        nc.gpsimd.tensor_scalar(w2_rest[:], w2_raw[:, :, W2_SPLIT:N].rearrange("p j n -> p n j"), 1.0, 0.0, ALU.mult, ALU.add)
+        w2_rest = keep.tile([P, N - HALF, PACK], BF16, name="w2_rest", tag="centre3", align_bytes=64)
+        nc.gpsimd.tensor_scalar(w2_rest[:], w2_raw[:, :, HALF:N].rearrange("p j n -> p n j"), 1.0, 0.0, ALU.mult, ALU.add)
 
         def leave(b):
             pool, tag = (acc, "acc") if b == 2 else (turn, "turned")
@@ -211,9 +210,8 @@ def tile_picked_census8_none_p_kernel(tc, x_words, x_scales, w1, gn, w2, offs, p
         pack_w2(slice(0, P), w2_first[:, 0:P])
         pack(0, z_tiles[0])
         pack(1, z_tiles[1])
-        pack_w2(slice(P, W2_SPLIT), w2_first[:, P:W2_SPLIT])
-        pack_w2(slice(W2_SPLIT, HALF), w2_rest[:, 0 : HALF - W2_SPLIT])
-        pack_w2(high, w2_rest[:, HALF - W2_SPLIT : N - W2_SPLIT])
+        pack_w2(slice(P, HALF), w2_first[:, P:HALF])
+        pack_w2(high, w2_rest[:])
         pack(2, z_tiles[2])
         pack(3, z_tiles[3])
 

@@ -53,6 +53,9 @@ def tile_picked_census8_none_p_kernel(tc, x_words, x_scales, w1, gn, w2, offs, p
         nc.sync.dma_start(w1_raw[:, 2:4, :], w1_rows[:, 2:4, :])
         word_table = keep.tile([P, T], U32, name="word_table", align_bytes=64)
         nc.sync.dma_start(word_table[:].bitcast(I32), x_words[0].rearrange("p n t -> p (n t)").bitcast(I32))
+        w2_rows = w2.rearrange("(p j) c -> p j c", j=PACK)
+        w2_head = keep.tile([P, PACK, P], F32, name="w2_head")
+        nc.sync.dma_start(w2_head[:], w2_rows[:, :, 0:P])
         lists = (load_list("list3", p3), load_list("list2", p2), load_list("list1", p1))
 
         x_bytes = keep.tile([P, S], U8, name="x_bytes", align_bytes=64)
@@ -69,8 +72,8 @@ def tile_picked_census8_none_p_kernel(tc, x_words, x_scales, w1, gn, w2, offs, p
         w1_src = w1_raw[:].rearrange("p j (m t) -> p m j t", t=PACK)
         nc.scalar.copy(w1_dst[:, 0:SCALAR_SHARE], w1_src[:, 0:SCALAR_SHARE])
         nc.vector.tensor_copy(w1_dst[:, SCALAR_SHARE:P], w1_src[:, SCALAR_SHARE:P])
-        w2_raw = keep.tile([P, PACK, N], F32, name="w2_raw", tag="raw")
-        nc.sync.dma_start(w2_raw[:], w2.rearrange("(p j) c -> p j c", j=PACK))
+        w2_raw = keep.tile([P, PACK, N - P], F32, name="w2_raw", tag="raw")
+        nc.sync.dma_start(w2_raw[:], w2_rows[:, :, P:N])
 
         w1_codes = keep.tile([P, H], U32, name="w1_codes", align_bytes=64)
         w1_scales = keep.tile([P, H], U8, name="w1_scales", align_bytes=64)
@@ -87,6 +90,15 @@ def tile_picked_census8_none_p_kernel(tc, x_words, x_scales, w1, gn, w2, offs, p
         x_codes = keep.tile([P, S], U32, name="x_codes", align_bytes=64)
         for cells in (low, third, fourth):
             nc.vector.tensor_copy(x_codes[:, cells], word_table[:].indirect(picks[:, cells.start // 16 : cells.stop // 16]))
+
+        head_codes = keep.tile([P, P], U32, name="head_codes", align_bytes=64)
+        w2_scales = keep.tile([P, N], U8, name="w2_scales", align_bytes=64)
+
+        def pack_w2(columns, rounded, codes):
+            nc.vector.quantize_mx(codes.bitcast(FP8X4), w2_scales[:, columns], rounded.rearrange("p n j -> p (n j)"))
+
+        w2_head_bf = keep.tile([P, P, PACK], BF16, name="w2_head_bf", align_bytes=64)
+        nc.vector.tensor_copy(w2_head_bf[:].rearrange("p (c i) j -> p c j i", i=4), w2_head[:].rearrange("p j (c i) -> p c j i", i=4))
 
         def first_product(t, cells, y_ps):
             cols = slice(t * P, (t + 1) * P)
@@ -110,6 +122,7 @@ def tile_picked_census8_none_p_kernel(tc, x_words, x_scales, w1, gn, w2, offs, p
         nc.scalar.copy(windows[0][:, low], y_low[:])
         nc.scalar.copy(centres[0][:, low], y_low[:])
         nc.vector.tensor_copy(windows[0][:, third], y_third[:])
+        pack_w2(slice(0, P), w2_head_bf[:], head_codes[:])
         nc.vector.tensor_copy(windows[0][:, fourth], y_fourth[:])
         nc.scalar.copy(centres[0][:, third], y_third[:])
         nc.scalar.copy(centres[0][:, fourth], y_fourth[:])
@@ -172,13 +185,10 @@ def tile_picked_census8_none_p_kernel(tc, x_words, x_scales, w1, gn, w2, offs, p
             for term in (SINGLE, NEAR):
                 add_up(3, term, cells, centre3[:].indirect(lists[term][:, cells.start // 16 : cells.stop // 16]), own=windows)
 
-        w2_first = ring.tile([P, HALF, PACK], BF16, name="w2_first", tag="work", align_bytes=64)
-        w2_src = w2_raw[:].rearrange("p j (c i) -> p c j i", i=4)
-        w2_dst = w2_first[:].rearrange("p (c i) j -> p c j i", i=4)
-        for groups in (slice(0, P // 4), slice(P // 4, HALF // 4)):
-            nc.scalar.copy(w2_dst[:, groups], w2_src[:, groups])
-        w2_rest = keep.tile([P, N - HALF, PACK], BF16, name="w2_rest", tag="centre3", align_bytes=64)
-        nc.gpsimd.tensor_scalar(w2_rest[:], w2_raw[:, :, HALF:N].rearrange("p j n -> p n j"), 1.0, 0.0, ALU.mult, ALU.add)
+        w2_second = ring.tile([P, P, PACK], BF16, name="w2_second", tag="work", align_bytes=64)
+        nc.scalar.copy(w2_second[:].rearrange("p (c i) j -> p c j i", i=4), w2_raw[:, :, 0:P].rearrange("p j (c i) -> p c j i", i=4))
+        w2_rest = keep.tile([P, HALF, PACK], BF16, name="w2_rest", tag="centre3", align_bytes=64)
+        nc.gpsimd.tensor_scalar(w2_rest[:], w2_raw[:, :, P : N - P].rearrange("p j n -> p n j"), 1.0, 0.0, ALU.mult, ALU.add)
 
         def leave(b):
             pool, tag = (acc, "acc") if b == 2 else (turn, "turned")
@@ -193,11 +203,6 @@ def tile_picked_census8_none_p_kernel(tc, x_words, x_scales, w1, gn, w2, offs, p
             nc.scalar.copy(z_words, turned[:].rearrange("p u j -> p j u"))
             return z_bf
 
-        w2_scales = keep.tile([P, N], U8, name="w2_scales", align_bytes=64)
-
-        def pack_w2(columns, rounded):
-            nc.vector.quantize_mx(w2_codes[:, columns].bitcast(FP8X4), w2_scales[:, columns], rounded.rearrange("p n j -> p (n j)"))
-
         z_codes = keep.tile([P, S], U32, name="z_codes", align_bytes=64)
         z_scales = keep.tile([P, S], U8, name="z_scales", align_bytes=64)
 
@@ -206,12 +211,12 @@ def tile_picked_census8_none_p_kernel(tc, x_words, x_scales, w1, gn, w2, offs, p
             nc.vector.quantize_mx(z_codes[:, cells].bitcast(FP8X4), z_scales[:, cells], z_bf[:].rearrange("p j t -> p (j t)"))
 
         z_tiles = [leave(b) for b in range(4)]
-        w2_codes = ring.tile([P, N], U32, name="w2_codes", tag="work", align_bytes=64)
-        pack_w2(slice(0, P), w2_first[:, 0:P])
+        rest_codes = ring.tile([P, N - P], U32, name="rest_codes", tag="work", align_bytes=64)
+        w2_codes = [head_codes[:]] + [rest_codes[:, m * P : (m + 1) * P] for m in range(PACK - 1)]
         pack(0, z_tiles[0])
         pack(1, z_tiles[1])
-        pack_w2(slice(P, HALF), w2_first[:, P:HALF])
-        pack_w2(high, w2_rest[:])
+        pack_w2(slice(P, HALF), w2_second[:], w2_codes[1])
+        pack_w2(high, w2_rest[:], rest_codes[:, P : N - P])
         pack(2, z_tiles[2])
         pack(3, z_tiles[3])
 
@@ -223,7 +228,7 @@ def tile_picked_census8_none_p_kernel(tc, x_words, x_scales, w1, gn, w2, offs, p
         def project(m, cells, place, mover):
             rows = slice(m * P, (m + 1) * P)
             o_ps = place[0].tile([P, cells.stop - cells.start], F32, name="o_ps", tag=place[1])
-            nc.tensor.matmul_mx(o_ps[:], w2_codes[:, rows].bitcast(FP8X4), w2_scales[:, rows], z_codes[:, cells].bitcast(FP8X4), z_scales[:, cells], start=True, stop=True)
+            nc.tensor.matmul_mx(o_ps[:], w2_codes[m].bitcast(FP8X4), w2_scales[:, rows], z_codes[:, cells].bitcast(FP8X4), z_scales[:, cells], start=True, stop=True)
             mover(held(m, cells), o_ps[:])
 
         def store(m, cells):

@@ -45,7 +45,7 @@ def tile_picked_census8_none_p_kernel(tc, x_words, x_scales, w1, gn, w2, offs, p
         nc.gpsimd.memset(warm[:], 0.0)
 
         w1_rows = w1.rearrange("(p j) c -> p j c", j=PACK)
-        w1_raw = keep.tile([P, PACK, H], F32, name="w1_raw", tag="raw")
+        w1_raw = keep.tile([P, PACK, H], F32, name="w1_raw")
         nc.sync.dma_start(w1_raw[:, 0:2, :], w1_rows[:, 0:2, :])
         picks = load_list("picks", offs)
         for r in range(4):
@@ -72,8 +72,6 @@ def tile_picked_census8_none_p_kernel(tc, x_words, x_scales, w1, gn, w2, offs, p
         w1_src = w1_raw[:].rearrange("p j (m t) -> p m j t", t=PACK)
         nc.scalar.copy(w1_dst[:, 0:SCALAR_SHARE], w1_src[:, 0:SCALAR_SHARE])
         nc.vector.tensor_copy(w1_dst[:, SCALAR_SHARE:P], w1_src[:, SCALAR_SHARE:P])
-        w2_raw = keep.tile([P, PACK, N - P], F32, name="w2_raw", tag="raw")
-        nc.sync.dma_start(w2_raw[:], w2_rows[:, :, P:N])
 
         w1_codes = keep.tile([P, H], U32, name="w1_codes", align_bytes=64)
         w1_scales = keep.tile([P, H], U8, name="w1_scales", align_bytes=64)
@@ -163,7 +161,9 @@ def tile_picked_census8_none_p_kernel(tc, x_words, x_scales, w1, gn, w2, offs, p
         fetch(1, NEAR, low, near1[:, low])
         census(0, SINGLE, whole, keep, "single2")
         fetch(1, NEAR, high, near1[:, high])
-        census(0, NEAR, whole)
+        census(0, NEAR, whole, keep, "w2_raw")
+        w2_raw = keep.tile([P, PACK, N - P], F32, name="w2_raw", align_bytes=64)
+        nc.sync.dma_start(w2_raw[:], w2_rows[:, :, P:N])
         single2 = keep.tile([P, HALF], F32, name="single2", align_bytes=64)
         fetch(2, SINGLE, high, single2[:])
         census(1, DOUBLED, whole, keep, "near2")

from contextlib import ExitStack

import concourse.mybir as mybir
from concourse.masks import make_identity

K, T, S, N, H = 512, 2048, 512, 512, 512
FLOPS = 2 * K * H * S + 2 * H * N * S

F32 = mybir.dt.float32
BF16 = mybir.dt.bfloat16
I32 = mybir.dt.int32
U32 = mybir.dt.uint32
U16 = mybir.dt.uint16
U8 = mybir.dt.uint8
FP8X4 = mybir.dt.float8_e4m3fn_x4
ACT = mybir.ActivationFunctionType
ALU = mybir.AluOpType

P = 128
PACK = 4
HALF = S // 2
SCALAR_SHARE = 44
DOUBLED, SINGLE, NEAR = 0, 1, 2
RING = 5
ADDS = 4 * PACK


def tile_picked_census8_none_p_kernel(tc, x_words, x_scales, w1, gn, w2, offs, p1, p2, p3, out):
    nc = tc.nc
    with ExitStack() as ctx:
        keep = ctx.enter_context(tc.tile_pool(name="keep", bufs=1))
        ring = ctx.enter_context(tc.tile_pool(name="ring", bufs=RING))
        acc = ctx.enter_context(tc.psum_pool(name="acc", bufs=2))
        sums = ctx.enter_context(tc.psum_pool(name="sums", bufs=4))
        turn = ctx.enter_context(tc.psum_pool(name="turn", bufs=2))

        def load_list(name, source):
            held = keep.tile([P, S // 16], U16, name=name)
            nc.sync.dma_start(held[:], source)
            return held

        scale_table = keep.tile([P, T], U8, name="scale_table", align_bytes=64)
        nc.gpsimd.memset(scale_table[:].bitcast(I32), 0)
        warm = keep.tile([P, 1], F32, name="warm")
        nc.gpsimd.memset(warm[:], 0.0)

        w1_rows = w1.rearrange("(p j) c -> p j c", j=PACK)
        w1_raw = keep.tile([P, PACK, H], F32, name="w1_raw")
        nc.sync.dma_start(w1_raw[:, 0:2, :], w1_rows[:, 0:2, :])
        picks = load_list("picks", offs)
        for r in range(4):
            nc.sync.dma_start(scale_table[r:P:32, :].bitcast(I32), x_scales[0, r:16:4, :].bitcast(I32))
        nc.sync.dma_start(w1_raw[:, 2:4, :], w1_rows[:, 2:4, :])
        word_table = keep.tile([P, T], U32, name="word_table", align_bytes=64)
        nc.sync.dma_start(word_table[:].bitcast(I32), x_words[0].rearrange("p n t -> p (n t)").bitcast(I32))
        w2_rows = w2.rearrange("(p j) c -> p j c", j=PACK)
        w2_head = keep.tile([P, PACK, P], F32, name="w2_head")
        nc.sync.dma_start(w2_head[:], w2_rows[:, :, 0:P])
        lists = (load_list("list3", p3), load_list("list2", p2), load_list("list1", p1))

        x_bytes = keep.tile([P, S], U8, name="x_bytes", align_bytes=64)
        nc.vector.tensor_copy(x_bytes[:], scale_table[:].indirect(picks[:]))

        nc.scalar.activation(warm[:], warm[:], ACT.Sigmoid)
        ident = keep.tile([P, P], F32, name="ident")
        make_identity(nc, ident[:])
        gain = keep.tile([P, PACK], F32, name="gain")
        nc.gpsimd.dma_start(gain[:], gn.rearrange("(p t) o -> p (t o)", t=PACK))

        w1_bf = keep.tile([P, PACK, P, PACK], BF16, name="w1_bf", align_bytes=64)
        w1_dst = w1_bf[:].rearrange("p t m j -> p m j t")
        w1_src = w1_raw[:].rearrange("p j (m t) -> p m j t", t=PACK)
        nc.scalar.copy(w1_dst[:, 0:SCALAR_SHARE], w1_src[:, 0:SCALAR_SHARE])
        nc.vector.tensor_copy(w1_dst[:, SCALAR_SHARE:P], w1_src[:, SCALAR_SHARE:P])

        w1_codes = keep.tile([P, H], U32, name="w1_codes", align_bytes=64)
        w1_scales = keep.tile([P, H], U8, name="w1_scales", align_bytes=64)
        nc.vector.quantize_mx(w1_codes[:].bitcast(FP8X4), w1_scales[:], w1_bf[:].rearrange("p t m j -> p (t m j)"))

        gain_rows = keep.tile([P, 2, P, 2], F32, name="gain_rows", tag="w1_bf", align_bytes=64)
        gain_ps = turn.tile([P, PACK, P], F32, name="gain_ps", tag="turned")
        for t in range(PACK):
            nc.tensor.transpose(gain_ps[:, t, :], gain[:, t : t + 1].to_broadcast([P, P]), ident[:])
        nc.scalar.activation(gain_rows[:], gain_ps[:].rearrange("j (u e) p -> j u p e", e=2), ACT.Copy, scale=0.5)

        low, high, whole = slice(0, HALF), slice(HALF, S), slice(0, S)
        third, fourth = slice(HALF, HALF + P), slice(HALF + P, S)
        x_codes = keep.tile([P, S], U32, name="x_codes", align_bytes=64)
        for cells in (low, third, fourth):
            nc.vector.tensor_copy(x_codes[:, cells], word_table[:].indirect(picks[:, cells.start // 16 : cells.stop // 16]))

        head_codes = keep.tile([P, P], U32, name="head_codes", align_bytes=64)
        w2_scales = keep.tile([P, N], U8, name="w2_scales", align_bytes=64)

        def pack_w2(columns, rounded, codes):
            nc.vector.quantize_mx(codes.bitcast(FP8X4), w2_scales[:, columns], rounded.rearrange("p n j -> p (n j)"))

        w2_head_bf = keep.tile([P, P, PACK], BF16, name="w2_head_bf", align_bytes=64)
        nc.vector.tensor_copy(w2_head_bf[:].rearrange("p (c i) j -> p c j i", i=4), w2_head[:].rearrange("p j (c i) -> p c j i", i=4))

        def first_product(t, cells, y_ps):
            cols = slice(t * P, (t + 1) * P)
            nc.tensor.matmul_mx(y_ps, w1_codes[:, cols].bitcast(FP8X4), w1_scales[:, cols], x_codes[:, cells].bitcast(FP8X4), x_bytes[:, cells], start=True, stop=True)

        windows = [keep.tile([P, 2 * S], F32, name="window%d" % t, align_bytes=64) for t in range(PACK)]
        nc.gpsimd.memset(windows[0][:, S : 2 * S], 0.0)
        centre3 = keep.tile([P, S], F32, name="centre3", align_bytes=64)
        centres = [windows[1][:, S : 2 * S], windows[2][:, S : 2 * S], windows[3][:, S : 2 * S], centre3[:]]

        y_low = acc.tile([P, HALF], F32, name="y_low", tag="acc")
        y_third = acc.tile([P, P], F32, name="y_third", tag="acc")
        y_fourth = sums.tile([P, P], F32, name="y_fourth", tag="bank")
        first_product(0, low, y_low[:])
        first_product(0, third, y_third[:])
        first_product(0, fourth, y_fourth[:])
        later = {}
        for t, (pool, tag) in ((1, (turn, "turned")), (2, (turn, "turned")), (3, (acc, "acc"))):
            later[t] = pool.tile([P, S], F32, name="y_ps", tag=tag)
            first_product(t, whole, later[t][:])
        nc.scalar.copy(windows[0][:, low], y_low[:])
        nc.scalar.copy(centres[0][:, low], y_low[:])
        nc.vector.tensor_copy(windows[0][:, third], y_third[:])
        pack_w2(slice(0, P), w2_head_bf[:], head_codes[:])
        nc.vector.tensor_copy(windows[0][:, fourth], y_fourth[:])
        nc.scalar.copy(centres[0][:, third], y_third[:])
        nc.scalar.copy(centres[0][:, fourth], y_fourth[:])

        def open_window(t):
            nc.scalar.copy(windows[t][:, whole], later[t][:])
            nc.sync.dma_start(centres[t], windows[t][:, whole])

        softs = [keep.tile([P, 3, S], F32, name="soft%d" % t) for t in range(PACK)]
        banks = [sums.tile([P, 2, 2, P], F32, name="bank", tag="bank") for b in range(4)]
        added = [[] for b in range(4)]

        def looked_up(t, term, cells):
            return windows[t][:].indirect(lists[term][:, cells.start // 16 : cells.stop // 16])

        def add_up(t, term, cells, neighbours, pool=ring, tag="work", own=None):
            gap = pool.tile([P, cells.stop - cells.start], F32, name="gap", tag=tag, align_bytes=64)
            nc.vector.tensor_tensor(gap[:], neighbours, (own or centres)[t][:, cells], ALU.subtract)
            func, scale = (ACT.Sigmoid, 4.0) if term == NEAR else (ACT.Tanh, 2.0)
            nc.scalar.activation(softs[t][:, term, cells], gap[:], func, scale=scale)
            for b in range(cells.start // P, cells.stop // P):
                for again in range(2 if term == DOUBLED else 1):
                    added[b].append(term)
                    nc.tensor.matmul(banks[b][:, t % 2, t // 2, :], softs[t][:, term, b * P : (b + 1) * P], ident[:], start=len(added[b]) == 1, stop=len(added[b]) == ADDS, is_transpose=True)

        def census(t, term, cells, *place):
            add_up(t, term, cells, looked_up(t, term, cells), *place)

        def fetch(t, term, cells, into):
            nc.scalar.activation(into, looked_up(t, term, cells), ACT.Copy)

        open_window(1)
        census(0, DOUBLED, low, keep, "near1")
        open_window(2)
        census(0, DOUBLED, high)
        open_window(3)
        near1 = keep.tile([P, S], F32, name="near1", align_bytes=64)
        fetch(1, NEAR, low, near1[:, low])
        census(0, SINGLE, whole, keep, "single2")
        fetch(1, NEAR, high, near1[:, high])
        census(0, NEAR, whole, keep, "w2_raw")
        w2_raw = keep.tile([P, PACK, N - P], F32, name="w2_raw", align_bytes=64)
        nc.sync.dma_start(w2_raw[:], w2_rows[:, :, P:N])
        single2 = keep.tile([P, HALF], F32, name="single2", align_bytes=64)
        fetch(2, SINGLE, high, single2[:])
        census(1, DOUBLED, whole, keep, "near2")
        census(2, DOUBLED, whole, keep, "single1")
        near2 = keep.tile([P, S], F32, name="near2", align_bytes=64)
        fetch(2, NEAR, whole, near2[:])
        census(3, DOUBLED, whole)
        single1 = keep.tile([P, HALF], F32, name="single1", align_bytes=64)
        fetch(1, SINGLE, high, single1[:])
        add_up(1, NEAR, whole, near1[:])
        census(1, SINGLE, low)
        census(2, SINGLE, low)
        add_up(2, NEAR, whole, near2[:])
        census(3, SINGLE, low)
        census(3, NEAR, low)
        add_up(1, SINGLE, high, single1[:])
        add_up(2, SINGLE, high, single2[:])
        for cells in (third, fourth):
            for term in (SINGLE, NEAR):
                add_up(3, term, cells, centre3[:].indirect(lists[term][:, cells.start // 16 : cells.stop // 16]), own=windows)

        w2_second = ring.tile([P, P, PACK], BF16, name="w2_second", tag="work", align_bytes=64)
        nc.scalar.copy(w2_second[:].rearrange("p (c i) j -> p c j i", i=4), w2_raw[:, :, 0:P].rearrange("p j (c i) -> p c j i", i=4))
        w2_rest = keep.tile([P, HALF, PACK], BF16, name="w2_rest", tag="centre3", align_bytes=64)
        nc.gpsimd.tensor_scalar(w2_rest[:], w2_raw[:, :, P : N - P].rearrange("p j n -> p n j"), 1.0, 0.0, ALU.mult, ALU.add)

        def leave(b):
            pool, tag = (acc, "acc") if b == 2 else (turn, "turned")
            turned = pool.tile([P, 2, P], F32, name="turned", tag=tag)
            z_rows = ring.tile([P, 2, P, 2], BF16, name="z_rows", tag="work", align_bytes=64)
            for us in (slice(0, 1), slice(1, 2)) if b % 2 else (slice(0, 2),):
                nc.vector.scalar_tensor_tensor(z_rows[:, us].rearrange("j u p e -> j (u p) e"), banks[b][:, :, us].rearrange("j e u p -> j (u p) e"), -0.5, gain_rows[:, us].rearrange("j u p e -> j (u p) e"), ALU.add, ALU.mult)
            for u in range(2):
                nc.tensor.transpose(turned[:, u, :], z_rows[:, u].rearrange("j p e -> j (p e)").bitcast(F32), ident[:])
            z_bf = keep.tile([P, P, PACK], BF16, name="z%d" % b, align_bytes=64)
            z_words = z_bf[:].rearrange("p j t -> p (j t)").bitcast(F32).rearrange("p (j u) -> p j u", u=2)
            nc.scalar.copy(z_words, turned[:].rearrange("p u j -> p j u"))
            return z_bf

        z_codes = keep.tile([P, S], U32, name="z_codes", align_bytes=64)
        z_scales = keep.tile([P, S], U8, name="z_scales", align_bytes=64)

        def pack(b, z_bf):
            cells = slice(b * P, (b + 1) * P)
            nc.vector.quantize_mx(z_codes[:, cells].bitcast(FP8X4), z_scales[:, cells], z_bf[:].rearrange("p j t -> p (j t)"))

        z_tiles = [leave(b) for b in range(4)]
        rest_codes = ring.tile([P, N - P], U32, name="rest_codes", tag="work", align_bytes=64)
        w2_codes = [head_codes[:]] + [rest_codes[:, m * P : (m + 1) * P] for m in range(PACK - 1)]
        pack(0, z_tiles[0])
        pack(1, z_tiles[1])
        pack_w2(slice(P, HALF), w2_second[:], w2_codes[1])
        pack_w2(high, w2_rest[:], rest_codes[:, P : N - P])
        pack(2, z_tiles[2])
        pack(3, z_tiles[3])

        results = [keep.tile([P, PACK, HALF], F32, name="result%d" % h) for h in range(2)]

        def held(m, cells):
            return results[cells.start // HALF][:, m, cells.start % HALF : (cells.stop - 1) % HALF + 1]

        def project(m, cells, place, mover):
            rows = slice(m * P, (m + 1) * P)
            o_ps = place[0].tile([P, cells.stop - cells.start], F32, name="o_ps", tag=place[1])
            nc.tensor.matmul_mx(o_ps[:], w2_codes[m].bitcast(FP8X4), w2_scales[:, rows], z_codes[:, cells].bitcast(FP8X4), z_scales[:, cells], start=True, stop=True)
            mover(held(m, cells), o_ps[:])

        def store(m, cells):
            nc.sync.dma_start(out[m * P : (m + 1) * P, cells], held(m, cells))

        in_sums, in_acc, in_turn = (sums, "bank"), (acc, "acc"), (turn, "turned")
        movers = (nc.scalar.copy, nc.vector.tensor_copy)
        project(0, slice(0, P), in_sums, movers[0])
        project(0, slice(P, HALF), in_sums, movers[0])
        store(0, low)
        for m, place in ((1, in_sums), (2, in_sums), (3, in_acc)):
            project(m, low, place, movers[m // 3])
            store(m, low)
        project(0, third, in_acc, movers[1])
        project(0, fourth, in_sums, movers[0])
        store(0, high)
        for m in (1, 2):
            project(m, high, in_turn, movers[m % 2])
            store(m, high)
        project(3, third, in_sums, movers[0])
        project(3, fourth, in_sums, movers[1])
        store(3, high)
